import numpy as np
import ml_dtypes


def mxq(x, axis, fmt="e4m3"):
    dtype, down = {"e4m3": (ml_dtypes.float8_e4m3fn, 7), "e5m2": (ml_dtypes.float8_e5m2, 14)}[fmt]
    v = np.moveaxis(np.asarray(x, np.float32).astype(ml_dtypes.bfloat16).astype(np.float64), axis, -1)
    blocks = v.reshape(v.shape[:-1] + (-1, 32))
    amax = np.abs(blocks).max(-1, keepdims=True)
    byte = np.maximum(np.where(amax > 0, np.frexp(amax)[1] - 1 + 127, 0) - down, 1)
    scale = np.exp2(byte - 127.0)
    codes = (blocks / scale).astype(np.float32).astype(dtype).astype(np.float64)
    return np.moveaxis((codes * scale).reshape(v.shape), -1, axis)


WIDE = False


def mx_kscale(k):
    if not WIDE:
        return np.ones(k)
    levels = np.array([18, -18])
    if k % 512:
        return np.exp2(np.random.permutation(np.resize(levels, k // 32))).repeat(32)
    a = np.empty((k // 512, 16))
    for p in range(k // 512):
        a[p, :8] = np.random.permutation(np.resize(levels, 8))
        for g in range(8):
            far = levels[np.abs(levels - a[p, g]) >= 10]
            a[p, g + 8] = far[np.random.randint(len(far))]
    return np.exp2(a.ravel()).repeat(32)


def f64(x):
    return np.asarray(x).astype(np.float64)


def striped(idx):
    return np.tile(np.asarray(idx).reshape(-1, 16).T, (8, 1)).astype(np.uint16)


def unstriped(offs):
    return offs[:16].T.reshape(-1).astype(np.int64)


def setup_inputs():
    n = np.random.standard_normal
    uni = np.random.uniform
    idx = np.random.permutation(2048)[:512]
    f_d = mx_kscale(512)
    f_e = mx_kscale(512)
    f_r = mx_kscale(512)
    return {
        "xT": (n((512, 512)) * f_d[:, None] * f_r[None, :]).astype(np.float32),
        "qT": (n((512, 2048)) / np.sqrt(512) / f_d[:, None]).astype(np.float32),
        "dyT": (n((512, 512)) * f_e[:, None]).astype(np.float32),
        "pT": (n((512, 2048)) / np.sqrt(512) / f_e[:, None]).astype(np.float32),
        "lam": np.tile(uni(0.75, 1.3, 2048), (128, 1)).astype(np.float32),
        "us": (uni(0.75, 1.3, (512, 1)) / f_r[:, None]).astype(np.float32),
        "offs": striped(idx),
    }


def reference(xT, qT, dyT, pT, lam, us, offs):
    idx = unstriped(offs)
    qT_i = f64(qT)[:, idx]
    pT_i = f64(pT)[:, idx]
    lam_i = f64(lam)[:1][:, idx]
    u = mxq(f64(xT), 0, "e4m3").T @ mxq(qT_i, 0, "e4m3")
    v = mxq(f64(dyT), 0, "e5m2").T @ mxq(pT_i, 0, "e4m3")
    h = f64(us) * u * v
    ht = h.T
    s = (ht).sum(-1, keepdims=True)
    out_0 = s.T
    g = f64(us) * lam_i * v
    dq = mxq(f64(xT), 1, "e4m3") @ mxq(g, 0, "e5m2")
    out_1 = np.zeros((512, 2048))
    out_1[:, idx] = dq
    return out_0, out_1

@@ -1,0 +1,250 @@
+from contextlib import ExitStack
+
+import concourse.mybir as mybir
+from concourse.masks import make_identity
+
+F32 = mybir.dt.float32
+BF16 = mybir.dt.bfloat16
+U32 = mybir.dt.uint32
+U16 = mybir.dt.uint16
+U8 = mybir.dt.uint8
+E4M3 = mybir.dt.float8_e4m3fn_x4
+E5M2 = mybir.dt.float8_e5m2_x4
+MULT = mybir.AluOpType.mult
+COPY = mybir.ActivationFunctionType.Copy
+
+P = 128
+PACK = 4
+K = P * PACK
+SLOTS = 512
+PIECES = 2048
+HALF = SLOTS // 2
+RUN = 4
+QUAD = 32
+
+FLOPS = 3 * 2 * K * K * SLOTS
+BYTES = 4 * (2 * K * K + 3 * K * PIECES + PIECES + K + SLOTS) + 2 * P * SLOTS // 16
+
+
+def interleave(copy, dst, planes, first, count):
+    copy(
+        dst.rearrange("p (c i t) -> p c t i", i=RUN, t=PACK),
+        planes.rearrange("p (t n) -> p t n", t=PACK)[:, :, first : first + count].rearrange(
+            "p t (c i) -> p c t i", i=RUN
+        ),
+    )
+
+
+def tile_attend_gadal_kernel(tc, xT, qT, dyT, pT, lam, us, offs, out_0, out_1):
+    nc = tc.nc
+    with ExitStack() as ctx:
+        sb = ctx.enter_context(tc.tile_pool(name="sb", bufs=1))
+        ps = ctx.enter_context(tc.psum_pool(name="ps", bufs=1))
+
+        def tile(name, width, dtype, tag=None):
+            return sb.tile([P, width], dtype, name=name, tag=tag or name, align_bytes=64)
+
+        def bank(name, tag):
+            return ps.tile([P, SLOTS], F32, name=name, tag=tag)
+
+        def quantize(codes, scales, values, fmt):
+            nc.vector.quantize_mx(out=codes.bitcast(fmt), scales=scales, in_=values)
+
+        def matmul(out, lhs, lhs_scales, lhs_fmt, rhs, rhs_scales, rhs_fmt):
+            nc.tensor.matmul_mx(
+                out=out,
+                lhsT=lhs.bitcast(lhs_fmt),
+                lhsT_scale=lhs_scales,
+                rhs=rhs.bitcast(rhs_fmt),
+                rhs_scale=rhs_scales,
+                start=True,
+                stop=True,
+            )
+
+        offsets = tile("offsets", SLOTS // 16, U16)
+        nc.sync.dma_start(offsets[:], offs)
+        lam_cols = tile("lam_cols", PIECES // P, F32)
+        nc.scalar.dma_start(lam_cols[:], lam[0:1, :].rearrange("o (p c) -> (o p) c", p=P))
+        us_cols = tile("us_cols", PACK, F32)
+        nc.scalar.dma_start(us_cols[:], us.rearrange("(p t) o -> p (t o)", t=PACK))
+
+        p_rows = pT.rearrange("(p t) n -> t p n", t=PACK)
+        q_rows = qT.rearrange("(p t) n -> t p n", t=PACK)
+        x_rows = xT.rearrange("(p t) r -> p (t r)", t=PACK)
+        p_tables = [tile(f"p_table{t}", PIECES, F32) for t in range(PACK)]
+        q_tables = [tile(f"q_table{t}", PIECES, F32) for t in range(PACK)]
+        dy_raw = tile("dy_raw", PACK * K, F32)
+        x_raw = tile("x_raw", PACK * K, F32)
+        for t in range(PACK):
+            nc.sync.dma_start(p_tables[t][:], p_rows[t])
+        nc.sync.dma_start(dy_raw[:], dyT.rearrange("(p t) r -> p (t r)", t=PACK))
+        nc.sync.dma_start(x_raw[:, 0:K], x_rows[:, 0:K])
+        nc.sync.dma_start(q_tables[0][:], q_rows[0])
+        nc.sync.dma_start(x_raw[:, K:], x_rows[:, K:])
+        for t in range(1, PACK):
+            nc.sync.dma_start(q_tables[t][:], q_rows[t])
+
+        ident = tile("ident", P, F32)
+        make_identity(nc, ident[:])
+        windows = [tile(f"window{n}", PIECES, F32) for n in range(2)]
+        for window in windows:
+            nc.vector.memset(window[:], 0.0)
+
+        lam_table = tile("lam_table", PIECES, F32)
+        for k in range(PACK):
+            spread = bank(f"lam_spread{k}", f"v{k}")
+            for c in range(PACK):
+                col = PACK * k + c
+                nc.tensor.transpose(
+                    spread[:, c * P : (c + 1) * P], lam_cols[:, col : col + 1].to_broadcast([P, P]), ident[:]
+                )
+            nc.scalar.activation(
+                lam_table[:].rearrange("p (n k c) -> p k n c", k=PACK, c=PACK)[:, k],
+                spread[:].rearrange("p (c n) -> p n c", c=PACK),
+                COPY,
+            )
+        lam_slots = tile("lam_slots", SLOTS, F32)
+        nc.vector.tensor_copy(lam_slots[:], lam_table[:].indirect(offsets[:]))
+
+        p_words = tile("p_words", PACK * SLOTS, BF16)
+        for t in range(PACK):
+            nc.vector.tensor_copy(p_words[:, t : PACK * SLOTS : PACK], p_tables[t][:].indirect(offsets[:]))
+        p_codes = tile("p_codes", SLOTS, U32)
+        p_scales = tile("p_scales", SLOTS, U8)
+        quantize(p_codes[:], p_scales[:], p_words[:], E4M3)
+
+        dy_view = dy_raw[:].rearrange("p (j m t) -> p m j t", j=PACK, t=PACK)
+        dy_codes, dy_scales = {}, {}
+        for pair, copy in ((1, nc.vector.tensor_copy), (0, nc.scalar.copy)):
+            words = tile(f"dy_words{pair}", 2 * K, BF16)
+            copy(
+                words[:].rearrange("p (t m j) -> p m j t", t=2, j=PACK),
+                dy_view[:, :, :, 2 * pair : 2 * pair + 2],
+            )
+            dy_codes[pair] = tile(f"dy_codes{pair}", 2 * P, U32)
+            dy_scales[pair] = tile(f"dy_scales{pair}", 2 * P, U8)
+            quantize(dy_codes[pair][:], dy_scales[pair][:], words[:], E5M2)
+
+        g_planes = tile("g_planes", PACK * SLOTS, BF16)
+        w_planes = tile("w_planes", PACK * SLOTS, F32)
+        order = (2, 3, 0, 1)
+        v_banks = {}
+        for t in order:
+            v_banks[t] = bank(f"v{t}", f"v{t}")
+            cols = slice((t % 2) * P, (t % 2 + 1) * P)
+            matmul(v_banks[t][:], dy_codes[t // 2][:, cols], dy_scales[t // 2][:, cols], E5M2,
+                   p_codes[:], p_scales[:], E4M3)
+        for t in order:
+            nc.vector.scalar_tensor_tensor(
+                g_planes[:, t * SLOTS : (t + 1) * SLOTS], v_banks[t][:], us_cols[:, t : t + 1], lam_slots[:],
+                MULT, MULT,
+            )
+
+        def x_along_rows(j):
+            turned = bank(f"x_turned{j}", f"turn{j % 2}")
+            for t in range(PACK):
+                nc.tensor.transpose(turned[:, t * P : (t + 1) * P], x_raw[:, j * K + t : (j + 1) * K : PACK], ident[:])
+            words = tile(f"xr_words{j}", K, BF16)
+            nc.scalar.copy(
+                words[:].rearrange("p (c t) -> p c t", t=PACK), turned[:].rearrange("p (t c) -> p c t", t=PACK)
+            )
+            codes = tile(f"xr_codes{j}", P, U32)
+            scales = tile(f"xr_scales{j}", P, U8)
+            quantize(codes[:], scales[:], words[:], E4M3)
+            return codes, scales
+
+        xr = [x_along_rows(0)]
+
+        g_words = tile("g_words", PACK * SLOTS, BF16)
+        g_codes = tile("g_codes", SLOTS, U32, tag="g_codes")
+        g_scales = tile("g_scales", SLOTS, U8)
+        for half, copy in ((0, nc.scalar.copy), (1, nc.vector.tensor_copy)):
+            interleave(copy, g_words[:, half * PACK * HALF : (half + 1) * PACK * HALF], g_planes[:], half * HALF, HALF)
+        for half in (1, 0):
+            cols = slice(half * HALF, (half + 1) * HALF)
+            quantize(g_codes[:, cols], g_scales[:, cols],
+                     g_words[:, half * PACK * HALF : (half + 1) * PACK * HALF], E5M2)
+
+        out_rows = out_1.rearrange("(p j) n -> j p n", j=PACK)
+
+        def dq_product(j, tag):
+            acc = bank(f"dq_acc{j}", tag)
+            matmul(acc[:], xr[j][0][:], xr[j][1][:], E4M3, g_codes[:], g_scales[:], E5M2)
+            return acc
+
+        def dq_out(j, acc, tag):
+            dq = tile(f"dq{j}", SLOTS, F32, tag=tag)
+            nc.scalar.copy(dq[:], acc[:])
+            window = windows[j % 2]
+            nc.vector.tensor_copy(window[:].indirect(offsets[:]), dq[:])
+            nc.sync.dma_start(out_rows[j], window[:])
+
+        dq_out(0, dq_product(0, "dq0"), "dq_sb0")
+
+        for t in order:
+            nc.scalar.activation(
+                w_planes[:, t * SLOTS : (t + 1) * SLOTS].rearrange("p (b a k) -> p a b k", b=PACK, a=PACK),
+                v_banks[t][:].rearrange("p (a b k) -> p a b k", a=PACK, b=PACK),
+                COPY,
+                scale=us_cols[:, t : t + 1],
+            )
+
+        xr.extend(x_along_rows(j) for j in range(1, PACK))
+        dq_out(1, dq_product(1, "dq1"), "dq_sb1")
+        acc2 = dq_product(2, "v2")
+        acc3 = dq_product(3, "v3")
+
+        q_planes = tile("q_planes", PACK * SLOTS, BF16, tag="g_words")
+        for t in range(PACK):
+            nc.vector.tensor_copy(q_planes[:, t * SLOTS : (t + 1) * SLOTS], q_tables[t][:].indirect(offsets[:]))
+
+        dq_out(2, acc2, "dq_sb2")
+
+        xd_words = tile("xd_words", PACK * K, BF16, tag="g_codes")
+        interleave(nc.scalar.copy, xd_words[:], x_raw[:], 0, K)
+
+        w_turned = []
+        for b in range(PACK):
+            turned = bank(f"w_bank{b}", f"dq{b % 2}")
+            for t in range(PACK):
+                nc.tensor.transpose(turned[:, t * P : (t + 1) * P],
+                                    w_planes[:, t * SLOTS + b * P : t * SLOTS + (b + 1) * P], ident[:])
+            w_rows = tile(f"w_turned{b}", K, F32)
+            nc.scalar.copy(
+                w_rows[:].rearrange("p (m t) -> p m t", t=PACK), turned[:].rearrange("p (t m) -> p m t", t=PACK)
+            )
+            w_turned.append(w_rows)
+
+        q_words = [tile(f"q_words{half}", PACK * HALF, BF16) for half in range(2)]
+        q_view = q_planes[:].rearrange("p (t a b c i) -> p b a c t i", t=PACK, a=PACK, b=PACK, i=RUN)
+        for b in range(PACK):
+            nc.scalar.copy(
+                q_words[b // 2][:, (b % 2) * K : (b % 2 + 1) * K].rearrange(
+                    "p (a c i t) -> p a c t i", a=PACK, i=RUN, t=PACK
+                ),
+                q_view[:, b],
+            )
+        q_codes = tile("q_codes", SLOTS, U32, tag="dq_sb2")
+        q_scales = tile("q_scales", SLOTS, U8)
+        for half in range(2):
+            cols = slice(half * HALF, (half + 1) * HALF)
+            quantize(q_codes[:, cols], q_scales[:, cols], q_words[half][:], E4M3)
+        xd_codes = tile("xd_codes", K, U32, tag="q_words1")
+        xd_scales = tile("xd_scales", K, U8)
+        quantize(xd_codes[:], xd_scales[:], xd_words[:], E4M3)
+
+        dq_out(3, acc3, "q_words0")
+
+        sums = tile("sums", QUAD, F32)
+        nc.gpsimd.memset(sums[:], 0.0)
+        for b, tag in enumerate(("v0", "v1", "turn0", "turn1")):
+            cols = slice(b * P, (b + 1) * P)
+            u = bank(f"u{b}", tag)
+            matmul(u[:], q_codes[:, cols], q_scales[:, cols], E4M3, xd_codes[:], xd_scales[:], E4M3)
+            col = b * QUAD // PACK
+            products = tile(f"products{b}", K, F32)
+            nc.vector.scalar_tensor_tensor(products[:], u[:], 1.0, w_turned[b][:], MULT, MULT,
+                                           accum_out=sums[:, col : col + 1])
+        s_rows = tile("s_rows", QUAD, F32)
+        nc.vector.transpose(s_rows[:], sums[:])
+        nc.sync.dma_start(out_0.rearrange("o (n k) -> (o n) k", k=QUAD), s_rows[0:P : QUAD // PACK, :])

@@ -79,14 +79,13 @@ def tile_attend_gadal_kernel(tc, xT, qT, dyT, pT, lam, us, offs, out_0, out_1):
             nc.sync.dma_start(p_tables[t][:], p_rows[t])
         nc.sync.dma_start(dy_raw[:], dyT.rearrange("(p t) r -> p (t r)", t=PACK))
         nc.sync.dma_start(x_raw[:, 0:K], x_rows[:, 0:K])
-        nc.sync.dma_start(q_tables[0][:], q_rows[0])
         nc.sync.dma_start(x_raw[:, K:], x_rows[:, K:])
-        for t in range(1, PACK):
+        for t in range(PACK):
             nc.sync.dma_start(q_tables[t][:], q_rows[t])
 
         ident = tile("ident", P, F32)
         make_identity(nc, ident[:])
-        windows = [tile(f"window{n}", PIECES, F32) for n in range(2)]
+        windows = [tile(f"window{n}", PIECES, F32) for n in range(3)]
         for window in windows:
             nc.vector.memset(window[:], 0.0)
 
@@ -126,7 +125,6 @@ def tile_attend_gadal_kernel(tc, xT, qT, dyT, pT, lam, us, offs, out_0, out_1):
             quantize(dy_codes[pair][:], dy_scales[pair][:], words[:], E5M2)
 
         g_planes = tile("g_planes", PACK * SLOTS, BF16)
-        w_planes = tile("w_planes", PACK * SLOTS, F32)
         order = (2, 3, 0, 1)
         v_banks = {}
         for t in order:
@@ -140,8 +138,8 @@ def tile_attend_gadal_kernel(tc, xT, qT, dyT, pT, lam, us, offs, out_0, out_1):
                 MULT, MULT,
             )
 
-        def x_along_rows(j):
-            turned = bank(f"x_turned{j}", f"turn{j % 2}")
+        def x_along_rows(j, tag):
+            turned = bank(f"x_turned{j}", tag)
             for t in range(PACK):
                 nc.tensor.transpose(turned[:, t * P : (t + 1) * P], x_raw[:, j * K + t : (j + 1) * K : PACK], ident[:])
             words = tile(f"xr_words{j}", K, BF16)
@@ -153,14 +151,14 @@ def tile_attend_gadal_kernel(tc, xT, qT, dyT, pT, lam, us, offs, out_0, out_1):
             quantize(codes[:], scales[:], words[:], E4M3)
             return codes, scales
 
-        xr = [x_along_rows(0)]
+        xr = [x_along_rows(0, "turn0")]
 
         g_words = tile("g_words", PACK * SLOTS, BF16)
         g_codes = tile("g_codes", SLOTS, U32, tag="g_codes")
         g_scales = tile("g_scales", SLOTS, U8)
-        for half, copy in ((0, nc.scalar.copy), (1, nc.vector.tensor_copy)):
-            interleave(copy, g_words[:, half * PACK * HALF : (half + 1) * PACK * HALF], g_planes[:], half * HALF, HALF)
-        for half in (1, 0):
+        for half in range(2):
+            interleave(nc.vector.tensor_copy, g_words[:, half * PACK * HALF : (half + 1) * PACK * HALF], g_planes[:], half * HALF, HALF)
+        for half in range(2):
             cols = slice(half * HALF, (half + 1) * HALF)
             quantize(g_codes[:, cols], g_scales[:, cols],
                      g_words[:, half * PACK * HALF : (half + 1) * PACK * HALF], E5M2)
@@ -175,45 +173,44 @@ def tile_attend_gadal_kernel(tc, xT, qT, dyT, pT, lam, us, offs, out_0, out_1):
         def dq_out(j, acc, tag):
             dq = tile(f"dq{j}", SLOTS, F32, tag=tag)
             nc.scalar.copy(dq[:], acc[:])
-            window = windows[j % 2]
+            window = windows[j % 3]
             nc.vector.tensor_copy(window[:].indirect(offsets[:]), dq[:])
             nc.sync.dma_start(out_rows[j], window[:])
 
         dq_out(0, dq_product(0, "dq0"), "dq_sb0")
 
-        for t in order:
+        xr.append(x_along_rows(1, "turn1"))
+        xr.append(x_along_rows(2, "dq1"))
+        xr.append(x_along_rows(3, "turn0"))
+        dq_out(1, dq_product(1, "turn1"), "dq_sb1")
+        dq_out(2, dq_product(2, "dq1"), "dq_sb2")
+        acc3 = dq_product(3, "turn0")
+
+        def w_plane(t, tag):
+            plane = tile(f"w_plane{t}", SLOTS, F32, tag=tag)
             nc.scalar.activation(
-                w_planes[:, t * SLOTS : (t + 1) * SLOTS].rearrange("p (b a k) -> p a b k", b=PACK, a=PACK),
+                plane[:].rearrange("p (b a k) -> p a b k", b=PACK, a=PACK),
                 v_banks[t][:].rearrange("p (a b k) -> p a b k", a=PACK, b=PACK),
                 COPY,
                 scale=us_cols[:, t : t + 1],
             )
+            return plane
 
-        xr.extend(x_along_rows(j) for j in range(1, PACK))
-        dq_out(1, dq_product(1, "dq1"), "dq_sb1")
-        acc2 = dq_product(2, "v2")
-        acc3 = dq_product(3, "v3")
+        w_planes = {t: w_plane(t, f"w_plane{t}") for t in order[:2]}
 
         q_planes = tile("q_planes", PACK * SLOTS, BF16, tag="g_words")
-        for t in range(PACK):
+        for t in range(2):
             nc.vector.tensor_copy(q_planes[:, t * SLOTS : (t + 1) * SLOTS], q_tables[t][:].indirect(offsets[:]))
+        for t, tag in ((2, "xr_codes0"), (3, "q_narrow3")):
+            narrow = tile(f"q_narrow{t}", PIECES, BF16, tag=tag)
+            for half in range(2):
+                cols = slice(half * PIECES // 2, (half + 1) * PIECES // 2)
+                nc.scalar.activation(narrow[:, cols], q_tables[t][:, cols], COPY)
+            nc.scalar.activation(q_planes[:, t * SLOTS : (t + 1) * SLOTS], narrow[:].indirect(offsets[:]), COPY)
 
-        dq_out(2, acc2, "dq_sb2")
-
-        xd_words = tile("xd_words", PACK * K, BF16, tag="g_codes")
-        interleave(nc.scalar.copy, xd_words[:], x_raw[:], 0, K)
-
-        w_turned = []
+        xd_words = tile("xd_words", PACK * K, BF16)
         for b in range(PACK):
-            turned = bank(f"w_bank{b}", f"dq{b % 2}")
-            for t in range(PACK):
-                nc.tensor.transpose(turned[:, t * P : (t + 1) * P],
-                                    w_planes[:, t * SLOTS + b * P : t * SLOTS + (b + 1) * P], ident[:])
-            w_rows = tile(f"w_turned{b}", K, F32)
-            nc.scalar.copy(
-                w_rows[:].rearrange("p (m t) -> p m t", t=PACK), turned[:].rearrange("p (t m) -> p m t", t=PACK)
-            )
-            w_turned.append(w_rows)
+            interleave(nc.scalar.copy, xd_words[:, b * K : (b + 1) * K], x_raw[:], b * P, P)
 
         q_words = [tile(f"q_words{half}", PACK * HALF, BF16) for half in range(2)]
         q_view = q_planes[:].rearrange("p (t a b c i) -> p b a c t i", t=PACK, a=PACK, b=PACK, i=RUN)
@@ -235,15 +232,28 @@ def tile_attend_gadal_kernel(tc, xT, qT, dyT, pT, lam, us, offs, out_0, out_1):
 
         dq_out(3, acc3, "q_words0")
 
+        for t, tag in zip(order[2:], ("g_words", "q_narrow3")):
+            w_planes[t] = w_plane(t, tag)
+        w_turned = tile("w_turned", PACK * K, F32)
+        for b in range(PACK):
+            turned = bank(f"w_bank{b}", f"v{order[b]}")
+            for t in order:
+                nc.tensor.transpose(turned[:, t * P : (t + 1) * P],
+                                    w_planes[t][:, b * P : (b + 1) * P], ident[:])
+            nc.scalar.copy(
+                w_turned[:, b * K : (b + 1) * K].rearrange("p (m t) -> p m t", t=PACK),
+                turned[:].rearrange("p (t m) -> p m t", t=PACK),
+            )
+
         sums = tile("sums", QUAD, F32)
         nc.gpsimd.memset(sums[:], 0.0)
-        for b, tag in enumerate(("v0", "v1", "turn0", "turn1")):
+        for b, tag in enumerate(("dq0", "dq1", "turn1", "turn0")):
             cols = slice(b * P, (b + 1) * P)
             u = bank(f"u{b}", tag)
             matmul(u[:], q_codes[:, cols], q_scales[:, cols], E4M3, xd_codes[:], xd_scales[:], E4M3)
             col = b * QUAD // PACK
             products = tile(f"products{b}", K, F32)
-            nc.vector.scalar_tensor_tensor(products[:], u[:], 1.0, w_turned[b][:], MULT, MULT,
+            nc.vector.scalar_tensor_tensor(products[:], u[:], 1.0, w_turned[:, b * K : (b + 1) * K], MULT, MULT,
                                            accum_out=sums[:, col : col + 1])
         s_rows = tile("s_rows", QUAD, F32)
         nc.vector.transpose(s_rows[:], sums[:])

@@ -21,6 +21,7 @@ PIECES = 2048
 HALF = SLOTS // 2
 RUN = 4
 QUAD = 32
+WINDOWS = 3
 
 FLOPS = 3 * 2 * K * K * SLOTS
 BYTES = 4 * (2 * K * K + 3 * K * PIECES + PIECES + K + SLOTS) + 2 * P * SLOTS // 16
@@ -64,9 +65,8 @@ def tile_attend_gadal_kernel(tc, xT, qT, dyT, pT, lam, us, offs, out_0, out_1):
         offsets = tile("offsets", SLOTS // 16, U16)
         nc.sync.dma_start(offsets[:], offs)
         lam_cols = tile("lam_cols", PIECES // P, F32)
-        nc.scalar.dma_start(lam_cols[:], lam[0:1, :].rearrange("o (p c) -> (o p) c", p=P))
+        nc.sync.dma_start(lam_cols[:], lam[0:1, :].rearrange("o (p c) -> (o p) c", p=P))
         us_cols = tile("us_cols", PACK, F32)
-        nc.scalar.dma_start(us_cols[:], us.rearrange("(p t) o -> p (t o)", t=PACK))
 
         p_rows = pT.rearrange("(p t) n -> t p n", t=PACK)
         q_rows = qT.rearrange("(p t) n -> t p n", t=PACK)
@@ -77,6 +77,7 @@ def tile_attend_gadal_kernel(tc, xT, qT, dyT, pT, lam, us, offs, out_0, out_1):
         x_raw = tile("x_raw", PACK * K, F32)
         for t in range(PACK):
             nc.sync.dma_start(p_tables[t][:], p_rows[t])
+        nc.sync.dma_start(us_cols[:], us.rearrange("(p t) o -> p (t o)", t=PACK))
         nc.sync.dma_start(dy_raw[:], dyT.rearrange("(p t) r -> p (t r)", t=PACK))
         nc.sync.dma_start(x_raw[:, 0:K], x_rows[:, 0:K])
         nc.sync.dma_start(x_raw[:, K:], x_rows[:, K:])
@@ -85,20 +86,20 @@ def tile_attend_gadal_kernel(tc, xT, qT, dyT, pT, lam, us, offs, out_0, out_1):
 
         ident = tile("ident", P, F32)
         make_identity(nc, ident[:])
-        windows = [tile(f"window{n}", PIECES, F32) for n in range(3)]
+        windows = [tile(f"window{n}", PIECES, F32) for n in range(WINDOWS)]
         for window in windows:
             nc.vector.memset(window[:], 0.0)
 
         lam_table = tile("lam_table", PIECES, F32)
-        for k in range(PACK):
-            spread = bank(f"lam_spread{k}", f"v{k}")
+        for group in range(PACK):
+            spread = bank(f"lam_spread{group}", f"v{group}")
             for c in range(PACK):
-                col = PACK * k + c
+                col = PACK * group + c
                 nc.tensor.transpose(
                     spread[:, c * P : (c + 1) * P], lam_cols[:, col : col + 1].to_broadcast([P, P]), ident[:]
                 )
             nc.scalar.activation(
-                lam_table[:].rearrange("p (n k c) -> p k n c", k=PACK, c=PACK)[:, k],
+                lam_table[:].rearrange("p (n g c) -> p g n c", g=PACK, c=PACK)[:, group],
                 spread[:].rearrange("p (c n) -> p n c", c=PACK),
                 COPY,
             )
@@ -130,61 +131,60 @@ def tile_attend_gadal_kernel(tc, xT, qT, dyT, pT, lam, us, offs, out_0, out_1):
         for t in order:
             v_banks[t] = bank(f"v{t}", f"v{t}")
             cols = slice((t % 2) * P, (t % 2 + 1) * P)
-            matmul(v_banks[t][:], dy_codes[t // 2][:, cols], dy_scales[t // 2][:, cols], E5M2,
-                   p_codes[:], p_scales[:], E4M3)
+            matmul(
+                v_banks[t][:], dy_codes[t // 2][:, cols], dy_scales[t // 2][:, cols], E5M2, p_codes[:], p_scales[:], E4M3
+            )
         for t in order:
             nc.vector.scalar_tensor_tensor(
-                g_planes[:, t * SLOTS : (t + 1) * SLOTS], v_banks[t][:], us_cols[:, t : t + 1], lam_slots[:],
-                MULT, MULT,
+                g_planes[:, t * SLOTS : (t + 1) * SLOTS], v_banks[t][:], us_cols[:, t : t + 1], lam_slots[:], MULT, MULT
             )
 
-        def x_along_rows(j, tag):
-            turned = bank(f"x_turned{j}", tag)
+        def x_along_rows(j, bank_tag, codes):
+            turned = bank(f"x_turned{j}", bank_tag)
             for t in range(PACK):
                 nc.tensor.transpose(turned[:, t * P : (t + 1) * P], x_raw[:, j * K + t : (j + 1) * K : PACK], ident[:])
             words = tile(f"xr_words{j}", K, BF16)
             nc.scalar.copy(
                 words[:].rearrange("p (c t) -> p c t", t=PACK), turned[:].rearrange("p (t c) -> p c t", t=PACK)
             )
-            codes = tile(f"xr_codes{j}", P, U32)
             scales = tile(f"xr_scales{j}", P, U8)
-            quantize(codes[:], scales[:], words[:], E4M3)
-            return codes, scales
+            quantize(codes, scales[:], words[:], E4M3)
+            return codes, scales[:]
 
-        xr = [x_along_rows(0, "turn0")]
+        xr_first = tile("xr_codes0", P, U32)
+        xr = [x_along_rows(0, "turn0", xr_first[:])]
 
         g_words = tile("g_words", PACK * SLOTS, BF16)
-        g_codes = tile("g_codes", SLOTS, U32, tag="g_codes")
+        g_codes = tile("g_codes", SLOTS, U32)
         g_scales = tile("g_scales", SLOTS, U8)
+        g_halves = [g_words[:, half * PACK * HALF : (half + 1) * PACK * HALF] for half in range(2)]
         for half in range(2):
-            interleave(nc.vector.tensor_copy, g_words[:, half * PACK * HALF : (half + 1) * PACK * HALF], g_planes[:], half * HALF, HALF)
+            interleave(nc.vector.tensor_copy, g_halves[half], g_planes[:], half * HALF, HALF)
         for half in range(2):
             cols = slice(half * HALF, (half + 1) * HALF)
-            quantize(g_codes[:, cols], g_scales[:, cols],
-                     g_words[:, half * PACK * HALF : (half + 1) * PACK * HALF], E5M2)
+            quantize(g_codes[:, cols], g_scales[:, cols], g_halves[half], E5M2)
 
         out_rows = out_1.rearrange("(p j) n -> j p n", j=PACK)
 
-        def dq_product(j, tag):
-            acc = bank(f"dq_acc{j}", tag)
-            matmul(acc[:], xr[j][0][:], xr[j][1][:], E4M3, g_codes[:], g_scales[:], E5M2)
+        def dq_product(j, bank_tag):
+            acc = bank(f"dq_acc{j}", bank_tag)
+            matmul(acc[:], xr[j][0], xr[j][1], E4M3, g_codes[:], g_scales[:], E5M2)
             return acc
 
         def dq_out(j, acc, tag):
             dq = tile(f"dq{j}", SLOTS, F32, tag=tag)
             nc.scalar.copy(dq[:], acc[:])
-            window = windows[j % 3]
+            window = windows[j % WINDOWS]
             nc.vector.tensor_copy(window[:].indirect(offsets[:]), dq[:])
             nc.sync.dma_start(out_rows[j], window[:])
 
         dq_out(0, dq_product(0, "dq0"), "dq_sb0")
 
-        xr.append(x_along_rows(1, "turn1"))
-        xr.append(x_along_rows(2, "dq1"))
-        xr.append(x_along_rows(3, "turn0"))
+        xr_rest = tile("xr_rest", (PACK - 1) * P, U32, tag="g_planes")
+        xr.append(x_along_rows(1, "turn1", xr_rest[:, 0:P]))
+        xr.append(x_along_rows(2, "dq1", xr_rest[:, P : 2 * P]))
         dq_out(1, dq_product(1, "turn1"), "dq_sb1")
         dq_out(2, dq_product(2, "dq1"), "dq_sb2")
-        acc3 = dq_product(3, "turn0")
 
         def w_plane(t, tag):
             plane = tile(f"w_plane{t}", SLOTS, F32, tag=tag)
@@ -201,6 +201,8 @@ def tile_attend_gadal_kernel(tc, xT, qT, dyT, pT, lam, us, offs, out_0, out_1):
         q_planes = tile("q_planes", PACK * SLOTS, BF16, tag="g_words")
         for t in range(2):
             nc.vector.tensor_copy(q_planes[:, t * SLOTS : (t + 1) * SLOTS], q_tables[t][:].indirect(offsets[:]))
+        xr.append(x_along_rows(3, "turn0", xr_rest[:, 2 * P : 3 * P]))
+        last_acc = dq_product(3, "turn0")
         for t, tag in ((2, "xr_codes0"), (3, "q_narrow3")):
             narrow = tile(f"q_narrow{t}", PIECES, BF16, tag=tag)
             for half in range(2):
@@ -209,8 +211,8 @@ def tile_attend_gadal_kernel(tc, xT, qT, dyT, pT, lam, us, offs, out_0, out_1):
             nc.scalar.activation(q_planes[:, t * SLOTS : (t + 1) * SLOTS], narrow[:].indirect(offsets[:]), COPY)
 
         xd_words = tile("xd_words", PACK * K, BF16)
-        for b in range(PACK):
-            interleave(nc.scalar.copy, xd_words[:, b * K : (b + 1) * K], x_raw[:], b * P, P)
+        for part in range(PACK):
+            interleave(nc.scalar.copy, xd_words[:, part * K : (part + 1) * K], x_raw[:], part * P, P)
 
         q_words = [tile(f"q_words{half}", PACK * HALF, BF16) for half in range(2)]
         q_view = q_planes[:].rearrange("p (t a b c i) -> p b a c t i", t=PACK, a=PACK, b=PACK, i=RUN)
@@ -221,6 +223,7 @@ def tile_attend_gadal_kernel(tc, xT, qT, dyT, pT, lam, us, offs, out_0, out_1):
                 ),
                 q_view[:, b],
             )
+
         q_codes = tile("q_codes", SLOTS, U32, tag="dq_sb2")
         q_scales = tile("q_scales", SLOTS, U8)
         for half in range(2):
@@ -230,7 +233,7 @@ def tile_attend_gadal_kernel(tc, xT, qT, dyT, pT, lam, us, offs, out_0, out_1):
         xd_scales = tile("xd_scales", K, U8)
         quantize(xd_codes[:], xd_scales[:], xd_words[:], E4M3)
 
-        dq_out(3, acc3, "q_words0")
+        dq_out(3, last_acc, "q_words0")
 
         for t, tag in zip(order[2:], ("g_words", "q_narrow3")):
             w_planes[t] = w_plane(t, tag)
@@ -238,8 +241,7 @@ def tile_attend_gadal_kernel(tc, xT, qT, dyT, pT, lam, us, offs, out_0, out_1):
         for b in range(PACK):
             turned = bank(f"w_bank{b}", f"v{order[b]}")
             for t in order:
-                nc.tensor.transpose(turned[:, t * P : (t + 1) * P],
-                                    w_planes[t][:, b * P : (b + 1) * P], ident[:])
+                nc.tensor.transpose(turned[:, t * P : (t + 1) * P], w_planes[t][:, b * P : (b + 1) * P], ident[:])
             nc.scalar.copy(
                 w_turned[:, b * K : (b + 1) * K].rearrange("p (m t) -> p m t", t=PACK),
                 turned[:].rearrange("p (t m) -> p m t", t=PACK),
@@ -247,14 +249,15 @@ def tile_attend_gadal_kernel(tc, xT, qT, dyT, pT, lam, us, offs, out_0, out_1):
 
         sums = tile("sums", QUAD, F32)
         nc.gpsimd.memset(sums[:], 0.0)
-        for b, tag in enumerate(("dq0", "dq1", "turn1", "turn0")):
+        for b, bank_tag in enumerate(("dq0", "dq1", "turn1", "turn0")):
             cols = slice(b * P, (b + 1) * P)
-            u = bank(f"u{b}", tag)
+            u = bank(f"u{b}", bank_tag)
             matmul(u[:], q_codes[:, cols], q_scales[:, cols], E4M3, xd_codes[:], xd_scales[:], E4M3)
             col = b * QUAD // PACK
             products = tile(f"products{b}", K, F32)
-            nc.vector.scalar_tensor_tensor(products[:], u[:], 1.0, w_turned[:, b * K : (b + 1) * K], MULT, MULT,
-                                           accum_out=sums[:, col : col + 1])
+            nc.vector.scalar_tensor_tensor(
+                products[:], u[:], 1.0, w_turned[:, b * K : (b + 1) * K], MULT, MULT, accum_out=sums[:, col : col + 1]
+            )
         s_rows = tile("s_rows", QUAD, F32)
         nc.vector.transpose(s_rows[:], sums[:])
         nc.sync.dma_start(out_0.rearrange("o (n k) -> (o n) k", k=QUAD), s_rows[0:P : QUAD // PACK, :])

@@ -36,6 +36,10 @@ def interleave(copy, dst, planes, first, count):
     )
 
 
+def dealt(ap):
+    return ap.rearrange("p (b a k) -> p a b k", b=PACK, a=PACK)
+
+
 def tile_attend_gadal_kernel(tc, xT, qT, dyT, pT, lam, us, offs, out_0, out_1):
     nc = tc.nc
     with ExitStack() as ctx:
@@ -196,11 +200,11 @@ def tile_attend_gadal_kernel(tc, xT, qT, dyT, pT, lam, us, offs, out_0, out_1):
             )
             return plane
 
-        w_planes = {t: w_plane(t, f"w_plane{t}") for t in order[:2]}
+        w_planes = {t: w_plane(t, f"w_plane{t}") for t in order}
 
         q_planes = tile("q_planes", PACK * SLOTS, BF16, tag="g_words")
         for t in range(2):
-            nc.vector.tensor_copy(q_planes[:, t * SLOTS : (t + 1) * SLOTS], q_tables[t][:].indirect(offsets[:]))
+            nc.vector.tensor_copy(dealt(q_planes[:, t : 2 * SLOTS : 2]), q_tables[t][:].indirect(offsets[:]))
         xr.append(x_along_rows(3, "turn0", xr_rest[:, 2 * P : 3 * P]))
         last_acc = dq_product(3, "turn0")
         for t, tag in ((2, "xr_codes0"), (3, "q_narrow3")):
@@ -208,20 +212,18 @@ def tile_attend_gadal_kernel(tc, xT, qT, dyT, pT, lam, us, offs, out_0, out_1):
             for half in range(2):
                 cols = slice(half * PIECES // 2, (half + 1) * PIECES // 2)
                 nc.scalar.activation(narrow[:, cols], q_tables[t][:, cols], COPY)
-            nc.scalar.activation(q_planes[:, t * SLOTS : (t + 1) * SLOTS], narrow[:].indirect(offsets[:]), COPY)
+            place = dealt(q_planes[:, 2 * SLOTS + t % 2 : PACK * SLOTS : 2])
+            nc.scalar.activation(place, narrow[:].indirect(offsets[:]), COPY)
 
         xd_words = tile("xd_words", PACK * K, BF16)
         for part in range(PACK):
             interleave(nc.scalar.copy, xd_words[:, part * K : (part + 1) * K], x_raw[:], part * P, P)
 
         q_words = [tile(f"q_words{half}", PACK * HALF, BF16) for half in range(2)]
-        q_view = q_planes[:].rearrange("p (t a b c i) -> p b a c t i", t=PACK, a=PACK, b=PACK, i=RUN)
-        for b in range(PACK):
+        for half in range(2):
             nc.scalar.copy(
-                q_words[b // 2][:, (b % 2) * K : (b % 2 + 1) * K].rearrange(
-                    "p (a c i t) -> p a c t i", a=PACK, i=RUN, t=PACK
-                ),
-                q_view[:, b],
+                q_words[half][:].bitcast(U32).rearrange("p (s j) -> p s j", j=2),
+                q_planes[:].bitcast(U32).rearrange("p (j s) -> p s j", j=2)[:, half * HALF : (half + 1) * HALF],
             )
 
         q_codes = tile("q_codes", SLOTS, U32, tag="dq_sb2")
@@ -235,9 +237,7 @@ def tile_attend_gadal_kernel(tc, xT, qT, dyT, pT, lam, us, offs, out_0, out_1):
 
         dq_out(3, last_acc, "q_words0")
 
-        for t, tag in zip(order[2:], ("g_words", "q_narrow3")):
-            w_planes[t] = w_plane(t, tag)
-        w_turned = tile("w_turned", PACK * K, F32)
+        w_turned = tile("w_turned", PACK * K, F32, tag="g_words")
         for b in range(PACK):
             turned = bank(f"w_bank{b}", f"v{order[b]}")
             for t in order:
@@ -255,9 +255,17 @@ def tile_attend_gadal_kernel(tc, xT, qT, dyT, pT, lam, us, offs, out_0, out_1):
             matmul(u[:], q_codes[:, cols], q_scales[:, cols], E4M3, xd_codes[:], xd_scales[:], E4M3)
             col = b * QUAD // PACK
             products = tile(f"products{b}", K, F32)
-            nc.vector.scalar_tensor_tensor(
-                products[:], u[:], 1.0, w_turned[:, b * K : (b + 1) * K], MULT, MULT, accum_out=sums[:, col : col + 1]
-            )
+            if b == 0:
+                u_copy = tile("u_copy", K, F32)
+                nc.scalar.copy(u_copy[:], u[:])
+                nc.gpsimd.tensor_tensor(products[:], u_copy[:], w_turned[:, b * K : (b + 1) * K], MULT)
+                spent = tile("spent", K, BF16)
+                late = (spent, products, col)
+            else:
+                nc.vector.scalar_tensor_tensor(
+                    products[:], u[:], 1.0, w_turned[:, b * K : (b + 1) * K], MULT, MULT, accum_out=sums[:, col : col + 1]
+                )
+        nc.scalar.activation(late[0][:], late[1][:], COPY, accum_out=sums[:, late[2] : late[2] + 1])
         s_rows = tile("s_rows", QUAD, F32)
         nc.vector.transpose(s_rows[:], sums[:])
         nc.sync.dma_start(out_0.rearrange("o (n k) -> (o n) k", k=QUAD), s_rows[0:P : QUAD // PACK, :])

@@ -11,6 +11,7 @@ U8 = mybir.dt.uint8
 E4M3 = mybir.dt.float8_e4m3fn_x4
 E5M2 = mybir.dt.float8_e5m2_x4
 MULT = mybir.AluOpType.mult
+ADD = mybir.AluOpType.add
 COPY = mybir.ActivationFunctionType.Copy
 
 P = 128
@@ -217,7 +218,7 @@ def tile_attend_gadal_kernel(tc, xT, qT, dyT, pT, lam, us, offs, out_0, out_1):
 
         xd_words = tile("xd_words", PACK * K, BF16)
         for part in range(PACK):
-            interleave(nc.scalar.copy, xd_words[:, part * K : (part + 1) * K], x_raw[:], part * P, P)
+            interleave(lambda dst, src: nc.gpsimd.tensor_scalar(dst, src, 1.0, 0.0, MULT, ADD), xd_words[:, part * K : (part + 1) * K], x_raw[:], part * P, P)
 
         q_words = [tile(f"q_words{half}", PACK * HALF, BF16) for half in range(2)]
         for half in range(2):

@@ -91,7 +91,7 @@ def tile_attend_gadal_kernel(tc, xT, qT, dyT, pT, lam, us, offs, out_0, out_1):
 
         ident = tile("ident", P, F32)
         make_identity(nc, ident[:])
-        windows = [tile(f"window{n}", PIECES, F32) for n in range(WINDOWS)]
+        windows = [tile(f"window{n}", PIECES, F32) for n in range(WINDOWS - 1)]
         for window in windows:
             nc.vector.memset(window[:], 0.0)
 
@@ -108,11 +108,17 @@ def tile_attend_gadal_kernel(tc, xT, qT, dyT, pT, lam, us, offs, out_0, out_1):
                 spread[:].rearrange("p (c n) -> p n c", c=PACK),
                 COPY,
             )
+        windows.append(tile("window_last", PIECES, F32, tag="lam_cols"))
+        nc.gpsimd.memset(windows[-1][:], 0.0)
         lam_slots = tile("lam_slots", SLOTS, F32)
         nc.vector.tensor_copy(lam_slots[:], lam_table[:].indirect(offsets[:]))
 
-        p_words = tile("p_words", PACK * SLOTS, BF16)
-        for t in range(PACK):
+        p_pairs = tile("p_pairs", 2 * SLOTS, BF16)
+        for t in range(2):
+            nc.vector.tensor_copy(p_pairs[:, t : 2 * SLOTS : 2], p_tables[t][:].indirect(offsets[:]))
+        p_words = tile("p_words", PACK * SLOTS, BF16, tag="lam_table")
+        nc.scalar.copy(p_words[:].bitcast(U32)[:, 0 : 2 * SLOTS : 2], p_pairs[:].bitcast(U32))
+        for t in range(2, PACK):
             nc.vector.tensor_copy(p_words[:, t : PACK * SLOTS : PACK], p_tables[t][:].indirect(offsets[:]))
         p_codes = tile("p_codes", SLOTS, U32)
         p_scales = tile("p_scales", SLOTS, U8)

@@ -222,7 +222,7 @@ def tile_attend_gadal_kernel(tc, xT, qT, dyT, pT, lam, us, offs, out_0, out_1):
             place = dealt(q_planes[:, 2 * SLOTS + t % 2 : PACK * SLOTS : 2])
             nc.scalar.activation(place, narrow[:].indirect(offsets[:]), COPY)
 
-        xd_words = tile("xd_words", PACK * K, BF16)
+        xd_words = tile("xd_words", PACK * K, BF16, tag="xr_words2")
         for part in range(PACK):
             interleave(lambda dst, src: nc.gpsimd.tensor_scalar(dst, src, 1.0, 0.0, MULT, ADD), xd_words[:, part * K : (part + 1) * K], x_raw[:], part * P, P)
 

@@ -165,10 +165,9 @@ def tile_attend_gadal_kernel(tc, xT, qT, dyT, pT, lam, us, offs, out_0, out_1):
         xr_first = tile("xr_codes0", P, U32)
         xr = [x_along_rows(0, "turn0", xr_first[:])]
 
-        g_words = tile("g_words", PACK * SLOTS, BF16)
         g_codes = tile("g_codes", SLOTS, U32)
         g_scales = tile("g_scales", SLOTS, U8)
-        g_halves = [g_words[:, half * PACK * HALF : (half + 1) * PACK * HALF] for half in range(2)]
+        g_halves = [tile(f"g_words{half}", PACK * HALF, BF16)[:] for half in range(2)]
         for half in range(2):
             interleave(nc.vector.tensor_copy, g_halves[half], g_planes[:], half * HALF, HALF)
         for half in range(2):
@@ -191,7 +190,7 @@ def tile_attend_gadal_kernel(tc, xT, qT, dyT, pT, lam, us, offs, out_0, out_1):
 
         dq_out(0, dq_product(0, "dq0"), "dq_sb0")
 
-        xr_rest = tile("xr_rest", (PACK - 1) * P, U32, tag="g_planes")
+        xr_rest = tile("xr_rest", (PACK - 1) * P, U32, tag="g_words0")
         xr.append(x_along_rows(1, "turn1", xr_rest[:, 0:P]))
         xr.append(x_along_rows(2, "dq1", xr_rest[:, P : 2 * P]))
         dq_out(1, dq_product(1, "turn1"), "dq_sb1")
@@ -209,22 +208,31 @@ def tile_attend_gadal_kernel(tc, xT, qT, dyT, pT, lam, us, offs, out_0, out_1):
 
         w_planes = {t: w_plane(t, f"w_plane{t}") for t in order}
 
-        q_planes = tile("q_planes", PACK * SLOTS, BF16, tag="g_words")
-        for t in range(2):
-            nc.vector.tensor_copy(dealt(q_planes[:, t : 2 * SLOTS : 2]), q_tables[t][:].indirect(offsets[:]))
+        q_planes = tile("q_planes", PACK * SLOTS, BF16, tag="g_words1")
+        nc.vector.tensor_copy(dealt(q_planes[:, 0 : 2 * SLOTS : 2]), q_tables[0][:].indirect(offsets[:]))
         xr.append(x_along_rows(3, "turn0", xr_rest[:, 2 * P : 3 * P]))
         last_acc = dq_product(3, "turn0")
-        for t, tag in ((2, "xr_codes0"), (3, "q_narrow3")):
-            narrow = tile(f"q_narrow{t}", PIECES, BF16, tag=tag)
+        for t in range(1, PACK):
+            narrow = tile(f"q_narrow{t}", PIECES, BF16, tag="q_table0" if t == 1 else None)
             for half in range(2):
                 cols = slice(half * PIECES // 2, (half + 1) * PIECES // 2)
-                nc.scalar.activation(narrow[:, cols], q_tables[t][:, cols], COPY)
-            place = dealt(q_planes[:, 2 * SLOTS + t % 2 : PACK * SLOTS : 2])
+                if t == 1:
+                    nc.scalar.activation(narrow[:, cols], q_tables[t][:, cols], COPY)
+                else:
+                    nc.gpsimd.tensor_copy(narrow[:, cols], q_tables[t][:, cols])
+            first = 2 * SLOTS * (t // 2)
+            place = dealt(q_planes[:, first + t % 2 : first + 2 * SLOTS : 2])
             nc.scalar.activation(place, narrow[:].indirect(offsets[:]), COPY)
 
-        xd_words = tile("xd_words", PACK * K, BF16, tag="xr_words2")
+        xd_words = [tile("xd_words0", 2 * K, BF16), tile("xd_words1", 2 * K, BF16, tag="xr_words2")]
         for part in range(PACK):
-            interleave(lambda dst, src: nc.gpsimd.tensor_scalar(dst, src, 1.0, 0.0, MULT, ADD), xd_words[:, part * K : (part + 1) * K], x_raw[:], part * P, P)
+            interleave(
+                lambda dst, src: nc.gpsimd.tensor_scalar(dst, src, 1.0, 0.0, MULT, ADD),
+                xd_words[part // 2][:, part % 2 * K : (part % 2 + 1) * K],
+                x_raw[:],
+                part * P,
+                P,
+            )
 
         q_words = [tile(f"q_words{half}", PACK * HALF, BF16) for half in range(2)]
         for half in range(2):
@@ -240,11 +248,13 @@ def tile_attend_gadal_kernel(tc, xT, qT, dyT, pT, lam, us, offs, out_0, out_1):
             quantize(q_codes[:, cols], q_scales[:, cols], q_words[half][:], E4M3)
         xd_codes = tile("xd_codes", K, U32, tag="q_words1")
         xd_scales = tile("xd_scales", K, U8)
-        quantize(xd_codes[:], xd_scales[:], xd_words[:], E4M3)
+        for half in range(2):
+            cols = slice(half * HALF, (half + 1) * HALF)
+            quantize(xd_codes[:, cols], xd_scales[:, cols], xd_words[half][:], E4M3)
 
         dq_out(3, last_acc, "q_words0")
 
-        w_turned = tile("w_turned", PACK * K, F32, tag="g_words")
+        w_turned = tile("w_turned", PACK * K, F32, tag="g_words1")
         for b in range(PACK):
             turned = bank(f"w_bank{b}", f"v{order[b]}")
             for t in order:

@@ -208,7 +208,7 @@ def tile_attend_gadal_kernel(tc, xT, qT, dyT, pT, lam, us, offs, out_0, out_1):
 
         w_planes = {t: w_plane(t, f"w_plane{t}") for t in order}
 
-        q_planes = tile("q_planes", PACK * SLOTS, BF16, tag="g_words1")
+        q_planes = tile("q_planes", PACK * SLOTS, BF16)
         nc.vector.tensor_copy(dealt(q_planes[:, 0 : 2 * SLOTS : 2]), q_tables[0][:].indirect(offsets[:]))
         xr.append(x_along_rows(3, "turn0", xr_rest[:, 2 * P : 3 * P]))
         last_acc = dq_product(3, "turn0")
@@ -241,12 +241,12 @@ def tile_attend_gadal_kernel(tc, xT, qT, dyT, pT, lam, us, offs, out_0, out_1):
                 q_planes[:].bitcast(U32).rearrange("p (j s) -> p s j", j=2)[:, half * HALF : (half + 1) * HALF],
             )
 
-        q_codes = tile("q_codes", SLOTS, U32, tag="dq_sb2")
+        q_codes = tile("q_codes", SLOTS, U32)
         q_scales = tile("q_scales", SLOTS, U8)
         for half in range(2):
             cols = slice(half * HALF, (half + 1) * HALF)
             quantize(q_codes[:, cols], q_scales[:, cols], q_words[half][:], E4M3)
-        xd_codes = tile("xd_codes", K, U32, tag="q_words1")
+        xd_codes = tile("xd_codes", K, U32, tag="q_planes")
         xd_scales = tile("xd_scales", K, U8)
         for half in range(2):
             cols = slice(half * HALF, (half + 1) * HALF)
@@ -254,7 +254,7 @@ def tile_attend_gadal_kernel(tc, xT, qT, dyT, pT, lam, us, offs, out_0, out_1):
 
         dq_out(3, last_acc, "q_words0")
 
-        w_turned = tile("w_turned", PACK * K, F32, tag="g_words1")
+        w_turned = tile("w_turned", PACK * K, F32, tag="q_narrow3")
         for b in range(PACK):
             turned = bank(f"w_bank{b}", f"v{order[b]}")
             for t in order:

@@ -11,7 +11,6 @@ U8 = mybir.dt.uint8
 E4M3 = mybir.dt.float8_e4m3fn_x4
 E5M2 = mybir.dt.float8_e5m2_x4
 MULT = mybir.AluOpType.mult
-ADD = mybir.AluOpType.add
 COPY = mybir.ActivationFunctionType.Copy
 
 P = 128
@@ -77,7 +76,8 @@ def tile_attend_gadal_kernel(tc, xT, qT, dyT, pT, lam, us, offs, out_0, out_1):
         q_rows = qT.rearrange("(p t) n -> t p n", t=PACK)
         x_rows = xT.rearrange("(p t) r -> p (t r)", t=PACK)
         p_tables = [tile(f"p_table{t}", PIECES, F32) for t in range(PACK)]
-        q_tables = [tile(f"q_table{t}", PIECES, F32) for t in range(PACK)]
+        q_tables = {t: tile(f"q_table{t}", PIECES, F32) for t in range(1, PACK)}
+        q_first = [tile(f"q_first{half}", PIECES // 2, F32) for half in range(2)]
         dy_raw = tile("dy_raw", PACK * K, F32)
         x_raw = tile("x_raw", PACK * K, F32)
         for t in range(PACK):
@@ -85,9 +85,12 @@ def tile_attend_gadal_kernel(tc, xT, qT, dyT, pT, lam, us, offs, out_0, out_1):
         nc.sync.dma_start(us_cols[:], us.rearrange("(p t) o -> p (t o)", t=PACK))
         nc.sync.dma_start(dy_raw[:], dyT.rearrange("(p t) r -> p (t r)", t=PACK))
         nc.sync.dma_start(x_raw[:, 0:K], x_rows[:, 0:K])
+        nc.sync.dma_start(q_first[0][:], q_rows[0][:, 0 : PIECES // 2])
         nc.sync.dma_start(x_raw[:, K:], x_rows[:, K:])
-        for t in range(PACK):
+        for t in (1, 2):
             nc.sync.dma_start(q_tables[t][:], q_rows[t])
+        nc.sync.dma_start(q_first[1][:], q_rows[0][:, PIECES // 2 :])
+        nc.sync.dma_start(q_tables[3][:], q_rows[3])
 
         ident = tile("ident", P, F32)
         make_identity(nc, ident[:])
@@ -209,32 +212,39 @@ def tile_attend_gadal_kernel(tc, xT, qT, dyT, pT, lam, us, offs, out_0, out_1):
         w_planes = {t: w_plane(t, f"w_plane{t}") for t in order}
 
         q_planes = tile("q_planes", PACK * SLOTS, BF16)
-        nc.vector.tensor_copy(dealt(q_planes[:, 0 : 2 * SLOTS : 2]), q_tables[0][:].indirect(offsets[:]))
         xr.append(x_along_rows(3, "turn0", xr_rest[:, 2 * P : 3 * P]))
         last_acc = dq_product(3, "turn0")
-        for t in range(1, PACK):
-            narrow = tile(f"q_narrow{t}", PIECES, BF16, tag="q_table0" if t == 1 else None)
-            for half in range(2):
-                cols = slice(half * PIECES // 2, (half + 1) * PIECES // 2)
-                if t == 1:
-                    nc.scalar.activation(narrow[:, cols], q_tables[t][:, cols], COPY)
-                else:
-                    nc.gpsimd.tensor_copy(narrow[:, cols], q_tables[t][:, cols])
+        xd_codes = tile("xd_codes", K, U32)
+        xd_scales = tile("xd_scales", K, U8)
+
+        def x_along_features(half, tag):
+            words = tile(f"xd_words{half}", 2 * K, BF16, tag=tag)
+            for part in range(2):
+                first = (2 * half + part) * P
+                nc.gpsimd.tensor_copy(
+                    words[:, part * K : (part + 1) * K].rearrange("p (r j) -> p r j", j=PACK),
+                    x_raw[:].rearrange("p (j r) -> p r j", j=PACK)[:, first : first + P],
+                )
+            cols = slice(half * HALF, (half + 1) * HALF)
+            quantize(xd_codes[:, cols], xd_scales[:, cols], words[:], E4M3)
+
+        narrow = {0: tile("q_narrow0", PIECES, BF16)}
+        nc.gpsimd.tensor_copy(narrow[0][:, 0 : PIECES // 2], q_first[0][:])
+        x_along_features(0, "xd_words0")
+        for t in (1, 2, 0, 3):
+            if t == 0:
+                nc.scalar.activation(narrow[0][:, PIECES // 2 :], q_first[1][:], COPY)
+            else:
+                narrow[t] = tile(f"q_narrow{t}", PIECES, BF16, tag="xd_words0" if t == 1 else None)
+                for half in range(2):
+                    cols = slice(half * PIECES // 2, (half + 1) * PIECES // 2)
+                    nc.gpsimd.tensor_copy(narrow[t][:, cols], q_tables[t][:, cols])
             first = 2 * SLOTS * (t // 2)
             place = dealt(q_planes[:, first + t % 2 : first + 2 * SLOTS : 2])
-            nc.scalar.activation(place, narrow[:].indirect(offsets[:]), COPY)
+            nc.scalar.activation(place, narrow[t][:].indirect(offsets[:]), COPY)
+        x_along_features(1, "q_table3")
 
-        xd_words = [tile("xd_words0", 2 * K, BF16), tile("xd_words1", 2 * K, BF16, tag="xr_words2")]
-        for part in range(PACK):
-            interleave(
-                lambda dst, src: nc.gpsimd.tensor_scalar(dst, src, 1.0, 0.0, MULT, ADD),
-                xd_words[part // 2][:, part % 2 * K : (part % 2 + 1) * K],
-                x_raw[:],
-                part * P,
-                P,
-            )
-
-        q_words = [tile(f"q_words{half}", PACK * HALF, BF16) for half in range(2)]
+        q_words = [tile("q_words0", PACK * HALF, BF16, tag="x_raw"), tile("q_words1", PACK * HALF, BF16, tag="q_narrow3")]
         for half in range(2):
             nc.scalar.copy(
                 q_words[half][:].bitcast(U32).rearrange("p (s j) -> p s j", j=2),
@@ -246,17 +256,13 @@ def tile_attend_gadal_kernel(tc, xT, qT, dyT, pT, lam, us, offs, out_0, out_1):
         for half in range(2):
             cols = slice(half * HALF, (half + 1) * HALF)
             quantize(q_codes[:, cols], q_scales[:, cols], q_words[half][:], E4M3)
-        xd_codes = tile("xd_codes", K, U32, tag="q_planes")
-        xd_scales = tile("xd_scales", K, U8)
-        for half in range(2):
-            cols = slice(half * HALF, (half + 1) * HALF)
-            quantize(xd_codes[:, cols], xd_scales[:, cols], xd_words[half][:], E4M3)
 
-        dq_out(3, last_acc, "q_words0")
+        dq_out(3, last_acc, "q_planes")
 
-        w_turned = tile("w_turned", PACK * K, F32, tag="q_narrow3")
-        for b in range(PACK):
-            turned = bank(f"w_bank{b}", f"v{order[b]}")
+        w_turned = tile("w_turned", PACK * K, F32, tag="x_raw")
+
+        def turn_w(b):
+            turned = bank(f"w_bank{b}", ("dq0", "turn1", "dq1", "turn0")[b])
             for t in order:
                 nc.tensor.transpose(turned[:, t * P : (t + 1) * P], w_planes[t][:, b * P : (b + 1) * P], ident[:])
             nc.scalar.copy(
@@ -264,25 +270,35 @@ def tile_attend_gadal_kernel(tc, xT, qT, dyT, pT, lam, us, offs, out_0, out_1):
                 turned[:].rearrange("p (t m) -> p m t", t=PACK),
             )
 
+        def u_product(b):
+            cols = slice(b * P, (b + 1) * P)
+            u = bank(f"u{b}", f"v{order[b]}")
+            matmul(u[:], q_codes[:, cols], q_scales[:, cols], E4M3, xd_codes[:], xd_scales[:], E4M3)
+            return u
+
         sums = tile("sums", QUAD, F32)
         nc.gpsimd.memset(sums[:], 0.0)
-        for b, bank_tag in enumerate(("dq0", "dq1", "turn1", "turn0")):
-            cols = slice(b * P, (b + 1) * P)
-            u = bank(f"u{b}", bank_tag)
-            matmul(u[:], q_codes[:, cols], q_scales[:, cols], E4M3, xd_codes[:], xd_scales[:], E4M3)
-            col = b * QUAD // PACK
-            products = tile(f"products{b}", K, F32)
-            if b == 0:
-                u_copy = tile("u_copy", K, F32)
-                nc.scalar.copy(u_copy[:], u[:])
-                nc.gpsimd.tensor_tensor(products[:], u_copy[:], w_turned[:, b * K : (b + 1) * K], MULT)
-                spent = tile("spent", K, BF16)
-                late = (spent, products, col)
-            else:
-                nc.vector.scalar_tensor_tensor(
-                    products[:], u[:], 1.0, w_turned[:, b * K : (b + 1) * K], MULT, MULT, accum_out=sums[:, col : col + 1]
-                )
-        nc.scalar.activation(late[0][:], late[1][:], COPY, accum_out=sums[:, late[2] : late[2] + 1])
+        step = QUAD // PACK
+        products = [tile(f"products{b}", K, F32) for b in range(PACK)]
+
+        turn_w(0)
+        u_copy = tile("u_copy", K, F32)
+        nc.scalar.copy(u_copy[:], u_product(0)[:])
+        nc.gpsimd.tensor_tensor(products[0][:], u_copy[:], w_turned[:, 0:K], MULT)
+        for b in range(1, PACK):
+            turn_w(b)
+        for b in range(1, PACK):
+            nc.vector.scalar_tensor_tensor(
+                products[b][:],
+                u_product(b)[:],
+                1.0,
+                w_turned[:, b * K : (b + 1) * K],
+                MULT,
+                MULT,
+                accum_out=sums[:, b * step : b * step + 1],
+            )
+        spent = tile("spent", K, BF16)
+        nc.scalar.activation(spent[:], products[0][:], COPY, accum_out=sums[:, 0:1])
         s_rows = tile("s_rows", QUAD, F32)
         nc.vector.transpose(s_rows[:], sums[:])
-        nc.sync.dma_start(out_0.rearrange("o (n k) -> (o n) k", k=QUAD), s_rows[0:P : QUAD // PACK, :])
+        nc.sync.dma_start(out_0.rearrange("o (n k) -> (o n) k", k=QUAD), s_rows[0:P:step, :])

@@ -76,8 +76,12 @@ def tile_attend_gadal_kernel(tc, xT, qT, dyT, pT, lam, us, offs, out_0, out_1):
         q_rows = qT.rearrange("(p t) n -> t p n", t=PACK)
         x_rows = xT.rearrange("(p t) r -> p (t r)", t=PACK)
         p_tables = [tile(f"p_table{t}", PIECES, F32) for t in range(PACK)]
-        q_tables = {t: tile(f"q_table{t}", PIECES, F32) for t in range(1, PACK)}
-        q_first = [tile(f"q_first{half}", PIECES // 2, F32) for half in range(2)]
+        q_tables = {t: tile(f"q_table{t}", PIECES, F32) for t in (1, 2, 3)}
+        q_halves = {(t, half): tile(f"q_half{t}{half}", PIECES // 2, F32) for t in (0,) for half in range(2)}
+
+        def load_q_half(t, half):
+            nc.sync.dma_start(q_halves[t, half][:], q_rows[t][:, half * PIECES // 2 : (half + 1) * PIECES // 2])
+
         dy_raw = tile("dy_raw", PACK * K, F32)
         x_raw = tile("x_raw", PACK * K, F32)
         for t in range(PACK):
@@ -85,11 +89,11 @@ def tile_attend_gadal_kernel(tc, xT, qT, dyT, pT, lam, us, offs, out_0, out_1):
         nc.sync.dma_start(us_cols[:], us.rearrange("(p t) o -> p (t o)", t=PACK))
         nc.sync.dma_start(dy_raw[:], dyT.rearrange("(p t) r -> p (t r)", t=PACK))
         nc.sync.dma_start(x_raw[:, 0:K], x_rows[:, 0:K])
-        nc.sync.dma_start(q_first[0][:], q_rows[0][:, 0 : PIECES // 2])
+        load_q_half(0, 0)
         nc.sync.dma_start(x_raw[:, K:], x_rows[:, K:])
-        for t in (1, 2):
-            nc.sync.dma_start(q_tables[t][:], q_rows[t])
-        nc.sync.dma_start(q_first[1][:], q_rows[0][:, PIECES // 2 :])
+        nc.sync.dma_start(q_tables[1][:], q_rows[1])
+        nc.sync.dma_start(q_tables[2][:], q_rows[2])
+        load_q_half(0, 1)
         nc.sync.dma_start(q_tables[3][:], q_rows[3])
 
         ident = tile("ident", P, F32)
@@ -184,20 +188,42 @@ def tile_attend_gadal_kernel(tc, xT, qT, dyT, pT, lam, us, offs, out_0, out_1):
             matmul(acc[:], xr[j][0], xr[j][1], E4M3, g_codes[:], g_scales[:], E5M2)
             return acc
 
-        def dq_out(j, acc, tag):
+        def dq_copy(j, acc, tag):
             dq = tile(f"dq{j}", SLOTS, F32, tag=tag)
             nc.scalar.copy(dq[:], acc[:])
+            return dq
+
+        def dq_out(j, dq):
             window = windows[j % WINDOWS]
             nc.vector.tensor_copy(window[:].indirect(offsets[:]), dq[:])
             nc.sync.dma_start(out_rows[j], window[:])
 
-        dq_out(0, dq_product(0, "dq0"), "dq_sb0")
+        first_dq = dq_copy(0, dq_product(0, "dq0"), "dq_sb0")
+        xd_codes = tile("xd_codes", K, U32)
+        xd_scales = tile("xd_scales", K, U8)
+
+        def x_along_features(half, tag):
+            words = tile(f"xd_words{half}", 2 * K, BF16, tag=tag)
+            nc.gpsimd.tensor_copy(
+                words[:].rearrange("p (r j) -> p r j", j=PACK),
+                x_raw[:].rearrange("p (j r) -> p r j", j=PACK)[:, half * HALF : (half + 1) * HALF],
+            )
+            cols = slice(half * HALF, (half + 1) * HALF)
+            quantize(xd_codes[:, cols], xd_scales[:, cols], words[:], E4M3)
+
+        narrow = {0: tile("q_narrow0", PIECES, BF16, tag="dy_words0")}
+        nc.gpsimd.tensor_copy(narrow[0][:, 0 : PIECES // 2], q_halves[0, 0][:])
+        x_along_features(0, "xd_words0")
+        narrow[1] = tile("q_narrow1", PIECES, BF16, tag="g_words1")
+        nc.vector.tensor_copy(narrow[1][:], q_tables[1][:])
 
         xr_rest = tile("xr_rest", (PACK - 1) * P, U32, tag="g_words0")
         xr.append(x_along_rows(1, "turn1", xr_rest[:, 0:P]))
         xr.append(x_along_rows(2, "dq1", xr_rest[:, P : 2 * P]))
-        dq_out(1, dq_product(1, "turn1"), "dq_sb1")
-        dq_out(2, dq_product(2, "dq1"), "dq_sb2")
+        xr.append(x_along_rows(3, "turn0", xr_rest[:, 2 * P : 3 * P]))
+        dq_out(0, first_dq)
+        dq_out(1, dq_copy(1, dq_product(1, "turn1"), "dq_sb1"))
+        dq_out(2, dq_copy(2, dq_product(2, "dq1"), "dq_sb2"))
 
         def w_plane(t, tag):
             plane = tile(f"w_plane{t}", SLOTS, F32, tag=tag)
@@ -212,33 +238,13 @@ def tile_attend_gadal_kernel(tc, xT, qT, dyT, pT, lam, us, offs, out_0, out_1):
         w_planes = {t: w_plane(t, f"w_plane{t}") for t in order}
 
         q_planes = tile("q_planes", PACK * SLOTS, BF16)
-        xr.append(x_along_rows(3, "turn0", xr_rest[:, 2 * P : 3 * P]))
         last_acc = dq_product(3, "turn0")
-        xd_codes = tile("xd_codes", K, U32)
-        xd_scales = tile("xd_scales", K, U8)
-
-        def x_along_features(half, tag):
-            words = tile(f"xd_words{half}", 2 * K, BF16, tag=tag)
-            for part in range(2):
-                first = (2 * half + part) * P
-                nc.gpsimd.tensor_copy(
-                    words[:, part * K : (part + 1) * K].rearrange("p (r j) -> p r j", j=PACK),
-                    x_raw[:].rearrange("p (j r) -> p r j", j=PACK)[:, first : first + P],
-                )
-            cols = slice(half * HALF, (half + 1) * HALF)
-            quantize(xd_codes[:, cols], xd_scales[:, cols], words[:], E4M3)
-
-        narrow = {0: tile("q_narrow0", PIECES, BF16)}
-        nc.gpsimd.tensor_copy(narrow[0][:, 0 : PIECES // 2], q_first[0][:])
-        x_along_features(0, "xd_words0")
         for t in (1, 2, 0, 3):
             if t == 0:
-                nc.scalar.activation(narrow[0][:, PIECES // 2 :], q_first[1][:], COPY)
-            else:
-                narrow[t] = tile(f"q_narrow{t}", PIECES, BF16, tag="xd_words0" if t == 1 else None)
-                for half in range(2):
-                    cols = slice(half * PIECES // 2, (half + 1) * PIECES // 2)
-                    nc.gpsimd.tensor_copy(narrow[t][:, cols], q_tables[t][:, cols])
+                nc.gpsimd.tensor_copy(narrow[t][:, PIECES // 2 :], q_halves[t, 1][:])
+            elif t > 1:
+                narrow[t] = tile(f"q_narrow{t}", PIECES, BF16, tag="xr_words3" if t == 2 else None)
+                nc.gpsimd.tensor_copy(narrow[t][:], q_tables[t][:])
             first = 2 * SLOTS * (t // 2)
             place = dealt(q_planes[:, first + t % 2 : first + 2 * SLOTS : 2])
             nc.scalar.activation(place, narrow[t][:].indirect(offsets[:]), COPY)
@@ -257,7 +263,7 @@ def tile_attend_gadal_kernel(tc, xT, qT, dyT, pT, lam, us, offs, out_0, out_1):
             cols = slice(half * HALF, (half + 1) * HALF)
             quantize(q_codes[:, cols], q_scales[:, cols], q_words[half][:], E4M3)
 
-        dq_out(3, last_acc, "q_planes")
+        dq_out(3, dq_copy(3, last_acc, "q_planes"))
 
         w_turned = tile("w_turned", PACK * K, F32, tag="x_raw")
 

@@ -76,12 +76,7 @@ def tile_attend_gadal_kernel(tc, xT, qT, dyT, pT, lam, us, offs, out_0, out_1):
         q_rows = qT.rearrange("(p t) n -> t p n", t=PACK)
         x_rows = xT.rearrange("(p t) r -> p (t r)", t=PACK)
         p_tables = [tile(f"p_table{t}", PIECES, F32) for t in range(PACK)]
-        q_tables = {t: tile(f"q_table{t}", PIECES, F32) for t in (1, 2, 3)}
-        q_halves = {(t, half): tile(f"q_half{t}{half}", PIECES // 2, F32) for t in (0,) for half in range(2)}
-
-        def load_q_half(t, half):
-            nc.sync.dma_start(q_halves[t, half][:], q_rows[t][:, half * PIECES // 2 : (half + 1) * PIECES // 2])
-
+        q_tables = [tile(f"q_table{t}", PIECES, F32) for t in range(PACK)]
         dy_raw = tile("dy_raw", PACK * K, F32)
         x_raw = tile("x_raw", PACK * K, F32)
         for t in range(PACK):
@@ -89,12 +84,9 @@ def tile_attend_gadal_kernel(tc, xT, qT, dyT, pT, lam, us, offs, out_0, out_1):
         nc.sync.dma_start(us_cols[:], us.rearrange("(p t) o -> p (t o)", t=PACK))
         nc.sync.dma_start(dy_raw[:], dyT.rearrange("(p t) r -> p (t r)", t=PACK))
         nc.sync.dma_start(x_raw[:, 0:K], x_rows[:, 0:K])
-        load_q_half(0, 0)
         nc.sync.dma_start(x_raw[:, K:], x_rows[:, K:])
-        nc.sync.dma_start(q_tables[1][:], q_rows[1])
-        nc.sync.dma_start(q_tables[2][:], q_rows[2])
-        load_q_half(0, 1)
-        nc.sync.dma_start(q_tables[3][:], q_rows[3])
+        for t in range(PACK):
+            nc.sync.dma_start(q_tables[t][:], q_rows[t])
 
         ident = tile("ident", P, F32)
         make_identity(nc, ident[:])
@@ -125,11 +117,17 @@ def tile_attend_gadal_kernel(tc, xT, qT, dyT, pT, lam, us, offs, out_0, out_1):
             nc.vector.tensor_copy(p_pairs[:, t : 2 * SLOTS : 2], p_tables[t][:].indirect(offsets[:]))
         p_words = tile("p_words", PACK * SLOTS, BF16, tag="lam_table")
         nc.scalar.copy(p_words[:].bitcast(U32)[:, 0 : 2 * SLOTS : 2], p_pairs[:].bitcast(U32))
-        for t in range(2, PACK):
-            nc.vector.tensor_copy(p_words[:, t : PACK * SLOTS : PACK], p_tables[t][:].indirect(offsets[:]))
+        nc.vector.tensor_copy(p_words[:, 2 : PACK * SLOTS : PACK], p_tables[2][:].indirect(offsets[:]))
+        for half in range(2):
+            nc.vector.tensor_copy(
+                p_words[:, half * PACK * HALF + 3 : (half + 1) * PACK * HALF : PACK],
+                p_tables[3][:].indirect(offsets[:, half * HALF // 16 : (half + 1) * HALF // 16]),
+            )
         p_codes = tile("p_codes", SLOTS, U32)
         p_scales = tile("p_scales", SLOTS, U8)
-        quantize(p_codes[:], p_scales[:], p_words[:], E4M3)
+        for half in range(2):
+            cols = slice(half * HALF, (half + 1) * HALF)
+            quantize(p_codes[:, cols], p_scales[:, cols], p_words[:, half * PACK * HALF : (half + 1) * PACK * HALF], E4M3)
 
         dy_view = dy_raw[:].rearrange("p (j m t) -> p m j t", j=PACK, t=PACK)
         dy_codes, dy_scales = {}, {}
@@ -211,11 +209,9 @@ def tile_attend_gadal_kernel(tc, xT, qT, dyT, pT, lam, us, offs, out_0, out_1):
             cols = slice(half * HALF, (half + 1) * HALF)
             quantize(xd_codes[:, cols], xd_scales[:, cols], words[:], E4M3)
 
-        narrow = {0: tile("q_narrow0", PIECES, BF16, tag="dy_words0")}
-        nc.gpsimd.tensor_copy(narrow[0][:, 0 : PIECES // 2], q_halves[0, 0][:])
         x_along_features(0, "xd_words0")
-        narrow[1] = tile("q_narrow1", PIECES, BF16, tag="g_words1")
-        nc.vector.tensor_copy(narrow[1][:], q_tables[1][:])
+        narrow = {0: tile("q_narrow0", PIECES, BF16, tag="g_words1")}
+        nc.vector.tensor_copy(narrow[0][:], q_tables[0][:])
 
         xr_rest = tile("xr_rest", (PACK - 1) * P, U32, tag="g_words0")
         xr.append(x_along_rows(1, "turn1", xr_rest[:, 0:P]))
@@ -239,11 +235,13 @@ def tile_attend_gadal_kernel(tc, xT, qT, dyT, pT, lam, us, offs, out_0, out_1):
 
         q_planes = tile("q_planes", PACK * SLOTS, BF16)
         last_acc = dq_product(3, "turn0")
-        for t in (1, 2, 0, 3):
-            if t == 0:
-                nc.gpsimd.tensor_copy(narrow[t][:, PIECES // 2 :], q_halves[t, 1][:])
+        for t in range(PACK):
+            if t == 1:
+                narrow[t] = tile(f"q_narrow{t}", PIECES, BF16, tag="xr_words3")
+                nc.gpsimd.tensor_copy(narrow[t][:, PIECES // 2 :], q_tables[t][:, PIECES // 2 :])
+                nc.scalar.activation(narrow[t][:, 0 : PIECES // 2], q_tables[t][:, 0 : PIECES // 2], COPY)
             elif t > 1:
-                narrow[t] = tile(f"q_narrow{t}", PIECES, BF16, tag="xr_words3" if t == 2 else None)
+                narrow[t] = tile(f"q_narrow{t}", PIECES, BF16)
                 nc.gpsimd.tensor_copy(narrow[t][:], q_tables[t][:])
             first = 2 * SLOTS * (t // 2)
             place = dealt(q_planes[:, first + t % 2 : first + 2 * SLOTS : 2])

@@ -11,7 +11,9 @@ U8 = mybir.dt.uint8
 E4M3 = mybir.dt.float8_e4m3fn_x4
 E5M2 = mybir.dt.float8_e5m2_x4
 MULT = mybir.AluOpType.mult
+ADD = mybir.AluOpType.add
 COPY = mybir.ActivationFunctionType.Copy
+ALONG_FREE = mybir.AxisListType.X
 
 P = 128
 PACK = 4
@@ -19,25 +21,14 @@ K = P * PACK
 SLOTS = 512
 PIECES = 2048
 HALF = SLOTS // 2
-RUN = 4
 QUAD = 32
-WINDOWS = 3
 
 FLOPS = 3 * 2 * K * K * SLOTS
 BYTES = 4 * (2 * K * K + 3 * K * PIECES + PIECES + K + SLOTS) + 2 * P * SLOTS // 16
 
 
-def interleave(copy, dst, planes, first, count):
-    copy(
-        dst.rearrange("p (c i t) -> p c t i", i=RUN, t=PACK),
-        planes.rearrange("p (t n) -> p t n", t=PACK)[:, :, first : first + count].rearrange(
-            "p t (c i) -> p c t i", i=RUN
-        ),
-    )
-
-
-def dealt(ap):
-    return ap.rearrange("p (b a k) -> p a b k", b=PACK, a=PACK)
+def halves(half, width=HALF):
+    return slice(half * width, (half + 1) * width)
 
 
 def tile_attend_gadal_kernel(tc, xT, qT, dyT, pT, lam, us, offs, out_0, out_1):
@@ -66,12 +57,6 @@ def tile_attend_gadal_kernel(tc, xT, qT, dyT, pT, lam, us, offs, out_0, out_1):
                 stop=True,
             )
 
-        offsets = tile("offsets", SLOTS // 16, U16)
-        nc.sync.dma_start(offsets[:], offs)
-        lam_cols = tile("lam_cols", PIECES // P, F32)
-        nc.sync.dma_start(lam_cols[:], lam[0:1, :].rearrange("o (p c) -> (o p) c", p=P))
-        us_cols = tile("us_cols", PACK, F32)
-
         p_rows = pT.rearrange("(p t) n -> t p n", t=PACK)
         q_rows = qT.rearrange("(p t) n -> t p n", t=PACK)
         x_rows = xT.rearrange("(p t) r -> p (t r)", t=PACK)
@@ -79,20 +64,33 @@ def tile_attend_gadal_kernel(tc, xT, qT, dyT, pT, lam, us, offs, out_0, out_1):
         q_tables = [tile(f"q_table{t}", PIECES, F32) for t in range(PACK)]
         dy_raw = tile("dy_raw", PACK * K, F32)
         x_raw = tile("x_raw", PACK * K, F32)
+        offsets = tile("offsets", SLOTS // 16, U16)
+        lam_cols = tile("lam_cols", PIECES // P, F32)
+        us_cols = tile("us_cols", PACK, F32)
+
+        nc.sync.dma_start(lam_cols[:], lam[0:1, :].rearrange("o (p c) -> (o p) c", p=P))
+        nc.sync.dma_start(dy_raw[:], dyT.rearrange("(p t) r -> p (t r)", t=PACK))
+        nc.sync.dma_start(offsets[:], offs)
+        nc.sync.dma_start(us_cols[:], us.rearrange("(p t) o -> p (t o)", t=PACK))
         for t in range(PACK):
             nc.sync.dma_start(p_tables[t][:], p_rows[t])
-        nc.sync.dma_start(us_cols[:], us.rearrange("(p t) o -> p (t o)", t=PACK))
-        nc.sync.dma_start(dy_raw[:], dyT.rearrange("(p t) r -> p (t r)", t=PACK))
         nc.sync.dma_start(x_raw[:, 0:K], x_rows[:, 0:K])
         nc.sync.dma_start(x_raw[:, K:], x_rows[:, K:])
         for t in range(PACK):
             nc.sync.dma_start(q_tables[t][:], q_rows[t])
 
+        def listed(window, half=None):
+            if half is None:
+                return window[:].indirect(offsets[:])
+            return window[:].indirect(offsets[:, halves(half, HALF // 16)])
+
         ident = tile("ident", P, F32)
         make_identity(nc, ident[:])
-        windows = [tile(f"window{n}", PIECES, F32) for n in range(WINDOWS - 1)]
+        sums = tile("sums", QUAD, F32)
+        nc.gpsimd.memset(sums[:], 0.0)
+        windows = [tile(f"window{j}", PIECES, F32) for j in range(2)]
         for window in windows:
-            nc.vector.memset(window[:], 0.0)
+            nc.vector.memset(window[:].bitcast(U32), 0)
 
         lam_table = tile("lam_table", PIECES, F32)
         for group in range(PACK):
@@ -107,202 +105,221 @@ def tile_attend_gadal_kernel(tc, xT, qT, dyT, pT, lam, us, offs, out_0, out_1):
                 spread[:].rearrange("p (c n) -> p n c", c=PACK),
                 COPY,
             )
-        windows.append(tile("window_last", PIECES, F32, tag="lam_cols"))
-        nc.gpsimd.memset(windows[-1][:], 0.0)
         lam_slots = tile("lam_slots", SLOTS, F32)
-        nc.vector.tensor_copy(lam_slots[:], lam_table[:].indirect(offsets[:]))
+        nc.scalar.activation(lam_slots[:], listed(lam_table), COPY)
 
-        p_pairs = tile("p_pairs", 2 * SLOTS, BF16)
+        dy_words = tile("dy_words", PACK * K, BF16)
+        nc.vector.tensor_copy(
+            dy_words[:].rearrange("p (t m j) -> p m j t", t=PACK, j=PACK),
+            dy_raw[:].rearrange("p (j m t) -> p m j t", j=PACK, t=PACK),
+        )
+        dy_codes = tile("dy_codes", K, U32)
+        dy_scales = tile("dy_scales", K, U8)
+        quantize(dy_codes[:], dy_scales[:], dy_words[:], E5M2)
+
+        factors = tile("factors", PACK * SLOTS, F32)
+        nc.vector.tensor_tensor(
+            factors[:].rearrange("p (i t) -> p i t", t=PACK),
+            lam_slots[:].unsqueeze(2).to_broadcast([P, SLOTS, PACK]),
+            us_cols[:].unsqueeze(1).to_broadcast([P, SLOTS, PACK]),
+            MULT,
+        )
+
+        p_planes = tile("p_planes", 2 * SLOTS, BF16, tag="lam_table")
         for t in range(2):
-            nc.vector.tensor_copy(p_pairs[:, t : 2 * SLOTS : 2], p_tables[t][:].indirect(offsets[:]))
-        p_words = tile("p_words", PACK * SLOTS, BF16, tag="lam_table")
-        nc.scalar.copy(p_words[:].bitcast(U32)[:, 0 : 2 * SLOTS : 2], p_pairs[:].bitcast(U32))
-        nc.vector.tensor_copy(p_words[:, 2 : PACK * SLOTS : PACK], p_tables[2][:].indirect(offsets[:]))
+            nc.scalar.activation(p_planes[:, halves(t, SLOTS)], listed(p_tables[t]), COPY)
+        p_tile = tile("p_words", PACK * SLOTS, BF16, tag="lam_slots")
+        p_words = [p_tile[:, halves(half, PACK * HALF)] for half in range(2)]
         for half in range(2):
-            nc.vector.tensor_copy(
-                p_words[:, half * PACK * HALF + 3 : (half + 1) * PACK * HALF : PACK],
-                p_tables[3][:].indirect(offsets[:, half * HALF // 16 : (half + 1) * HALF // 16]),
+            nc.scalar.copy(
+                p_words[half].rearrange("p (c t) -> p c t", t=PACK)[:, :, 0:2],
+                p_planes[:].rearrange("p (t c) -> p c t", t=2)[:, halves(half)],
             )
+        for t in (2, 3):
+            for half in range(2):
+                nc.vector.tensor_copy(p_words[half][:, t : PACK * HALF : PACK], listed(p_tables[t], half))
+        for j, tag in ((2, "dy_words"), (3, "p_table0")):
+            windows.append(tile(f"window{j}", PIECES, F32, tag=tag))
+            nc.gpsimd.memset(windows[j][:], 0.0)
         p_codes = tile("p_codes", SLOTS, U32)
         p_scales = tile("p_scales", SLOTS, U8)
         for half in range(2):
-            cols = slice(half * HALF, (half + 1) * HALF)
-            quantize(p_codes[:, cols], p_scales[:, cols], p_words[:, half * PACK * HALF : (half + 1) * PACK * HALF], E4M3)
+            quantize(p_codes[:, halves(half)], p_scales[:, halves(half)], p_words[half], E4M3)
 
-        dy_view = dy_raw[:].rearrange("p (j m t) -> p m j t", j=PACK, t=PACK)
-        dy_codes, dy_scales = {}, {}
-        for pair, copy in ((1, nc.vector.tensor_copy), (0, nc.scalar.copy)):
-            words = tile(f"dy_words{pair}", 2 * K, BF16)
-            copy(
-                words[:].rearrange("p (t m j) -> p m j t", t=2, j=PACK),
-                dy_view[:, :, :, 2 * pair : 2 * pair + 2],
-            )
-            dy_codes[pair] = tile(f"dy_codes{pair}", 2 * P, U32)
-            dy_scales[pair] = tile(f"dy_scales{pair}", 2 * P, U8)
-            quantize(dy_codes[pair][:], dy_scales[pair][:], words[:], E5M2)
-
-        g_planes = tile("g_planes", PACK * SLOTS, BF16)
-        order = (2, 3, 0, 1)
-        v_banks = {}
-        for t in order:
-            v_banks[t] = bank(f"v{t}", f"v{t}")
-            cols = slice((t % 2) * P, (t % 2 + 1) * P)
-            matmul(
-                v_banks[t][:], dy_codes[t // 2][:, cols], dy_scales[t // 2][:, cols], E5M2, p_codes[:], p_scales[:], E4M3
-            )
-        for t in order:
-            nc.vector.scalar_tensor_tensor(
-                g_planes[:, t * SLOTS : (t + 1) * SLOTS], v_banks[t][:], us_cols[:, t : t + 1], lam_slots[:], MULT, MULT
-            )
-
-        def x_along_rows(j, bank_tag, codes):
-            turned = bank(f"x_turned{j}", bank_tag)
-            for t in range(PACK):
-                nc.tensor.transpose(turned[:, t * P : (t + 1) * P], x_raw[:, j * K + t : (j + 1) * K : PACK], ident[:])
-            words = tile(f"xr_words{j}", K, BF16)
-            nc.scalar.copy(
-                words[:].rearrange("p (c t) -> p c t", t=PACK), turned[:].rearrange("p (t c) -> p c t", t=PACK)
-            )
-            scales = tile(f"xr_scales{j}", P, U8)
-            quantize(codes, scales[:], words[:], E4M3)
-            return codes, scales[:]
-
+        turned = bank("x_turned0", "a0")
+        for t in range(PACK):
+            nc.tensor.transpose(turned[:, halves(t, P)], x_raw[:, t:K:PACK], ident[:])
+        words = tile("xr_words0", K, BF16, tag="lam_table")
+        nc.scalar.copy(words[:].rearrange("p (c t) -> p c t", t=PACK), turned[:].rearrange("p (t c) -> p c t", t=PACK))
         xr_first = tile("xr_codes0", P, U32)
-        xr = [x_along_rows(0, "turn0", xr_first[:])]
+        scales = tile("xr_scales0", P, U8, tag="p_table3")
+        quantize(xr_first[:], scales[:], words[:], E4M3)
+        xr = [(xr_first[:], scales[:])]
 
+        x_narrow = tile("x_narrow", (PACK - 1) * K, BF16, tag="lam_table")
+        for j in range(PACK - 1):
+            nc.gpsimd.tensor_copy(x_narrow[:, halves(j, K)], x_raw[:, halves(j + 1, K)])
+
+        v_banks = []
+        for a in range(PACK):
+            v_banks.append(bank(f"v{a}", f"v{a}"))
+            for t in range(PACK):
+                matmul(
+                    v_banks[a][:, halves(t, P)],
+                    dy_codes[:, halves(t, P)],
+                    dy_scales[:, halves(t, P)],
+                    E5M2,
+                    p_codes[:, halves(a, P)],
+                    p_scales[:, halves(a, P)],
+                    E4M3,
+                )
+
+        g_words = [tile(f"g_words{half}", PACK * HALF, BF16) for half in range(2)]
         g_codes = tile("g_codes", SLOTS, U32)
         g_scales = tile("g_scales", SLOTS, U8)
-        g_halves = [tile(f"g_words{half}", PACK * HALF, BF16)[:] for half in range(2)]
-        for half in range(2):
-            interleave(nc.vector.tensor_copy, g_halves[half], g_planes[:], half * HALF, HALF)
-        for half in range(2):
-            cols = slice(half * HALF, (half + 1) * HALF)
-            quantize(g_codes[:, cols], g_scales[:, cols], g_halves[half], E5M2)
+
+        def form_g(a):
+            nc.vector.tensor_tensor(
+                g_words[a // 2][:, halves(a % 2, K)].rearrange("p (n t) -> p n t", t=PACK),
+                v_banks[a][:].rearrange("p (t n) -> p n t", t=PACK),
+                factors[:, halves(a, K)].rearrange("p (n t) -> p n t", t=PACK),
+                MULT,
+            )
+
+        def quantize_g(half):
+            quantize(g_codes[:, halves(half)], g_scales[:, halves(half)], g_words[half][:], E5M2)
+
+        form_g(0)
+        form_g(1)
+        form_g(2)
+        quantize_g(0)
+        form_g(3)
+        quantize_g(1)
+
+        x_pairs = x_narrow[:].bitcast(F32)
+        xr_words = tile("xr_words", (PACK - 1) * K, BF16)
+        for planes, tag in (((0, 1), "a1"), ((2,), "a0")):
+            turned = bank(f"x_turned{planes[0] + 1}", tag)
+            for n, j in enumerate(planes):
+                for u in range(2):
+                    nc.tensor.transpose(
+                        turned[:, halves(2 * n + u, P)], x_pairs[:, j * HALF + u : (j + 1) * HALF : 2], ident[:]
+                    )
+            nc.scalar.copy(
+                xr_words[:].bitcast(F32)[:, planes[0] * HALF : (planes[-1] + 1) * HALF].rearrange(
+                    "p (j c u) -> p j c u", j=len(planes), u=2
+                ),
+                turned[:, 0 : len(planes) * HALF].rearrange("p (j u c) -> p j c u", j=len(planes), u=2),
+            )
+        xr_codes = tile("xr_codes", (PACK - 1) * P, U32)
+        xr_scales = tile("xr_scales", (PACK - 1) * P, U8)
+        quantize(xr_codes[:], xr_scales[:], xr_words[:], E4M3)
+        for j in range(PACK - 1):
+            xr.append((xr_codes[:, halves(j, P)], xr_scales[:, halves(j, P)]))
 
         out_rows = out_1.rearrange("(p j) n -> j p n", j=PACK)
 
-        def dq_product(j, bank_tag):
-            acc = bank(f"dq_acc{j}", bank_tag)
-            matmul(acc[:], xr[j][0], xr[j][1], E4M3, g_codes[:], g_scales[:], E5M2)
+        def dq_product(j, bank_tag, half=None):
+            acc = bank(f"dq_acc{j}_{half}", bank_tag)
+            cols = slice(0, SLOTS) if half is None else halves(half)
+            matmul(acc[:, cols], xr[j][0], xr[j][1], E4M3, g_codes[:, cols], g_scales[:, cols], E5M2)
             return acc
 
-        def dq_copy(j, acc, tag):
-            dq = tile(f"dq{j}", SLOTS, F32, tag=tag)
-            nc.scalar.copy(dq[:], acc[:])
+        def dq_copy(name, acc, cols, tag=None):
+            dq = tile(name, cols.stop - cols.start, F32, tag=tag)
+            nc.scalar.copy(dq[:], acc[:, cols])
             return dq
 
-        def dq_out(j, dq):
-            window = windows[j % WINDOWS]
-            nc.vector.tensor_copy(window[:].indirect(offsets[:]), dq[:])
-            nc.sync.dma_start(out_rows[j], window[:])
-
-        first_dq = dq_copy(0, dq_product(0, "dq0"), "dq_sb0")
-        xd_codes = tile("xd_codes", K, U32)
-        xd_scales = tile("xd_scales", K, U8)
-
-        def x_along_features(half, tag):
-            words = tile(f"xd_words{half}", 2 * K, BF16, tag=tag)
-            nc.gpsimd.tensor_copy(
-                words[:].rearrange("p (r j) -> p r j", j=PACK),
-                x_raw[:].rearrange("p (j r) -> p r j", j=PACK)[:, half * HALF : (half + 1) * HALF],
-            )
-            cols = slice(half * HALF, (half + 1) * HALF)
-            quantize(xd_codes[:, cols], xd_scales[:, cols], words[:], E4M3)
-
-        x_along_features(0, "xd_words0")
-        narrow = {0: tile("q_narrow0", PIECES, BF16, tag="g_words1")}
-        nc.vector.tensor_copy(narrow[0][:], q_tables[0][:])
-
-        xr_rest = tile("xr_rest", (PACK - 1) * P, U32, tag="g_words0")
-        xr.append(x_along_rows(1, "turn1", xr_rest[:, 0:P]))
-        xr.append(x_along_rows(2, "dq1", xr_rest[:, P : 2 * P]))
-        xr.append(x_along_rows(3, "turn0", xr_rest[:, 2 * P : 3 * P]))
-        dq_out(0, first_dq)
-        dq_out(1, dq_copy(1, dq_product(1, "turn1"), "dq_sb1"))
-        dq_out(2, dq_copy(2, dq_product(2, "dq1"), "dq_sb2"))
-
-        def w_plane(t, tag):
-            plane = tile(f"w_plane{t}", SLOTS, F32, tag=tag)
-            nc.scalar.activation(
-                plane[:].rearrange("p (b a k) -> p a b k", b=PACK, a=PACK),
-                v_banks[t][:].rearrange("p (a b k) -> p a b k", a=PACK, b=PACK),
-                COPY,
-                scale=us_cols[:, t : t + 1],
-            )
-            return plane
-
-        w_planes = {t: w_plane(t, f"w_plane{t}") for t in order}
-
-        q_planes = tile("q_planes", PACK * SLOTS, BF16)
-        last_acc = dq_product(3, "turn0")
-        for t in range(PACK):
-            if t == 1:
-                narrow[t] = tile(f"q_narrow{t}", PIECES, BF16, tag="xr_words3")
-                nc.gpsimd.tensor_copy(narrow[t][:, PIECES // 2 :], q_tables[t][:, PIECES // 2 :])
-                nc.scalar.activation(narrow[t][:, 0 : PIECES // 2], q_tables[t][:, 0 : PIECES // 2], COPY)
-            elif t > 1:
-                narrow[t] = tile(f"q_narrow{t}", PIECES, BF16)
-                nc.gpsimd.tensor_copy(narrow[t][:], q_tables[t][:])
-            first = 2 * SLOTS * (t // 2)
-            place = dealt(q_planes[:, first + t % 2 : first + 2 * SLOTS : 2])
-            nc.scalar.activation(place, narrow[t][:].indirect(offsets[:]), COPY)
-        x_along_features(1, "q_table3")
-
-        q_words = [tile("q_words0", PACK * HALF, BF16, tag="x_raw"), tile("q_words1", PACK * HALF, BF16, tag="q_narrow3")]
         for half in range(2):
+            dq = dq_copy(f"dq0_{half}", dq_product(0, f"d{half}", half), halves(half))
+            nc.vector.tensor_copy(listed(windows[0], half), dq[:])
+        nc.sync.dma_start(out_rows[0], windows[0][:])
+
+        v_dealt = tile("v_dealt", PACK * SLOTS, F32)
+        for a in range(PACK):
             nc.scalar.copy(
-                q_words[half][:].bitcast(U32).rearrange("p (s j) -> p s j", j=2),
-                q_planes[:].bitcast(U32).rearrange("p (j s) -> p s j", j=2)[:, half * HALF : (half + 1) * HALF],
+                v_dealt[:].rearrange("p (t b a k) -> p a t b k", t=PACK, b=PACK, a=PACK)[:, a],
+                v_banks[a][:].rearrange("p (t b k) -> p t b k", t=PACK, b=PACK),
             )
 
+        xd_words = tile("xd_words", PACK * K, BF16, tag="xr_words")
+        nc.gpsimd.tensor_copy(
+            xd_words[:].rearrange("p (t m j) -> p t m j", t=PACK, j=PACK),
+            x_raw[:].rearrange("p (j m t) -> p t m j", j=PACK, t=PACK),
+        )
+
+        whole = slice(0, SLOTS)
+        dq = dq_copy("dq1", dq_product(1, "a1"), whole)
+        nc.vector.tensor_copy(listed(windows[1]), dq[:])
+        nc.sync.dma_start(out_rows[1], windows[1][:])
+
+        acc2 = dq_product(2, "d0")
+        acc3 = dq_product(3, "a0")
+        dq = dq_copy("dq3_0", acc3, halves(0))
+        nc.vector.tensor_copy(listed(windows[3], 0), dq[:])
+
+        xd_codes = tile("xd_codes", K, U32)
+        xd_scales = tile("xd_scales", K, U8, tag="dq1")
+        quantize(xd_codes[:], xd_scales[:], xd_words[:], E4M3)
+
+        q_planes = tile("q_planes", PACK * SLOTS, BF16, tag="xr_codes0")
+        for t in range(PACK):
+            nc.scalar.activation(q_planes[:, halves(t, SLOTS)], listed(q_tables[t]), COPY)
+
+        dq = dq_copy("dq2", acc2, whole, tag="q_table3")
+        for half in range(2):
+            nc.scalar.activation(listed(windows[2], half), dq[:, halves(half)], COPY)
+        nc.sync.dma_start(out_rows[2], windows[2][:])
+        dq = dq_copy("dq3_1", acc3, halves(1), tag="q_table3")
+        nc.scalar.activation(listed(windows[3], 1), dq[:], COPY)
+        nc.sync.dma_start(out_rows[3], windows[3][:])
+
+        q_words = [tile(f"q_words{half}", PACK * HALF, BF16) for half in range(2)]
+        for half in range(2):
+            nc.vector.tensor_copy(
+                q_words[half][:].rearrange("p (b a k t) -> p b a k t", b=2, a=PACK, t=PACK),
+                q_planes[:].rearrange("p (t a b k) -> p b a k t", t=PACK, a=PACK, b=PACK)[:, 2 * half : 2 * half + 2],
+            )
         q_codes = tile("q_codes", SLOTS, U32)
         q_scales = tile("q_scales", SLOTS, U8)
         for half in range(2):
-            cols = slice(half * HALF, (half + 1) * HALF)
-            quantize(q_codes[:, cols], q_scales[:, cols], q_words[half][:], E4M3)
+            quantize(q_codes[:, halves(half)], q_scales[:, halves(half)], q_words[half][:], E4M3)
 
-        dq_out(3, dq_copy(3, last_acc, "q_planes"))
-
-        w_turned = tile("w_turned", PACK * K, F32, tag="x_raw")
-
-        def turn_w(b):
-            turned = bank(f"w_bank{b}", ("dq0", "turn1", "dq1", "turn0")[b])
-            for t in order:
-                nc.tensor.transpose(turned[:, t * P : (t + 1) * P], w_planes[t][:, b * P : (b + 1) * P], ident[:])
-            nc.scalar.copy(
-                w_turned[:, b * K : (b + 1) * K].rearrange("p (m t) -> p m t", t=PACK),
-                turned[:].rearrange("p (t m) -> p m t", t=PACK),
-            )
-
-        def u_product(b):
-            cols = slice(b * P, (b + 1) * P)
-            u = bank(f"u{b}", f"v{order[b]}")
-            matmul(u[:], q_codes[:, cols], q_scales[:, cols], E4M3, xd_codes[:], xd_scales[:], E4M3)
-            return u
-
-        sums = tile("sums", QUAD, F32)
-        nc.gpsimd.memset(sums[:], 0.0)
         step = QUAD // PACK
-        products = [tile(f"products{b}", K, F32) for b in range(PACK)]
-
-        turn_w(0)
-        u_copy = tile("u_copy", K, F32)
-        nc.scalar.copy(u_copy[:], u_product(0)[:])
-        nc.gpsimd.tensor_tensor(products[0][:], u_copy[:], w_turned[:, 0:K], MULT)
-        for b in range(1, PACK):
-            turn_w(b)
-        for b in range(1, PACK):
-            nc.vector.scalar_tensor_tensor(
-                products[b][:],
-                u_product(b)[:],
-                1.0,
-                w_turned[:, b * K : (b + 1) * K],
-                MULT,
-                MULT,
-                accum_out=sums[:, b * step : b * step + 1],
+        for half in range(2):
+            u_banks = [bank(f"u{half}_{pair}", f"v{2 * half + pair}") for pair in range(2)]
+            for t in range(PACK):
+                matmul(
+                    u_banks[t // 2][:, halves(t % 2)],
+                    xd_codes[:, halves(t, P)],
+                    xd_scales[:, halves(t, P)],
+                    E4M3,
+                    q_codes[:, halves(half)],
+                    q_scales[:, halves(half)],
+                    E4M3,
+                )
+            total = bank(f"total{half}", ("d1", "a1")[half])
+            for t in range(PACK):
+                h = tile(f"h{half}_{t}", HALF, F32)
+                first = t * SLOTS + half * HALF
+                nc.vector.scalar_tensor_tensor(
+                    h[:], u_banks[t // 2][:, halves(t % 2)], us_cols[:, t : t + 1], v_dealt[:, first : first + HALF], MULT, MULT
+                )
+                for b in range(2):
+                    nc.tensor.matmul(
+                        total[:, halves(b, P)],
+                        h[:, halves(b, P)],
+                        ident[:],
+                        start=(t == 0 and b == 0),
+                        stop=(t == PACK - 1 and b == 1),
+                        is_transpose=True,
+                    )
+            nc.vector.tensor_reduce(
+                sums[:, 2 * half * step : 2 * (half + 1) * step : step],
+                total[:, 0:HALF].rearrange("p (b m) -> p b m", b=2),
+                ALONG_FREE,
+                ADD,
             )
-        spent = tile("spent", K, BF16)
-        nc.scalar.activation(spent[:], products[0][:], COPY, accum_out=sums[:, 0:1])
         s_rows = tile("s_rows", QUAD, F32)
         nc.vector.transpose(s_rows[:], sums[:])
         nc.sync.dma_start(out_0.rearrange("o (n k) -> (o n) k", k=QUAD), s_rows[0:P:step, :])

@@ -6,6 +6,7 @@ from concourse.masks import make_identity
 F32 = mybir.dt.float32
 BF16 = mybir.dt.bfloat16
 U32 = mybir.dt.uint32
+I32 = mybir.dt.int32
 U16 = mybir.dt.uint16
 U8 = mybir.dt.uint8
 E4M3 = mybir.dt.float8_e4m3fn_x4
@@ -225,21 +226,25 @@ def tile_attend_gadal_kernel(tc, xT, qT, dyT, pT, lam, us, offs, out_0, out_1):
             matmul(acc[:, cols], xr[j][0], xr[j][1], E4M3, g_codes[:, cols], g_scales[:, cols], E5M2)
             return acc
 
-        def dq_copy(name, acc, cols, tag=None):
+        def dq_copy(copy, name, acc, cols, tag=None):
             dq = tile(name, cols.stop - cols.start, F32, tag=tag)
-            nc.scalar.copy(dq[:], acc[:, cols])
+            copy(dq[:], acc[:, cols])
             return dq
 
-        for half in range(2):
-            dq = dq_copy(f"dq0_{half}", dq_product(0, f"d{half}", half), halves(half))
-            nc.vector.tensor_copy(listed(windows[0], half), dq[:])
+        def scatter_on_scalar(j, dq, half):
+            nc.scalar.activation(listed(windows[j], half), dq, COPY)
+
+        for half, tag in ((0, "lam_table"), (1, None)):
+            dq = dq_copy(nc.scalar.copy, f"dq0_{half}", dq_product(0, f"d{half}", half), halves(half), tag=tag)
+            scatter_on_scalar(0, dq[:], half)
         nc.sync.dma_start(out_rows[0], windows[0][:])
 
-        v_dealt = tile("v_dealt", PACK * SLOTS, F32)
-        for a in range(PACK):
-            nc.scalar.copy(
-                v_dealt[:].rearrange("p (t b a k) -> p a t b k", t=PACK, b=PACK, a=PACK)[:, a],
-                v_banks[a][:].rearrange("p (t b k) -> p t b k", t=PACK, b=PACK),
+        v_dealt = [tile(f"v_dealt{half}", PACK * HALF, F32) for half in range(2)]
+        for n in range(PACK):
+            copy = nc.vector.tensor_copy if n == PACK - 1 else nc.scalar.copy
+            copy(
+                v_dealt[n // 2][:].rearrange("p (t b n a k) -> p n t a b k", t=PACK, b=2, n=2, a=2)[:, n % 2],
+                v_banks[n][:].rearrange("p (t a b k) -> p t a b k", t=PACK, a=2, b=2),
             )
 
         xd_words = tile("xd_words", PACK * K, BF16, tag="xr_words")
@@ -249,41 +254,44 @@ def tile_attend_gadal_kernel(tc, xT, qT, dyT, pT, lam, us, offs, out_0, out_1):
         )
 
         whole = slice(0, SLOTS)
-        dq = dq_copy("dq1", dq_product(1, "a1"), whole)
-        nc.vector.tensor_copy(listed(windows[1]), dq[:])
+        dq = dq_copy(nc.scalar.copy, "dq1", dq_product(1, "a1"), whole)
+        for half in range(2):
+            scatter_on_scalar(1, dq[:, halves(half)], half)
         nc.sync.dma_start(out_rows[1], windows[1][:])
 
-        acc2 = dq_product(2, "d0")
-        acc3 = dq_product(3, "a0")
-        dq = dq_copy("dq3_0", acc3, halves(0))
-        nc.vector.tensor_copy(listed(windows[3], 0), dq[:])
+        q_pairs = tile("q_pairs", PACK * SLOTS, BF16, tag="g_words1")
 
-        xd_codes = tile("xd_codes", K, U32)
-        xd_scales = tile("xd_scales", K, U8, tag="dq1")
-        quantize(xd_codes[:], xd_scales[:], xd_words[:], E4M3)
+        def gather_q(t):
+            first = 2 * SLOTS * (t // 2)
+            nc.vector.tensor_copy(q_pairs[:, first + t % 2 : first + 2 * SLOTS : 2], listed(q_tables[t]))
 
-        q_planes = tile("q_planes", PACK * SLOTS, BF16, tag="xr_codes0")
-        for t in range(PACK):
-            nc.scalar.activation(q_planes[:, halves(t, SLOTS)], listed(q_tables[t]), COPY)
-
-        dq = dq_copy("dq2", acc2, whole, tag="q_table3")
+        gather_q(0)
+        gather_q(1)
+        dq = dq_copy(nc.vector.tensor_copy, "dq2", dq_product(2, "a0"), whole)
         for half in range(2):
-            nc.scalar.activation(listed(windows[2], half), dq[:, halves(half)], COPY)
+            scatter_on_scalar(2, dq[:, halves(half)], half)
         nc.sync.dma_start(out_rows[2], windows[2][:])
-        dq = dq_copy("dq3_1", acc3, halves(1), tag="q_table3")
-        nc.scalar.activation(listed(windows[3], 1), dq[:], COPY)
-        nc.sync.dma_start(out_rows[3], windows[3][:])
+        gather_q(2)
+        gather_q(3)
 
         q_words = [tile(f"q_words{half}", PACK * HALF, BF16) for half in range(2)]
         for half in range(2):
             nc.vector.tensor_copy(
-                q_words[half][:].rearrange("p (b a k t) -> p b a k t", b=2, a=PACK, t=PACK),
-                q_planes[:].rearrange("p (t a b k) -> p b a k t", t=PACK, a=PACK, b=PACK)[:, 2 * half : 2 * half + 2],
+                q_words[half][:].bitcast(I32).rearrange("p (b a k j) -> p b a k j", b=2, a=PACK, j=2),
+                q_pairs[:].bitcast(I32).rearrange("p (j h a b k) -> p h b a k j", j=2, h=2, a=PACK, b=2)[:, half],
             )
         q_codes = tile("q_codes", SLOTS, U32)
         q_scales = tile("q_scales", SLOTS, U8)
         for half in range(2):
             quantize(q_codes[:, halves(half)], q_scales[:, halves(half)], q_words[half][:], E4M3)
+        xd_codes = tile("xd_codes", K, U32)
+        xd_scales = tile("xd_scales", K, U8, tag="g_words1")
+        quantize(xd_codes[:], xd_scales[:], xd_words[:], E4M3)
+
+        dq = dq_copy(nc.vector.tensor_copy, "dq3", dq_product(3, "d0"), whole, tag="q_words0")
+        nc.vector.tensor_copy(listed(windows[3], 0), dq[:, halves(0)])
+        scatter_on_scalar(3, dq[:, halves(1)], 1)
+        nc.sync.dma_start(out_rows[3], windows[3][:])
 
         step = QUAD // PACK
         for half in range(2):
@@ -301,9 +309,8 @@ def tile_attend_gadal_kernel(tc, xT, qT, dyT, pT, lam, us, offs, out_0, out_1):
             total = bank(f"total{half}", ("d1", "a1")[half])
             for t in range(PACK):
                 h = tile(f"h{half}_{t}", HALF, F32)
-                first = t * SLOTS + half * HALF
                 nc.vector.scalar_tensor_tensor(
-                    h[:], u_banks[t // 2][:, halves(t % 2)], us_cols[:, t : t + 1], v_dealt[:, first : first + HALF], MULT, MULT
+                    h[:], u_banks[t // 2][:, halves(t % 2)], us_cols[:, t : t + 1], v_dealt[half][:, halves(t)], MULT, MULT
                 )
                 for b in range(2):
                     nc.tensor.matmul(
@@ -315,11 +322,14 @@ def tile_attend_gadal_kernel(tc, xT, qT, dyT, pT, lam, us, offs, out_0, out_1):
                         is_transpose=True,
                     )
             nc.vector.tensor_reduce(
-                sums[:, 2 * half * step : 2 * (half + 1) * step : step],
+                sums[:, half * step : QUAD : 2 * step],
                 total[:, 0:HALF].rearrange("p (b m) -> p b m", b=2),
                 ALONG_FREE,
                 ADD,
             )
         s_rows = tile("s_rows", QUAD, F32)
         nc.vector.transpose(s_rows[:], sums[:])
-        nc.sync.dma_start(out_0.rearrange("o (n k) -> (o n) k", k=QUAD), s_rows[0:P:step, :])
+        for half in range(2):
+            nc.sync.dma_start(
+                out_0[:, halves(half)].rearrange("o (n k) -> (o n) k", k=QUAD), s_rows[half * step : P : 2 * step, :]
+            )

@@ -36,10 +36,14 @@ def tile_attend_gadal_kernel(tc, xT, qT, dyT, pT, lam, us, offs, out_0, out_1):
     nc = tc.nc
     with ExitStack() as ctx:
         sb = ctx.enter_context(tc.tile_pool(name="sb", bufs=1))
+        laid = ctx.enter_context(tc.tile_pool(name="laid", bufs=1))
         ps = ctx.enter_context(tc.psum_pool(name="ps", bufs=1))
 
         def tile(name, width, dtype, tag=None):
             return sb.tile([P, width], dtype, name=name, tag=tag or name, align_bytes=64)
+
+        def tile_at(name, width, dtype, offset):
+            return laid.tile([P, width], dtype, name=name, offset=offset, align_bytes=64)
 
         def bank(name, tag):
             return ps.tile([P, SLOTS], F32, name=name, tag=tag)
@@ -75,8 +79,8 @@ def tile_attend_gadal_kernel(tc, xT, qT, dyT, pT, lam, us, offs, out_0, out_1):
         nc.sync.dma_start(us_cols[:], us.rearrange("(p t) o -> p (t o)", t=PACK))
         for t in range(PACK):
             nc.sync.dma_start(p_tables[t][:], p_rows[t])
-        nc.sync.dma_start(x_raw[:, 0:K], x_rows[:, 0:K])
-        nc.sync.dma_start(x_raw[:, K:], x_rows[:, K:])
+        for pair in range(2):
+            nc.sync.dma_start(x_raw[:, halves(pair, 2 * K)], x_rows[:, halves(pair, 2 * K)])
         for t in range(PACK):
             nc.sync.dma_start(q_tables[t][:], q_rows[t])
 
@@ -89,9 +93,9 @@ def tile_attend_gadal_kernel(tc, xT, qT, dyT, pT, lam, us, offs, out_0, out_1):
         make_identity(nc, ident[:])
         sums = tile("sums", QUAD, F32)
         nc.gpsimd.memset(sums[:], 0.0)
-        windows = [tile(f"window{j}", PIECES, F32) for j in range(2)]
+        windows = [tile(f"window{j}", PIECES, F32) for j in range(PACK - 1)]
         for window in windows:
-            nc.vector.memset(window[:].bitcast(U32), 0)
+            nc.vector.memset(window[:], 0.0)
 
         lam_table = tile("lam_table", PIECES, F32)
         for group in range(PACK):
@@ -106,60 +110,52 @@ def tile_attend_gadal_kernel(tc, xT, qT, dyT, pT, lam, us, offs, out_0, out_1):
                 spread[:].rearrange("p (c n) -> p n c", c=PACK),
                 COPY,
             )
+        windows.append(tile("window3", PIECES, F32, tag="lam_cols"))
+        nc.gpsimd.memset(windows[-1][:], 0.0)
         lam_slots = tile("lam_slots", SLOTS, F32)
         nc.scalar.activation(lam_slots[:], listed(lam_table), COPY)
 
         dy_words = tile("dy_words", PACK * K, BF16)
-        nc.vector.tensor_copy(
-            dy_words[:].rearrange("p (t m j) -> p m j t", t=PACK, j=PACK),
-            dy_raw[:].rearrange("p (j m t) -> p m j t", j=PACK, t=PACK),
-        )
+        def deal(copy, words, raw, pair):
+            copy(
+                words.rearrange("p (t m j) -> p m j t", t=2, j=PACK),
+                raw[:].rearrange("p (j m t) -> p m j t", j=PACK, t=PACK)[:, :, :, 2 * pair : 2 * pair + 2],
+            )
+
+        for pair in range(2):
+            deal(nc.vector.tensor_copy, dy_words[:, halves(pair, 2 * K)], dy_raw, pair)
         dy_codes = tile("dy_codes", K, U32)
         dy_scales = tile("dy_scales", K, U8)
         quantize(dy_codes[:], dy_scales[:], dy_words[:], E5M2)
 
-        factors = tile("factors", PACK * SLOTS, F32)
-        nc.vector.tensor_tensor(
-            factors[:].rearrange("p (i t) -> p i t", t=PACK),
-            lam_slots[:].unsqueeze(2).to_broadcast([P, SLOTS, PACK]),
-            us_cols[:].unsqueeze(1).to_broadcast([P, SLOTS, PACK]),
-            MULT,
-        )
-
-        p_planes = tile("p_planes", 2 * SLOTS, BF16, tag="lam_table")
-        for t in range(2):
-            nc.scalar.activation(p_planes[:, halves(t, SLOTS)], listed(p_tables[t]), COPY)
-        p_tile = tile("p_words", PACK * SLOTS, BF16, tag="lam_slots")
-        p_words = [p_tile[:, halves(half, PACK * HALF)] for half in range(2)]
-        for half in range(2):
-            nc.scalar.copy(
-                p_words[half].rearrange("p (c t) -> p c t", t=PACK)[:, :, 0:2],
-                p_planes[:].rearrange("p (t c) -> p c t", t=2)[:, halves(half)],
+        factors = [tile(f"factors{a}", PACK * P, F32) for a in range(PACK)]
+        for a in range(PACK):
+            nc.gpsimd.tensor_tensor(
+                factors[a][:].rearrange("p (i t) -> p i t", t=PACK),
+                lam_slots[:, halves(a, P)].unsqueeze(2).to_broadcast([P, P, PACK]),
+                us_cols[:].unsqueeze(1).to_broadcast([P, P, PACK]),
+                MULT,
             )
-        for t in (2, 3):
+
+        p_words = [tile(f"p_words{half}", PACK * HALF, BF16)[:] for half in range(2)]
+        for t in range(2):
             for half in range(2):
                 nc.vector.tensor_copy(p_words[half][:, t : PACK * HALF : PACK], listed(p_tables[t], half))
-        for j, tag in ((2, "dy_words"), (3, "p_table0")):
-            windows.append(tile(f"window{j}", PIECES, F32, tag=tag))
-            nc.gpsimd.memset(windows[j][:], 0.0)
+        p_late = tile("p_late", 2 * HALF, BF16, tag="lam_table")
+        for t in (2, 3):
+            nc.vector.tensor_copy(p_words[0][:, t : PACK * HALF : PACK], listed(p_tables[t], 0))
+            nc.scalar.activation(p_late[:, halves(t - 2)], listed(p_tables[t], 1), COPY)
+        nc.scalar.copy(
+            p_words[1].rearrange("p (c t) -> p c t", t=PACK)[:, :, 2:PACK], p_late[:].rearrange("p (t c) -> p c t", t=2)
+        )
         p_codes = tile("p_codes", SLOTS, U32)
         p_scales = tile("p_scales", SLOTS, U8)
         for half in range(2):
             quantize(p_codes[:, halves(half)], p_scales[:, halves(half)], p_words[half], E4M3)
 
-        turned = bank("x_turned0", "a0")
-        for t in range(PACK):
-            nc.tensor.transpose(turned[:, halves(t, P)], x_raw[:, t:K:PACK], ident[:])
-        words = tile("xr_words0", K, BF16, tag="lam_table")
-        nc.scalar.copy(words[:].rearrange("p (c t) -> p c t", t=PACK), turned[:].rearrange("p (t c) -> p c t", t=PACK))
-        xr_first = tile("xr_codes0", P, U32)
-        scales = tile("xr_scales0", P, U8, tag="p_table3")
-        quantize(xr_first[:], scales[:], words[:], E4M3)
-        xr = [(xr_first[:], scales[:])]
-
-        x_narrow = tile("x_narrow", (PACK - 1) * K, BF16, tag="lam_table")
-        for j in range(PACK - 1):
-            nc.gpsimd.tensor_copy(x_narrow[:, halves(j, K)], x_raw[:, halves(j + 1, K)])
+        x_narrow = tile("x_narrow", PACK * K, BF16, tag="lam_slots")
+        for j in range(PACK):
+            nc.gpsimd.tensor_copy(x_narrow[:, halves(j, K)], x_raw[:, halves(j, K)])
 
         v_banks = []
         for a in range(PACK):
@@ -177,46 +173,49 @@ def tile_attend_gadal_kernel(tc, xT, qT, dyT, pT, lam, us, offs, out_0, out_1):
 
         g_words = [tile(f"g_words{half}", PACK * HALF, BF16) for half in range(2)]
         g_codes = tile("g_codes", SLOTS, U32)
-        g_scales = tile("g_scales", SLOTS, U8)
+        g_scales = tile("g_scales", SLOTS, U8, tag="factors1")
 
         def form_g(a):
             nc.vector.tensor_tensor(
                 g_words[a // 2][:, halves(a % 2, K)].rearrange("p (n t) -> p n t", t=PACK),
                 v_banks[a][:].rearrange("p (t n) -> p n t", t=PACK),
-                factors[:, halves(a, K)].rearrange("p (n t) -> p n t", t=PACK),
+                factors[a][:].rearrange("p (n t) -> p n t", t=PACK),
                 MULT,
             )
 
         def quantize_g(half):
             quantize(g_codes[:, halves(half)], g_scales[:, halves(half)], g_words[half][:], E5M2)
 
-        form_g(0)
-        form_g(1)
-        form_g(2)
-        quantize_g(0)
-        form_g(3)
-        quantize_g(1)
 
         x_pairs = x_narrow[:].bitcast(F32)
-        xr_words = tile("xr_words", (PACK - 1) * K, BF16)
-        for planes, tag in (((0, 1), "a1"), ((2,), "a0")):
-            turned = bank(f"x_turned{planes[0] + 1}", tag)
-            for n, j in enumerate(planes):
+        xr = []
+
+        def turn_x(pair, scales_tag):
+            turned = bank(f"x_turned{pair}", f"a{pair}")
+            for n in range(2):
+                j = 2 * pair + n
                 for u in range(2):
                     nc.tensor.transpose(
                         turned[:, halves(2 * n + u, P)], x_pairs[:, j * HALF + u : (j + 1) * HALF : 2], ident[:]
                     )
+            words = tile_at("xr_words1", 2 * K, BF16, 3072) if pair else tile("xr_words0", 2 * K, BF16)
             nc.scalar.copy(
-                xr_words[:].bitcast(F32)[:, planes[0] * HALF : (planes[-1] + 1) * HALF].rearrange(
-                    "p (j c u) -> p j c u", j=len(planes), u=2
-                ),
-                turned[:, 0 : len(planes) * HALF].rearrange("p (j u c) -> p j c u", j=len(planes), u=2),
+                words[:].bitcast(F32).rearrange("p (j c u) -> p j c u", j=2, u=2),
+                turned[:].rearrange("p (j u c) -> p j c u", j=2, u=2),
             )
-        xr_codes = tile("xr_codes", (PACK - 1) * P, U32)
-        xr_scales = tile("xr_scales", (PACK - 1) * P, U8)
-        quantize(xr_codes[:], xr_scales[:], xr_words[:], E4M3)
-        for j in range(PACK - 1):
-            xr.append((xr_codes[:, halves(j, P)], xr_scales[:, halves(j, P)]))
+            codes = tile(f"xr_codes{pair}", 2 * P, U32)
+            scales = tile(f"xr_scales{pair}", 2 * P, U8, tag=scales_tag)
+            quantize(codes[:], scales[:], words[:], E4M3)
+            for n in range(2):
+                xr.append((codes[:, halves(n, P)], scales[:, halves(n, P)]))
+
+        for a in range(PACK - 1):
+            form_g(a)
+        quantize_g(0)
+        turn_x(0, "factors2")
+        form_g(PACK - 1)
+        turn_x(1, "factors3")
+        quantize_g(1)
 
         out_rows = out_1.rearrange("(p j) n -> j p n", j=PACK)
 
@@ -247,27 +246,26 @@ def tile_attend_gadal_kernel(tc, xT, qT, dyT, pT, lam, us, offs, out_0, out_1):
                 v_banks[n][:].rearrange("p (t a b k) -> p t a b k", t=PACK, a=2, b=2),
             )
 
-        xd_words = tile("xd_words", PACK * K, BF16, tag="xr_words")
-        nc.gpsimd.tensor_copy(
-            xd_words[:].rearrange("p (t m j) -> p t m j", t=PACK, j=PACK),
-            x_raw[:].rearrange("p (j m t) -> p t m j", j=PACK, t=PACK),
-        )
-
         whole = slice(0, SLOTS)
-        dq = dq_copy(nc.scalar.copy, "dq1", dq_product(1, "a1"), whole)
+        dq = dq_copy(nc.scalar.copy, "dq1", dq_product(1, "a0"), whole)
         for half in range(2):
             scatter_on_scalar(1, dq[:, halves(half)], half)
         nc.sync.dma_start(out_rows[1], windows[1][:])
 
-        q_pairs = tile("q_pairs", PACK * SLOTS, BF16, tag="g_words1")
+        q_pairs = tile_at("q_pairs", PACK * SLOTS, BF16, 4096)
 
         def gather_q(t):
             first = 2 * SLOTS * (t // 2)
             nc.vector.tensor_copy(q_pairs[:, first + t % 2 : first + 2 * SLOTS : 2], listed(q_tables[t]))
 
         gather_q(0)
+        xd_words = tile_at("xd_words", PACK * K, BF16, 0)
+        nc.gpsimd.tensor_copy(
+            xd_words[:].rearrange("p (t m j) -> p t m j", t=PACK, j=PACK),
+            x_raw[:].rearrange("p (j m t) -> p t m j", j=PACK, t=PACK),
+        )
         gather_q(1)
-        dq = dq_copy(nc.vector.tensor_copy, "dq2", dq_product(2, "a0"), whole)
+        dq = dq_copy(nc.vector.tensor_copy, "dq2", dq_product(2, "a1"), whole)
         for half in range(2):
             scatter_on_scalar(2, dq[:, halves(half)], half)
         nc.sync.dma_start(out_rows[2], windows[2][:])
@@ -285,7 +283,7 @@ def tile_attend_gadal_kernel(tc, xT, qT, dyT, pT, lam, us, offs, out_0, out_1):
         for half in range(2):
             quantize(q_codes[:, halves(half)], q_scales[:, halves(half)], q_words[half][:], E4M3)
         xd_codes = tile("xd_codes", K, U32)
-        xd_scales = tile("xd_scales", K, U8, tag="g_words1")
+        xd_scales = tile_at("xd_scales", K, U8, 4096)
         quantize(xd_codes[:], xd_scales[:], xd_words[:], E4M3)
 
         dq = dq_copy(nc.vector.tensor_copy, "dq3", dq_product(3, "d0"), whole, tag="q_words0")
@@ -306,7 +304,7 @@ def tile_attend_gadal_kernel(tc, xT, qT, dyT, pT, lam, us, offs, out_0, out_1):
                     q_scales[:, halves(half)],
                     E4M3,
                 )
-            total = bank(f"total{half}", ("d1", "a1")[half])
+            total = bank(f"total{half}", ("d1", "a0")[half])
             for t in range(PACK):
                 h = tile(f"h{half}_{t}", HALF, F32)
                 nc.vector.scalar_tensor_tensor(

@@ -233,30 +233,30 @@ def tile_attend_gadal_kernel(tc, xT, qT, dyT, pT, lam, us, offs, out_0, out_1):
         def scatter_on_scalar(j, dq, half):
             nc.scalar.activation(listed(windows[j], half), dq, COPY)
 
-        for half, tag in ((0, "lam_table"), (1, None)):
-            dq = dq_copy(nc.scalar.copy, f"dq0_{half}", dq_product(0, f"d{half}", half), halves(half), tag=tag)
-            scatter_on_scalar(0, dq[:], half)
-        nc.sync.dma_start(out_rows[0], windows[0][:])
-
-        v_dealt = [tile(f"v_dealt{half}", PACK * HALF, F32) for half in range(2)]
-        for n in range(PACK):
-            copy = nc.vector.tensor_copy if n == PACK - 1 else nc.scalar.copy
-            copy(
-                v_dealt[n // 2][:].rearrange("p (t b n a k) -> p n t a b k", t=PACK, b=2, n=2, a=2)[:, n % 2],
-                v_banks[n][:].rearrange("p (t a b k) -> p t a b k", t=PACK, a=2, b=2),
+        v_dealt = tile("v_dealt", PACK * SLOTS, F32)
+        for a in range(PACK):
+            nc.scalar.copy(
+                v_dealt[:].rearrange("p (t b a k) -> p a t b k", t=PACK, b=PACK, a=PACK)[:, a],
+                v_banks[a][:].rearrange("p (t b k) -> p t b k", t=PACK, b=PACK),
             )
 
         whole = slice(0, SLOTS)
-        dq = dq_copy(nc.scalar.copy, "dq1", dq_product(1, "a0"), whole)
-        for half in range(2):
-            scatter_on_scalar(1, dq[:, halves(half)], half)
+        first_dq = dq_copy(nc.scalar.copy, "dq0_0", dq_product(0, "d0", 0), halves(0))
+        scatter_on_scalar(0, first_dq[:], 0)
+        first_dq = dq_copy(nc.scalar.copy, "dq0_1", dq_product(0, "d1", 1), halves(1))
+        second_dq = dq_copy(nc.scalar.copy, "dq1", dq_product(1, "a0"), whole)
+        scatter_on_scalar(0, first_dq[:], 1)
+        nc.sync.dma_start(out_rows[0], windows[0][:])
+        scatter_on_scalar(1, second_dq[:, halves(0)], 0)
+        third_dq = dq_copy(nc.scalar.copy, "dq2", dq_product(2, "a1"), whole, tag="dq0_1")
+        scatter_on_scalar(1, second_dq[:, halves(1)], 1)
         nc.sync.dma_start(out_rows[1], windows[1][:])
 
-        q_pairs = tile_at("q_pairs", PACK * SLOTS, BF16, 4096)
+        q_planes = tile_at("q_planes", PACK * SLOTS, BF16, 4096)
 
-        def gather_q(t):
-            first = 2 * SLOTS * (t // 2)
-            nc.vector.tensor_copy(q_pairs[:, first + t % 2 : first + 2 * SLOTS : 2], listed(q_tables[t]))
+        def gather_q(t, half=None):
+            place = q_planes[:, halves(t, SLOTS)]
+            nc.vector.tensor_copy(place if half is None else place[:, halves(half)], listed(q_tables[t], half))
 
         gather_q(0)
         xd_words = tile_at("xd_words", PACK * K, BF16, 0)
@@ -265,31 +265,31 @@ def tile_attend_gadal_kernel(tc, xT, qT, dyT, pT, lam, us, offs, out_0, out_1):
             x_raw[:].rearrange("p (j m t) -> p t m j", j=PACK, t=PACK),
         )
         gather_q(1)
-        dq = dq_copy(nc.vector.tensor_copy, "dq2", dq_product(2, "a1"), whole)
-        for half in range(2):
-            scatter_on_scalar(2, dq[:, halves(half)], half)
-        nc.sync.dma_start(out_rows[2], windows[2][:])
+        last_acc = dq_product(3, "d0")
+        dq = dq_copy(nc.vector.tensor_copy, "dq3_0", last_acc, halves(0))
         gather_q(2)
+        nc.vector.tensor_copy(listed(windows[3], 0), dq[:])
+        scatter_on_scalar(2, third_dq[:, halves(0)], 0)
+        dq = dq_copy(nc.scalar.copy, "dq3_1", last_acc, halves(1), tag="dq1")
+        scatter_on_scalar(2, third_dq[:, halves(1)], 1)
+        nc.sync.dma_start(out_rows[2], windows[2][:])
+        scatter_on_scalar(3, dq[:], 1)
+        nc.sync.dma_start(out_rows[3], windows[3][:])
         gather_q(3)
 
+        xd_codes = tile("xd_codes", K, U32)
+        xd_scales = tile("xd_scales", K, U8, tag="q_table3")
+        quantize(xd_codes[:], xd_scales[:], xd_words[:], E4M3)
         q_words = [tile(f"q_words{half}", PACK * HALF, BF16) for half in range(2)]
         for half in range(2):
             nc.vector.tensor_copy(
-                q_words[half][:].bitcast(I32).rearrange("p (b a k j) -> p b a k j", b=2, a=PACK, j=2),
-                q_pairs[:].bitcast(I32).rearrange("p (j h a b k) -> p h b a k j", j=2, h=2, a=PACK, b=2)[:, half],
+                q_words[half][:].rearrange("p (b a k t) -> p b a k t", b=2, a=PACK, t=PACK),
+                q_planes[:].rearrange("p (t a b k) -> p b a k t", t=PACK, a=PACK, b=PACK)[:, 2 * half : 2 * half + 2],
             )
         q_codes = tile("q_codes", SLOTS, U32)
         q_scales = tile("q_scales", SLOTS, U8)
         for half in range(2):
             quantize(q_codes[:, halves(half)], q_scales[:, halves(half)], q_words[half][:], E4M3)
-        xd_codes = tile("xd_codes", K, U32)
-        xd_scales = tile_at("xd_scales", K, U8, 4096)
-        quantize(xd_codes[:], xd_scales[:], xd_words[:], E4M3)
-
-        dq = dq_copy(nc.vector.tensor_copy, "dq3", dq_product(3, "d0"), whole, tag="q_words0")
-        nc.vector.tensor_copy(listed(windows[3], 0), dq[:, halves(0)])
-        scatter_on_scalar(3, dq[:, halves(1)], 1)
-        nc.sync.dma_start(out_rows[3], windows[3][:])
 
         step = QUAD // PACK
         for half in range(2):
@@ -308,7 +308,7 @@ def tile_attend_gadal_kernel(tc, xT, qT, dyT, pT, lam, us, offs, out_0, out_1):
             for t in range(PACK):
                 h = tile(f"h{half}_{t}", HALF, F32)
                 nc.vector.scalar_tensor_tensor(
-                    h[:], u_banks[t // 2][:, halves(t % 2)], us_cols[:, t : t + 1], v_dealt[half][:, halves(t)], MULT, MULT
+                    h[:], u_banks[t // 2][:, halves(t % 2)], us_cols[:, t : t + 1], v_dealt[:, halves(2 * t + half)], MULT, MULT
                 )
                 for b in range(2):
                     nc.tensor.matmul(
@@ -320,14 +320,11 @@ def tile_attend_gadal_kernel(tc, xT, qT, dyT, pT, lam, us, offs, out_0, out_1):
                         is_transpose=True,
                     )
             nc.vector.tensor_reduce(
-                sums[:, half * step : QUAD : 2 * step],
+                sums[:, 2 * half * step : 2 * (half + 1) * step : step],
                 total[:, 0:HALF].rearrange("p (b m) -> p b m", b=2),
                 ALONG_FREE,
                 ADD,
             )
         s_rows = tile("s_rows", QUAD, F32)
         nc.vector.transpose(s_rows[:], sums[:])
-        for half in range(2):
-            nc.sync.dma_start(
-                out_0[:, halves(half)].rearrange("o (n k) -> (o n) k", k=QUAD), s_rows[half * step : P : 2 * step, :]
-            )
+        nc.sync.dma_start(out_0.rearrange("o (n k) -> (o n) k", k=QUAD), s_rows[0:P:step, :])

@@ -32,6 +32,10 @@ def halves(half, width=HALF):
     return slice(half * width, (half + 1) * width)
 
 
+def by_slot(ap, inner):
+    return ap.rearrange("p (b a k t) -> p a b k t", b=2, a=PACK, t=inner)
+
+
 def tile_attend_gadal_kernel(tc, xT, qT, dyT, pT, lam, us, offs, out_0, out_1):
     nc = tc.nc
     with ExitStack() as ctx:
@@ -66,7 +70,7 @@ def tile_attend_gadal_kernel(tc, xT, qT, dyT, pT, lam, us, offs, out_0, out_1):
         q_rows = qT.rearrange("(p t) n -> t p n", t=PACK)
         x_rows = xT.rearrange("(p t) r -> p (t r)", t=PACK)
         p_tables = [tile(f"p_table{t}", PIECES, F32) for t in range(PACK)]
-        q_tables = [tile(f"q_table{t}", PIECES, F32) for t in range(PACK)]
+        q_tables = [tile_at("q_table0", PIECES, F32, 8192)] + [tile(f"q_table{t}", PIECES, F32) for t in range(1, PACK)]
         dy_raw = tile("dy_raw", PACK * K, F32)
         x_raw = tile("x_raw", PACK * K, F32)
         offsets = tile("offsets", SLOTS // 16, U16)
@@ -115,6 +119,12 @@ def tile_attend_gadal_kernel(tc, xT, qT, dyT, pT, lam, us, offs, out_0, out_1):
         lam_slots = tile("lam_slots", SLOTS, F32)
         nc.scalar.activation(lam_slots[:], listed(lam_table), COPY)
 
+        spread = bank("us_spread", "a0")
+        for t in range(PACK):
+            nc.tensor.transpose(spread[:, halves(t, P)], us_cols[:, t : t + 1].to_broadcast([P, P]), ident[:])
+        us_rows = tile("us_rows", K, F32)
+        nc.scalar.copy(us_rows[:], spread[:])
+
         dy_words = tile("dy_words", PACK * K, BF16)
         def deal(copy, words, raw, pair):
             copy(
@@ -131,22 +141,26 @@ def tile_attend_gadal_kernel(tc, xT, qT, dyT, pT, lam, us, offs, out_0, out_1):
         factors = [tile(f"factors{a}", PACK * P, F32) for a in range(PACK)]
         for a in range(PACK):
             nc.gpsimd.tensor_tensor(
-                factors[a][:].rearrange("p (i t) -> p i t", t=PACK),
-                lam_slots[:, halves(a, P)].unsqueeze(2).to_broadcast([P, P, PACK]),
-                us_cols[:].unsqueeze(1).to_broadcast([P, P, PACK]),
+                factors[a][:].rearrange("p (a k t) -> p a k t", a=PACK, t=PACK),
+                lam_slots[:, halves(a // 2)]
+                .rearrange("p (a b k) -> p b a k", a=PACK, b=2)[:, a % 2]
+                .unsqueeze(3)
+                .to_broadcast([P, PACK, QUAD, PACK]),
+                us_cols[:].unsqueeze(1).unsqueeze(1).to_broadcast([P, PACK, QUAD, PACK]),
                 MULT,
             )
 
         p_words = [tile(f"p_words{half}", PACK * HALF, BF16)[:] for half in range(2)]
         for t in range(2):
             for half in range(2):
-                nc.vector.tensor_copy(p_words[half][:, t : PACK * HALF : PACK], listed(p_tables[t], half))
+                nc.vector.tensor_copy(by_slot(p_words[half], PACK)[:, :, :, :, t], listed(p_tables[t], half))
         p_late = tile("p_late", 2 * HALF, BF16, tag="lam_table")
         for t in (2, 3):
-            nc.vector.tensor_copy(p_words[0][:, t : PACK * HALF : PACK], listed(p_tables[t], 0))
+            nc.vector.tensor_copy(by_slot(p_words[0], PACK)[:, :, :, :, t], listed(p_tables[t], 0))
             nc.scalar.activation(p_late[:, halves(t - 2)], listed(p_tables[t], 1), COPY)
         nc.scalar.copy(
-            p_words[1].rearrange("p (c t) -> p c t", t=PACK)[:, :, 2:PACK], p_late[:].rearrange("p (t c) -> p c t", t=2)
+            by_slot(p_words[1], PACK)[:, :, :, :, 2:PACK],
+            p_late[:].rearrange("p (t a b k) -> p a b k t", t=2, a=PACK, b=2),
         )
         p_codes = tile("p_codes", SLOTS, U32)
         p_scales = tile("p_scales", SLOTS, U8)
@@ -203,7 +217,7 @@ def tile_attend_gadal_kernel(tc, xT, qT, dyT, pT, lam, us, offs, out_0, out_1):
                 words[:].bitcast(F32).rearrange("p (j c u) -> p j c u", j=2, u=2),
                 turned[:].rearrange("p (j u c) -> p j c u", j=2, u=2),
             )
-            codes = tile(f"xr_codes{pair}", 2 * P, U32)
+            codes = tile("xr_codes1", 2 * P, U32) if pair else tile_at("xr_codes0", 2 * P, U32, 5120)
             scales = tile(f"xr_scales{pair}", 2 * P, U8, tag=scales_tag)
             quantize(codes[:], scales[:], words[:], E4M3)
             for n in range(2):
@@ -225,56 +239,65 @@ def tile_attend_gadal_kernel(tc, xT, qT, dyT, pT, lam, us, offs, out_0, out_1):
             matmul(acc[:, cols], xr[j][0], xr[j][1], E4M3, g_codes[:, cols], g_scales[:, cols], E5M2)
             return acc
 
-        def dq_copy(copy, name, acc, cols, tag=None):
-            dq = tile(name, cols.stop - cols.start, F32, tag=tag)
-            copy(dq[:], acc[:, cols])
+        def dq_copy(copy, name, acc, cols, offset=None):
+            width = cols.stop - cols.start
+            dq = tile(name, width, F32) if offset is None else tile_at(name, width, F32, offset)
+            copy(
+                dq[:].rearrange("p (h a b k) -> p h a b k", a=PACK, b=2, k=QUAD),
+                acc[:, cols].rearrange("p (h b a k) -> p h a b k", a=PACK, b=2, k=QUAD),
+            )
             return dq
 
         def scatter_on_scalar(j, dq, half):
             nc.scalar.activation(listed(windows[j], half), dq, COPY)
 
-        v_dealt = tile("v_dealt", PACK * SLOTS, F32)
-        for a in range(PACK):
+        v_planes = tile("v_planes", PACK * HALF, F32)
+        for b in range(2):
             nc.scalar.copy(
-                v_dealt[:].rearrange("p (t b a k) -> p a t b k", t=PACK, b=PACK, a=PACK)[:, a],
-                v_banks[a][:].rearrange("p (t b k) -> p t b k", t=PACK, b=PACK),
+                v_planes[:].rearrange("p (t b n) -> p b t n", t=PACK, b=2)[:, b],
+                v_banks[b][:].rearrange("p (t n) -> p t n", t=PACK),
             )
 
-        whole = slice(0, SLOTS)
-        first_dq = dq_copy(nc.scalar.copy, "dq0_0", dq_product(0, "d0", 0), halves(0))
-        scatter_on_scalar(0, first_dq[:], 0)
-        first_dq = dq_copy(nc.scalar.copy, "dq0_1", dq_product(0, "d1", 1), halves(1))
-        second_dq = dq_copy(nc.scalar.copy, "dq1", dq_product(1, "a0"), whole)
-        scatter_on_scalar(0, first_dq[:], 1)
-        nc.sync.dma_start(out_rows[0], windows[0][:])
-        scatter_on_scalar(1, second_dq[:, halves(0)], 0)
-        third_dq = dq_copy(nc.scalar.copy, "dq2", dq_product(2, "a1"), whole, tag="dq0_1")
-        scatter_on_scalar(1, second_dq[:, halves(1)], 1)
-        nc.sync.dma_start(out_rows[1], windows[1][:])
-
-        q_planes = tile_at("q_planes", PACK * SLOTS, BF16, 4096)
-
-        def gather_q(t, half=None):
-            place = q_planes[:, halves(t, SLOTS)]
-            nc.vector.tensor_copy(place if half is None else place[:, halves(half)], listed(q_tables[t], half))
-
-        gather_q(0)
         xd_words = tile_at("xd_words", PACK * K, BF16, 0)
         nc.gpsimd.tensor_copy(
             xd_words[:].rearrange("p (t m j) -> p t m j", t=PACK, j=PACK),
             x_raw[:].rearrange("p (j m t) -> p t m j", j=PACK, t=PACK),
         )
+
+        q_planes = tile_at("q_planes", PACK * SLOTS, BF16, 4096)
+
+        def gather_q(t):
+            nc.vector.tensor_copy(q_planes[:, halves(t, SLOTS)], listed(q_tables[t]))
+
+        whole = slice(0, SLOTS)
+        first_dq = dq_copy(nc.scalar.copy, "dq0_0", dq_product(0, "d0", 0), halves(0))
+        scatter_on_scalar(0, first_dq[:], 0)
+        second_dq = dq_copy(nc.vector.tensor_copy, "dq1", dq_product(1, "a0"), whole, offset=16384)
+        first_dq = dq_copy(nc.vector.tensor_copy, "dq0_1", dq_product(0, "d1", 1), halves(1))
+        third_dq = dq_copy(nc.vector.tensor_copy, "dq2", dq_product(2, "a1"), whole)
+        gather_q(0)
+        nc.vector.tensor_copy(listed(windows[0], 1), first_dq[:])
+        nc.sync.dma_start(out_rows[0], windows[0][:])
         gather_q(1)
-        last_acc = dq_product(3, "d0")
-        dq = dq_copy(nc.vector.tensor_copy, "dq3_0", last_acc, halves(0))
-        gather_q(2)
-        nc.vector.tensor_copy(listed(windows[3], 0), dq[:])
+        for half in range(2):
+            scatter_on_scalar(1, second_dq[:, halves(half)], half)
+        nc.sync.dma_start(out_rows[1], windows[1][:])
         scatter_on_scalar(2, third_dq[:, halves(0)], 0)
-        dq = dq_copy(nc.scalar.copy, "dq3_1", last_acc, halves(1), tag="dq1")
+        last_dq = dq_copy(nc.scalar.copy, "dq3", dq_product(3, "v2"), whole, offset=16384)
         scatter_on_scalar(2, third_dq[:, halves(1)], 1)
         nc.sync.dma_start(out_rows[2], windows[2][:])
-        scatter_on_scalar(3, dq[:], 1)
+        for half in range(2):
+            scatter_on_scalar(3, last_dq[:, halves(half)], half)
         nc.sync.dma_start(out_rows[3], windows[3][:])
+
+        w_turned = []
+        for b in range(2):
+            v_turned = bank(f"v_turned{b}", f"d{b}")
+            cols = halves(2 + b, P)
+            matmul(v_turned[:], p_codes[:, cols], p_scales[:, cols], E4M3, dy_codes[:], dy_scales[:], E5M2)
+            w_turned.append(tile(f"w_turned{b}", K, F32, tag=("g_words1", "q_table1")[b]))
+            nc.vector.tensor_tensor(w_turned[b][:], v_turned[:], us_rows[:], MULT)
+        gather_q(2)
         gather_q(3)
 
         xd_codes = tile("xd_codes", K, U32)
@@ -284,7 +307,7 @@ def tile_attend_gadal_kernel(tc, xT, qT, dyT, pT, lam, us, offs, out_0, out_1):
         for half in range(2):
             nc.vector.tensor_copy(
                 q_words[half][:].rearrange("p (b a k t) -> p b a k t", b=2, a=PACK, t=PACK),
-                q_planes[:].rearrange("p (t a b k) -> p b a k t", t=PACK, a=PACK, b=PACK)[:, 2 * half : 2 * half + 2],
+                q_planes[:].rearrange("p (t h a b k) -> p h b a k t", t=PACK, h=2, a=PACK, b=2)[:, half],
             )
         q_codes = tile("q_codes", SLOTS, U32)
         q_scales = tile("q_scales", SLOTS, U8)
@@ -292,39 +315,49 @@ def tile_attend_gadal_kernel(tc, xT, qT, dyT, pT, lam, us, offs, out_0, out_1):
             quantize(q_codes[:, halves(half)], q_scales[:, halves(half)], q_words[half][:], E4M3)
 
         step = QUAD // PACK
-        for half in range(2):
-            u_banks = [bank(f"u{half}_{pair}", f"v{2 * half + pair}") for pair in range(2)]
-            for t in range(PACK):
-                matmul(
-                    u_banks[t // 2][:, halves(t % 2)],
-                    xd_codes[:, halves(t, P)],
-                    xd_scales[:, halves(t, P)],
-                    E4M3,
-                    q_codes[:, halves(half)],
-                    q_scales[:, halves(half)],
-                    E4M3,
-                )
-            total = bank(f"total{half}", ("d1", "a0")[half])
-            for t in range(PACK):
-                h = tile(f"h{half}_{t}", HALF, F32)
-                nc.vector.scalar_tensor_tensor(
-                    h[:], u_banks[t // 2][:, halves(t % 2)], us_cols[:, t : t + 1], v_dealt[:, halves(2 * t + half)], MULT, MULT
-                )
-                for b in range(2):
-                    nc.tensor.matmul(
-                        total[:, halves(b, P)],
-                        h[:, halves(b, P)],
-                        ident[:],
-                        start=(t == 0 and b == 0),
-                        stop=(t == PACK - 1 and b == 1),
-                        is_transpose=True,
-                    )
-            nc.vector.tensor_reduce(
-                sums[:, 2 * half * step : 2 * (half + 1) * step : step],
-                total[:, 0:HALF].rearrange("p (b m) -> p b m", b=2),
-                ALONG_FREE,
-                ADD,
+        u_banks = [bank(f"u{pair}", f"v{pair}") for pair in range(2)]
+        for t in range(PACK):
+            matmul(
+                u_banks[t // 2][:, halves(t % 2)],
+                xd_codes[:, halves(t, P)],
+                xd_scales[:, halves(t, P)],
+                E4M3,
+                q_codes[:, halves(0)],
+                q_scales[:, halves(0)],
+                E4M3,
             )
+        u_turned = []
+        for b, tag in ((0, "a0"), (1, "v3")):
+            u_turned.append(bank(f"u_turned{b}", tag))
+            cols = halves(2 + b, P)
+            matmul(u_turned[b][:], q_codes[:, cols], q_scales[:, cols], E4M3, xd_codes[:], xd_scales[:], E4M3)
+        total = bank("total", "a1")
+        for t in range(PACK):
+            h = tile(f"h{t}", HALF, F32)
+            nc.vector.scalar_tensor_tensor(
+                h[:], u_banks[t // 2][:, halves(t % 2)], us_cols[:, t : t + 1], v_planes[:, halves(t)], MULT, MULT
+            )
+            for b in range(2):
+                nc.tensor.matmul(
+                    total[:, halves(b, P)],
+                    h[:, halves(b, P)],
+                    ident[:],
+                    start=(t == 0 and b == 0),
+                    stop=(t == PACK - 1 and b == 1),
+                    is_transpose=True,
+                )
+        for b in range(2):
+            h = tile(f"h_turned{b}", K, F32)
+            col = (2 * b + 1) * step
+            nc.vector.scalar_tensor_tensor(
+                h[:], u_turned[b][:], 1.0, w_turned[b][:], MULT, MULT, accum_out=sums[:, col : col + 1]
+            )
+        nc.vector.tensor_reduce(
+            sums[:, 0 : QUAD : 2 * step], total[:, 0:HALF].rearrange("p (b m) -> p b m", b=2), ALONG_FREE, ADD
+        )
         s_rows = tile("s_rows", QUAD, F32)
         nc.vector.transpose(s_rows[:], sums[:])
-        nc.sync.dma_start(out_0.rearrange("o (n k) -> (o n) k", k=QUAD), s_rows[0:P:step, :])
+        for half in range(2):
+            nc.sync.dma_start(
+                out_0[:, halves(half)].rearrange("o (n k) -> (o n) k", k=QUAD), s_rows[half * step : P : 2 * step, :]
+            )

@@ -12,9 +12,7 @@ U8 = mybir.dt.uint8
 E4M3 = mybir.dt.float8_e4m3fn_x4
 E5M2 = mybir.dt.float8_e5m2_x4
 MULT = mybir.AluOpType.mult
-ADD = mybir.AluOpType.add
 COPY = mybir.ActivationFunctionType.Copy
-ALONG_FREE = mybir.AxisListType.X
 
 P = 128
 PACK = 4
@@ -272,9 +270,10 @@ def tile_attend_gadal_kernel(tc, xT, qT, dyT, pT, lam, us, offs, out_0, out_1):
         whole = slice(0, SLOTS)
         first_dq = dq_copy(nc.scalar.copy, "dq0_0", dq_product(0, "d0", 0), halves(0))
         scatter_on_scalar(0, first_dq[:], 0)
-        second_dq = dq_copy(nc.vector.tensor_copy, "dq1", dq_product(1, "a0"), whole, offset=16384)
-        first_dq = dq_copy(nc.vector.tensor_copy, "dq0_1", dq_product(0, "d1", 1), halves(1))
+        second_dq = dq_copy(nc.vector.tensor_copy, "dq1", dq_product(1, "a0"), whole)
+        first_dq = dq_copy(nc.scalar.copy, "dq0_1", dq_product(0, "d1", 1), halves(1))
         third_dq = dq_copy(nc.vector.tensor_copy, "dq2", dq_product(2, "a1"), whole)
+        last_dq = dq_copy(nc.vector.tensor_copy, "dq3", dq_product(3, "v2"), whole)
         gather_q(0)
         nc.vector.tensor_copy(listed(windows[0], 1), first_dq[:])
         nc.sync.dma_start(out_rows[0], windows[0][:])
@@ -283,7 +282,6 @@ def tile_attend_gadal_kernel(tc, xT, qT, dyT, pT, lam, us, offs, out_0, out_1):
             scatter_on_scalar(1, second_dq[:, halves(half)], half)
         nc.sync.dma_start(out_rows[1], windows[1][:])
         scatter_on_scalar(2, third_dq[:, halves(0)], 0)
-        last_dq = dq_copy(nc.scalar.copy, "dq3", dq_product(3, "v2"), whole, offset=16384)
         scatter_on_scalar(2, third_dq[:, halves(1)], 1)
         nc.sync.dma_start(out_rows[2], windows[2][:])
         for half in range(2):
@@ -291,12 +289,15 @@ def tile_attend_gadal_kernel(tc, xT, qT, dyT, pT, lam, us, offs, out_0, out_1):
         nc.sync.dma_start(out_rows[3], windows[3][:])
 
         w_turned = []
-        for b in range(2):
+
+        def make_w(b, tag):
             v_turned = bank(f"v_turned{b}", f"d{b}")
             cols = halves(2 + b, P)
             matmul(v_turned[:], p_codes[:, cols], p_scales[:, cols], E4M3, dy_codes[:], dy_scales[:], E5M2)
-            w_turned.append(tile(f"w_turned{b}", K, F32, tag=("g_words1", "q_table1")[b]))
+            w_turned.append(tile(f"w_turned{b}", K, F32, tag=tag))
             nc.vector.tensor_tensor(w_turned[b][:], v_turned[:], us_rows[:], MULT)
+
+        make_w(0, "g_words1")
         gather_q(2)
         gather_q(3)
 
@@ -313,6 +314,8 @@ def tile_attend_gadal_kernel(tc, xT, qT, dyT, pT, lam, us, offs, out_0, out_1):
         q_scales = tile("q_scales", SLOTS, U8)
         for half in range(2):
             quantize(q_codes[:, halves(half)], q_scales[:, halves(half)], q_words[half][:], E4M3)
+
+        make_w(1, "q_words0")
 
         step = QUAD // PACK
         u_banks = [bank(f"u{pair}", f"v{pair}") for pair in range(2)]
@@ -352,9 +355,10 @@ def tile_attend_gadal_kernel(tc, xT, qT, dyT, pT, lam, us, offs, out_0, out_1):
             nc.vector.scalar_tensor_tensor(
                 h[:], u_turned[b][:], 1.0, w_turned[b][:], MULT, MULT, accum_out=sums[:, col : col + 1]
             )
-        nc.vector.tensor_reduce(
-            sums[:, 0 : QUAD : 2 * step], total[:, 0:HALF].rearrange("p (b m) -> p b m", b=2), ALONG_FREE, ADD
-        )
+        spent = tile("spent", HALF, BF16)
+        for b in range(2):
+            col = 2 * b * step
+            nc.scalar.activation(spent[:, halves(b, P)], total[:, halves(b, P)], COPY, accum_out=sums[:, col : col + 1])
         s_rows = tile("s_rows", QUAD, F32)
         nc.vector.transpose(s_rows[:], sums[:])
         for half in range(2):

@@ -237,9 +237,9 @@ def tile_attend_gadal_kernel(tc, xT, qT, dyT, pT, lam, us, offs, out_0, out_1):
             matmul(acc[:, cols], xr[j][0], xr[j][1], E4M3, g_codes[:, cols], g_scales[:, cols], E5M2)
             return acc
 
-        def dq_copy(copy, name, acc, cols, offset=None):
+        def dq_copy(copy, name, acc, cols, offset=None, tag=None):
             width = cols.stop - cols.start
-            dq = tile(name, width, F32) if offset is None else tile_at(name, width, F32, offset)
+            dq = tile(name, width, F32, tag=tag) if offset is None else tile_at(name, width, F32, offset)
             copy(
                 dq[:].rearrange("p (h a b k) -> p h a b k", a=PACK, b=2, k=QUAD),
                 acc[:, cols].rearrange("p (h b a k) -> p h a b k", a=PACK, b=2, k=QUAD),
@@ -270,23 +270,23 @@ def tile_attend_gadal_kernel(tc, xT, qT, dyT, pT, lam, us, offs, out_0, out_1):
         whole = slice(0, SLOTS)
         first_dq = dq_copy(nc.scalar.copy, "dq0_0", dq_product(0, "d0", 0), halves(0))
         scatter_on_scalar(0, first_dq[:], 0)
-        second_dq = dq_copy(nc.vector.tensor_copy, "dq1", dq_product(1, "a0"), whole)
+        second_acc = dq_product(1, "a0")
         first_dq = dq_copy(nc.scalar.copy, "dq0_1", dq_product(0, "d1", 1), halves(1))
-        third_dq = dq_copy(nc.vector.tensor_copy, "dq2", dq_product(2, "a1"), whole)
-        last_dq = dq_copy(nc.vector.tensor_copy, "dq3", dq_product(3, "v2"), whole)
-        gather_q(0)
-        nc.vector.tensor_copy(listed(windows[0], 1), first_dq[:])
+        scatter_on_scalar(0, first_dq[:], 1)
         nc.sync.dma_start(out_rows[0], windows[0][:])
-        gather_q(1)
-        for half in range(2):
-            scatter_on_scalar(1, second_dq[:, halves(half)], half)
+        second_dq = [
+            dq_copy(nc.vector.tensor_copy, "dq1_0", second_acc, halves(0), offset=6144),
+            dq_copy(nc.vector.tensor_copy, "dq1_1", second_acc, halves(1)),
+        ]
+        nc.vector.tensor_copy(listed(windows[1], 0), second_dq[0][:])
+        scatter_on_scalar(1, second_dq[1][:], 1)
         nc.sync.dma_start(out_rows[1], windows[1][:])
+        third_dq = dq_copy(nc.vector.tensor_copy, "dq2", dq_product(2, "a1"), whole)
+        gather_q(0)
+        gather_q(1)
         scatter_on_scalar(2, third_dq[:, halves(0)], 0)
         scatter_on_scalar(2, third_dq[:, halves(1)], 1)
         nc.sync.dma_start(out_rows[2], windows[2][:])
-        for half in range(2):
-            scatter_on_scalar(3, last_dq[:, halves(half)], half)
-        nc.sync.dma_start(out_rows[3], windows[3][:])
 
         w_turned = []
 
@@ -299,6 +299,11 @@ def tile_attend_gadal_kernel(tc, xT, qT, dyT, pT, lam, us, offs, out_0, out_1):
 
         make_w(0, "g_words1")
         gather_q(2)
+        last_dq = dq_copy(nc.vector.tensor_copy, "dq3", dq_product(3, "v2"), whole, tag="q_table2")
+        for half in range(2):
+            scatter_on_scalar(3, last_dq[:, halves(half)], half)
+        nc.sync.dma_start(out_rows[3], windows[3][:])
+
         gather_q(3)
 
         xd_codes = tile("xd_codes", K, U32)

@@ -20,6 +20,7 @@ K = P * PACK
 SLOTS = 512
 PIECES = 2048
 HALF = SLOTS // 2
+RUN = 4
 QUAD = 32
 
 FLOPS = 3 * 2 * K * K * SLOTS
@@ -237,12 +238,10 @@ def tile_attend_gadal_kernel(tc, xT, qT, dyT, pT, lam, us, offs, out_0, out_1):
             matmul(acc[:, cols], xr[j][0], xr[j][1], E4M3, g_codes[:, cols], g_scales[:, cols], E5M2)
             return acc
 
-        def dq_copy(copy, name, acc, cols, offset=None, tag=None):
-            width = cols.stop - cols.start
-            dq = tile(name, width, F32, tag=tag) if offset is None else tile_at(name, width, F32, offset)
+        def dq_copy(dq, acc, copy=nc.scalar.copy):
             copy(
-                dq[:].rearrange("p (h a b k) -> p h a b k", a=PACK, b=2, k=QUAD),
-                acc[:, cols].rearrange("p (h b a k) -> p h a b k", a=PACK, b=2, k=QUAD),
+                dq.rearrange("p (h a b k) -> p h a b k", a=PACK, b=2, k=QUAD),
+                acc.rearrange("p (h b a k) -> p h a b k", a=PACK, b=2, k=QUAD),
             )
             return dq
 
@@ -262,31 +261,30 @@ def tile_attend_gadal_kernel(tc, xT, qT, dyT, pT, lam, us, offs, out_0, out_1):
             x_raw[:].rearrange("p (j m t) -> p t m j", j=PACK, t=PACK),
         )
 
+        first_dq = [tile(f"dq0_{half}", HALF, F32)[:] for half in range(2)]
+        scatter_on_scalar(0, dq_copy(first_dq[0], dq_product(0, "d0", 0)[:, halves(0)]), 0)
+        second_dq = dq_copy(tile_at("dq1", SLOTS, F32, 6144)[:], dq_product(1, "a0")[:], nc.vector.tensor_copy)
+        dq_copy(first_dq[1], dq_product(0, "d1", 1)[:, halves(1)])
+        third_dq = dq_copy(tile("dq2", SLOTS, F32)[:], dq_product(2, "a1")[:])
+        scatter_on_scalar(0, first_dq[1], 1)
+        nc.sync.dma_start(out_rows[0], windows[0][:])
+        nc.vector.tensor_copy(listed(windows[1]), second_dq)
+        nc.sync.dma_start(out_rows[1], windows[1][:])
+
         q_planes = tile_at("q_planes", PACK * SLOTS, BF16, 4096)
 
         def gather_q(t):
             nc.vector.tensor_copy(q_planes[:, halves(t, SLOTS)], listed(q_tables[t]))
 
-        whole = slice(0, SLOTS)
-        first_dq = dq_copy(nc.scalar.copy, "dq0_0", dq_product(0, "d0", 0), halves(0))
-        scatter_on_scalar(0, first_dq[:], 0)
-        second_acc = dq_product(1, "a0")
-        first_dq = dq_copy(nc.scalar.copy, "dq0_1", dq_product(0, "d1", 1), halves(1))
-        scatter_on_scalar(0, first_dq[:], 1)
-        nc.sync.dma_start(out_rows[0], windows[0][:])
-        second_dq = [
-            dq_copy(nc.vector.tensor_copy, "dq1_0", second_acc, halves(0), offset=6144),
-            dq_copy(nc.vector.tensor_copy, "dq1_1", second_acc, halves(1)),
-        ]
-        nc.vector.tensor_copy(listed(windows[1], 0), second_dq[0][:])
-        scatter_on_scalar(1, second_dq[1][:], 1)
-        nc.sync.dma_start(out_rows[1], windows[1][:])
-        third_dq = dq_copy(nc.vector.tensor_copy, "dq2", dq_product(2, "a1"), whole)
-        gather_q(0)
         gather_q(1)
         scatter_on_scalar(2, third_dq[:, halves(0)], 0)
+        nc.scalar.activation(q_planes[:, halves(0, SLOTS)], listed(q_tables[0]), COPY)
+        last_dq = dq_copy(tile("dq3", SLOTS, F32, tag="dq0_1")[:], dq_product(3, "v2")[:])
         scatter_on_scalar(2, third_dq[:, halves(1)], 1)
         nc.sync.dma_start(out_rows[2], windows[2][:])
+        for half in range(2):
+            scatter_on_scalar(3, last_dq[:, halves(half)], half)
+        nc.sync.dma_start(out_rows[3], windows[3][:])
 
         w_turned = []
 
@@ -299,11 +297,6 @@ def tile_attend_gadal_kernel(tc, xT, qT, dyT, pT, lam, us, offs, out_0, out_1):
 
         make_w(0, "g_words1")
         gather_q(2)
-        last_dq = dq_copy(nc.vector.tensor_copy, "dq3", dq_product(3, "v2"), whole, tag="q_table2")
-        for half in range(2):
-            scatter_on_scalar(3, last_dq[:, halves(half)], half)
-        nc.sync.dma_start(out_rows[3], windows[3][:])
-
         gather_q(3)
 
         xd_codes = tile("xd_codes", K, U32)
@@ -311,10 +304,11 @@ def tile_attend_gadal_kernel(tc, xT, qT, dyT, pT, lam, us, offs, out_0, out_1):
         quantize(xd_codes[:], xd_scales[:], xd_words[:], E4M3)
         q_words = [tile(f"q_words{half}", PACK * HALF, BF16) for half in range(2)]
         for half in range(2):
-            nc.vector.tensor_copy(
-                q_words[half][:].rearrange("p (b a k t) -> p b a k t", b=2, a=PACK, t=PACK),
-                q_planes[:].rearrange("p (t h a b k) -> p h b a k t", t=PACK, h=2, a=PACK, b=2)[:, half],
-            )
+            for b in range(2):
+                nc.vector.tensor_copy(
+                    q_words[half][:, halves(b, K)].rearrange("p (a c i t) -> p a c t i", a=PACK, i=RUN, t=PACK),
+                    q_planes[:].rearrange("p (t h a b c i) -> p h b a c t i", t=PACK, h=2, a=PACK, b=2, i=RUN)[:, half, b],
+                )
         q_codes = tile("q_codes", SLOTS, U32)
         q_scales = tile("q_scales", SLOTS, U8)
         for half in range(2):

@@ -69,7 +69,9 @@ def tile_attend_gadal_kernel(tc, xT, qT, dyT, pT, lam, us, offs, out_0, out_1):
         q_rows = qT.rearrange("(p t) n -> t p n", t=PACK)
         x_rows = xT.rearrange("(p t) r -> p (t r)", t=PACK)
         p_tables = [tile(f"p_table{t}", PIECES, F32) for t in range(PACK)]
-        q_tables = [tile_at("q_table0", PIECES, F32, 8192)] + [tile(f"q_table{t}", PIECES, F32) for t in range(1, PACK)]
+        q_tables = [tile(f"q_table{t}", PIECES, F32) for t in range(PACK)]
+        q_tables[0] = tile_at("q_table_first", PIECES, F32, 16384)
+        q_tables[1] = tile_at("q_table_scalar", PIECES, F32, 8192)
         dy_raw = tile("dy_raw", PACK * K, F32)
         x_raw = tile("x_raw", PACK * K, F32)
         offsets = tile("offsets", SLOTS // 16, U16)
@@ -82,8 +84,8 @@ def tile_attend_gadal_kernel(tc, xT, qT, dyT, pT, lam, us, offs, out_0, out_1):
         nc.sync.dma_start(us_cols[:], us.rearrange("(p t) o -> p (t o)", t=PACK))
         for t in range(PACK):
             nc.sync.dma_start(p_tables[t][:], p_rows[t])
-        for pair in range(2):
-            nc.sync.dma_start(x_raw[:, halves(pair, 2 * K)], x_rows[:, halves(pair, 2 * K)])
+        for cols in (slice(0, K), slice(K, 2 * K), slice(2 * K, PACK * K)):
+            nc.sync.dma_start(x_raw[:, cols], x_rows[:, cols])
         for t in range(PACK):
             nc.sync.dma_start(q_tables[t][:], q_rows[t])
 
@@ -125,14 +127,11 @@ def tile_attend_gadal_kernel(tc, xT, qT, dyT, pT, lam, us, offs, out_0, out_1):
         nc.scalar.copy(us_rows[:], spread[:])
 
         dy_words = tile("dy_words", PACK * K, BF16)
-        def deal(copy, words, raw, pair):
-            copy(
-                words.rearrange("p (t m j) -> p m j t", t=2, j=PACK),
-                raw[:].rearrange("p (j m t) -> p m j t", j=PACK, t=PACK)[:, :, :, 2 * pair : 2 * pair + 2],
-            )
-
         for pair in range(2):
-            deal(nc.vector.tensor_copy, dy_words[:, halves(pair, 2 * K)], dy_raw, pair)
+            nc.vector.tensor_copy(
+                dy_words[:, halves(pair, 2 * K)].rearrange("p (t m j) -> p m j t", t=2, j=PACK),
+                dy_raw[:].rearrange("p (j m t) -> p m j t", j=PACK, t=PACK)[:, :, :, 2 * pair : 2 * pair + 2],
+            )
         dy_codes = tile("dy_codes", K, U32)
         dy_scales = tile("dy_scales", K, U8)
         quantize(dy_codes[:], dy_scales[:], dy_words[:], E5M2)
@@ -157,7 +156,7 @@ def tile_attend_gadal_kernel(tc, xT, qT, dyT, pT, lam, us, offs, out_0, out_1):
         for t in (2, 3):
             nc.vector.tensor_copy(by_slot(p_words[0], PACK)[:, :, :, :, t], listed(p_tables[t], 0))
             nc.scalar.activation(p_late[:, halves(t - 2)], listed(p_tables[t], 1), COPY)
-        nc.scalar.copy(
+        nc.vector.tensor_copy(
             by_slot(p_words[1], PACK)[:, :, :, :, 2:PACK],
             p_late[:].rearrange("p (t a b k) -> p a b k t", t=2, a=PACK, b=2),
         )
@@ -166,12 +165,38 @@ def tile_attend_gadal_kernel(tc, xT, qT, dyT, pT, lam, us, offs, out_0, out_1):
         for half in range(2):
             quantize(p_codes[:, halves(half)], p_scales[:, halves(half)], p_words[half], E4M3)
 
-        x_narrow = tile("x_narrow", PACK * K, BF16, tag="lam_slots")
+        x_narrow = []
         for j in range(PACK):
-            nc.gpsimd.tensor_copy(x_narrow[:, halves(j, K)], x_raw[:, halves(j, K)])
+            x_narrow.append(tile(f"x_narrow{j}", K, BF16, tag={0: "p_words0", 2: "lam_slots"}.get(j)))
+            (nc.scalar.copy if j < 2 else nc.gpsimd.tensor_copy)(
+                x_narrow[j][:].rearrange("p (u m e) -> p u m e", u=2, e=2),
+                x_raw[:, halves(j, K)].rearrange("p (m u e) -> p u m e", u=2, e=2),
+            )
+
+        xr = {}
+
+        def turn_x(planes, bank_tag, words):
+            turned = bank(f"x_turned{planes[0]}", bank_tag)
+            for n, j in enumerate(planes):
+                for u in range(2):
+                    nc.tensor.transpose(
+                        turned[:, halves(2 * n + u, P)], x_narrow[j][:].bitcast(F32)[:, halves(u, P)], ident[:]
+                    )
+            nc.scalar.copy(
+                words[:].bitcast(F32).rearrange("p (j c u) -> p j c u", c=P, u=2),
+                turned[:, : len(planes) * 2 * P].rearrange("p (j u c) -> p j c u", c=P, u=2),
+            )
+            return words
+
+        def quantize_x(planes, words, codes, scales):
+            quantize(codes[:], scales[:], words[:], E4M3)
+            for n, j in enumerate(planes):
+                xr[j] = (codes[:, halves(n, P)], scales[:, halves(n, P)])
 
         v_banks = []
         for a in range(PACK):
+            if a == 2:
+                first_words = turn_x((0,), "a0", tile_at("xr_words0", K, BF16, 4096))
             v_banks.append(bank(f"v{a}", f"v{a}"))
             for t in range(PACK):
                 matmul(
@@ -184,9 +209,9 @@ def tile_attend_gadal_kernel(tc, xT, qT, dyT, pT, lam, us, offs, out_0, out_1):
                     E4M3,
                 )
 
-        g_words = [tile(f"g_words{half}", PACK * HALF, BF16) for half in range(2)]
+        g_words = [tile("g_words0", PACK * HALF, BF16), tile_at("g_words1", PACK * HALF, BF16, 4096)]
         g_codes = tile("g_codes", SLOTS, U32)
-        g_scales = tile("g_scales", SLOTS, U8, tag="factors1")
+        g_scales = tile("g_scales", SLOTS, U8)
 
         def form_g(a):
             nc.vector.tensor_tensor(
@@ -199,35 +224,22 @@ def tile_attend_gadal_kernel(tc, xT, qT, dyT, pT, lam, us, offs, out_0, out_1):
         def quantize_g(half):
             quantize(g_codes[:, halves(half)], g_scales[:, halves(half)], g_words[half][:], E5M2)
 
-
-        x_pairs = x_narrow[:].bitcast(F32)
-        xr = []
-
-        def turn_x(pair, scales_tag):
-            turned = bank(f"x_turned{pair}", f"a{pair}")
-            for n in range(2):
-                j = 2 * pair + n
-                for u in range(2):
-                    nc.tensor.transpose(
-                        turned[:, halves(2 * n + u, P)], x_pairs[:, j * HALF + u : (j + 1) * HALF : 2], ident[:]
-                    )
-            words = tile_at("xr_words1", 2 * K, BF16, 3072) if pair else tile("xr_words0", 2 * K, BF16)
-            nc.scalar.copy(
-                words[:].bitcast(F32).rearrange("p (j c u) -> p j c u", j=2, u=2),
-                turned[:].rearrange("p (j u c) -> p j c u", j=2, u=2),
-            )
-            codes = tile("xr_codes1", 2 * P, U32) if pair else tile_at("xr_codes0", 2 * P, U32, 5120)
-            scales = tile(f"xr_scales{pair}", 2 * P, U8, tag=scales_tag)
-            quantize(codes[:], scales[:], words[:], E4M3)
-            for n in range(2):
-                xr.append((codes[:, halves(n, P)], scales[:, halves(n, P)]))
-
-        for a in range(PACK - 1):
-            form_g(a)
+        form_g(0)
+        form_g(1)
+        quantize_x((0,), first_words, tile("xr_codes0", P, U32), tile("xr_scales0", P, U8))
         quantize_g(0)
-        turn_x(0, "factors2")
-        form_g(PACK - 1)
-        turn_x(1, "factors3")
+        form_g(2)
+        form_g(3)
+
+        v_planes = tile("v_planes", PACK * HALF, F32)
+        for b in range(2):
+            nc.scalar.copy(
+                v_planes[:].rearrange("p (t b n) -> p b t n", t=PACK, b=2)[:, b],
+                v_banks[b][:].rearrange("p (t n) -> p t n", t=PACK),
+            )
+
+        words = turn_x((1, 2), "a0", tile("xr_words12", 2 * K, BF16))
+        quantize_x((1, 2), words, tile("xr_codes12", 2 * P, U32), tile("xr_scales12", 2 * P, U8))
         quantize_g(1)
 
         out_rows = out_1.rearrange("(p j) n -> j p n", j=PACK)
@@ -248,12 +260,39 @@ def tile_attend_gadal_kernel(tc, xT, qT, dyT, pT, lam, us, offs, out_0, out_1):
         def scatter_on_scalar(j, dq, half):
             nc.scalar.activation(listed(windows[j], half), dq, COPY)
 
-        v_planes = tile("v_planes", PACK * HALF, F32)
-        for b in range(2):
-            nc.scalar.copy(
-                v_planes[:].rearrange("p (t b n) -> p b t n", t=PACK, b=2)[:, b],
-                v_banks[b][:].rearrange("p (t n) -> p t n", t=PACK),
-            )
+        dq0_0 = dq_copy(tile("dq0_0", HALF, F32)[:], dq_product(0, "d0", 0)[:, halves(0)])
+        last_words = turn_x((3,), "v1", tile_at("xr_words3", K, BF16, 0))
+        scatter_on_scalar(0, dq0_0, 0)
+
+        w_turned = []
+
+        def make_w(b, bank_tag, tag):
+            v_turned = bank(f"v_turned{b}", bank_tag)
+            cols = halves(2 + b, P)
+            matmul(v_turned[:], p_codes[:, cols], p_scales[:, cols], E4M3, dy_codes[:], dy_scales[:], E5M2)
+            w_turned.append(tile(f"w_turned{b}", K, F32, tag=tag))
+            nc.vector.tensor_tensor(w_turned[b][:], v_turned[:], us_rows[:], MULT)
+
+        q_planes = tile_at("q_planes", PACK * SLOTS, BF16, 4096)
+
+        def gather_q(t):
+            nc.vector.tensor_copy(q_planes[:, halves(t, SLOTS)], listed(q_tables[t]))
+
+        gather_q(0)
+        make_w(0, "v3", None)
+        dq0_1 = dq_copy(tile("dq0_1", HALF, F32)[:], dq_product(0, "d1", 1)[:, halves(1)])
+        dq1 = dq_copy(tile_at("dq1", SLOTS, F32, 16384)[:], dq_product(1, "v2")[:], nc.vector.tensor_copy)
+        acc2 = dq_product(2, "v0")
+        dq2_0 = dq_copy(tile("dq2_0", HALF, F32)[:], acc2[:, halves(0)])
+        scatter_on_scalar(0, dq0_1, 1)
+        nc.sync.dma_start(out_rows[0], windows[0][:])
+        scatter_on_scalar(2, dq2_0, 0)
+
+        quantize_x((3,), last_words, tile("xr_codes3", P, U32), tile_at("xr_scales3", P, U8, 18432))
+        nc.vector.tensor_copy(listed(windows[1]), dq1)
+        nc.sync.dma_start(out_rows[1], windows[1][:])
+        acc3 = dq_product(3, "a1")
+        dq3_1 = dq_copy(tile("dq3_1", HALF, F32)[:], acc3[:, halves(1)], nc.vector.tensor_copy)
 
         xd_words = tile_at("xd_words", PACK * K, BF16, 0)
         nc.gpsimd.tensor_copy(
@@ -261,60 +300,42 @@ def tile_attend_gadal_kernel(tc, xT, qT, dyT, pT, lam, us, offs, out_0, out_1):
             x_raw[:].rearrange("p (j m t) -> p t m j", j=PACK, t=PACK),
         )
 
-        first_dq = [tile(f"dq0_{half}", HALF, F32)[:] for half in range(2)]
-        scatter_on_scalar(0, dq_copy(first_dq[0], dq_product(0, "d0", 0)[:, halves(0)]), 0)
-        second_dq = dq_copy(tile_at("dq1", SLOTS, F32, 6144)[:], dq_product(1, "a0")[:], nc.vector.tensor_copy)
-        dq_copy(first_dq[1], dq_product(0, "d1", 1)[:, halves(1)])
-        third_dq = dq_copy(tile("dq2", SLOTS, F32)[:], dq_product(2, "a1")[:])
-        scatter_on_scalar(0, first_dq[1], 1)
-        nc.sync.dma_start(out_rows[0], windows[0][:])
-        nc.vector.tensor_copy(listed(windows[1]), second_dq)
-        nc.sync.dma_start(out_rows[1], windows[1][:])
-
-        q_planes = tile_at("q_planes", PACK * SLOTS, BF16, 4096)
-
-        def gather_q(t):
-            nc.vector.tensor_copy(q_planes[:, halves(t, SLOTS)], listed(q_tables[t]))
-
-        gather_q(1)
-        scatter_on_scalar(2, third_dq[:, halves(0)], 0)
-        nc.scalar.activation(q_planes[:, halves(0, SLOTS)], listed(q_tables[0]), COPY)
-        last_dq = dq_copy(tile("dq3", SLOTS, F32, tag="dq0_1")[:], dq_product(3, "v2")[:])
-        scatter_on_scalar(2, third_dq[:, halves(1)], 1)
-        nc.sync.dma_start(out_rows[2], windows[2][:])
-        for half in range(2):
-            scatter_on_scalar(3, last_dq[:, halves(half)], half)
-        nc.sync.dma_start(out_rows[3], windows[3][:])
-
-        w_turned = []
-
-        def make_w(b, tag):
-            v_turned = bank(f"v_turned{b}", f"d{b}")
-            cols = halves(2 + b, P)
-            matmul(v_turned[:], p_codes[:, cols], p_scales[:, cols], E4M3, dy_codes[:], dy_scales[:], E5M2)
-            w_turned.append(tile(f"w_turned{b}", K, F32, tag=tag))
-            nc.vector.tensor_tensor(w_turned[b][:], v_turned[:], us_rows[:], MULT)
-
-        make_w(0, "g_words1")
         gather_q(2)
-        gather_q(3)
+        for half in range(2):
+            nc.vector.tensor_copy(q_planes[:, halves(6 + half)], listed(q_tables[3], half))
+
+        nc.scalar.activation(q_planes[:, halves(1, SLOTS)], listed(q_tables[1]), COPY)
+        dq2_1 = dq_copy(tile_at("dq2_1", HALF, F32, 8192)[:], acc2[:, halves(1)])
+        dq3_0 = dq_copy(tile_at("dq3_0", HALF, F32, 9216)[:], acc3[:, halves(0)])
+        scatter_on_scalar(2, dq2_1, 1)
+        nc.sync.dma_start(out_rows[2], windows[2][:])
+        scatter_on_scalar(3, dq3_0, 0)
+        scatter_on_scalar(3, dq3_1, 1)
+        nc.sync.dma_start(out_rows[3], windows[3][:])
 
         xd_codes = tile("xd_codes", K, U32)
         xd_scales = tile("xd_scales", K, U8, tag="q_table3")
-        quantize(xd_codes[:], xd_scales[:], xd_words[:], E4M3)
         q_words = [tile(f"q_words{half}", PACK * HALF, BF16) for half in range(2)]
-        for half in range(2):
-            for b in range(2):
-                nc.vector.tensor_copy(
-                    q_words[half][:, halves(b, K)].rearrange("p (a c i t) -> p a c t i", a=PACK, i=RUN, t=PACK),
-                    q_planes[:].rearrange("p (t h a b c i) -> p h b a c t i", t=PACK, h=2, a=PACK, b=2, i=RUN)[:, half, b],
-                )
         q_codes = tile("q_codes", SLOTS, U32)
         q_scales = tile("q_scales", SLOTS, U8)
-        for half in range(2):
+
+        def interleave_q(half, b):
+            nc.vector.tensor_copy(
+                q_words[half][:, halves(b, K)].rearrange("p (a c i t) -> p a c t i", a=PACK, i=RUN, t=PACK),
+                q_planes[:].rearrange("p (t h a b c i) -> p h b a c t i", t=PACK, h=2, a=PACK, b=2, i=RUN)[:, half, b],
+            )
+
+        def quantize_q(half):
             quantize(q_codes[:, halves(half)], q_scales[:, halves(half)], q_words[half][:], E4M3)
 
-        make_w(1, "q_words0")
+        interleave_q(0, 0)
+        interleave_q(0, 1)
+        quantize(xd_codes[:], xd_scales[:], xd_words[:], E4M3)
+        quantize_q(0)
+        interleave_q(1, 0)
+        interleave_q(1, 1)
+        make_w(1, "d0", "q_words0")
+        quantize_q(1)
 
         step = QUAD // PACK
         u_banks = [bank(f"u{pair}", f"v{pair}") for pair in range(2)]
@@ -329,11 +350,11 @@ def tile_attend_gadal_kernel(tc, xT, qT, dyT, pT, lam, us, offs, out_0, out_1):
                 E4M3,
             )
         u_turned = []
-        for b, tag in ((0, "a0"), (1, "v3")):
+        for b, tag in ((0, "v3"), (1, "v2")):
             u_turned.append(bank(f"u_turned{b}", tag))
             cols = halves(2 + b, P)
             matmul(u_turned[b][:], q_codes[:, cols], q_scales[:, cols], E4M3, xd_codes[:], xd_scales[:], E4M3)
-        total = bank("total", "a1")
+        total = bank("total", "d1")
         for t in range(PACK):
             h = tile(f"h{t}", HALF, F32)
             nc.vector.scalar_tensor_tensor(

@@ -156,18 +156,19 @@ def tile_attend_gadal_kernel(tc, xT, qT, dyT, pT, lam, us, offs, out_0, out_1):
         for t in (2, 3):
             nc.vector.tensor_copy(by_slot(p_words[0], PACK)[:, :, :, :, t], listed(p_tables[t], 0))
             nc.scalar.activation(p_late[:, halves(t - 2)], listed(p_tables[t], 1), COPY)
+        p_codes = tile("p_codes", SLOTS, U32)
+        p_scales = tile("p_scales", SLOTS, U8)
+        quantize(p_codes[:, halves(0, P)], p_scales[:, halves(0, P)], p_words[0][:, halves(0, K)], E4M3)
         nc.vector.tensor_copy(
             by_slot(p_words[1], PACK)[:, :, :, :, 2:PACK],
             p_late[:].rearrange("p (t a b k) -> p a b k t", t=2, a=PACK, b=2),
         )
-        p_codes = tile("p_codes", SLOTS, U32)
-        p_scales = tile("p_scales", SLOTS, U8)
-        for half in range(2):
-            quantize(p_codes[:, halves(half)], p_scales[:, halves(half)], p_words[half], E4M3)
+        quantize(p_codes[:, halves(1, P)], p_scales[:, halves(1, P)], p_words[0][:, halves(1, K)], E4M3)
+        quantize(p_codes[:, halves(1)], p_scales[:, halves(1)], p_words[1], E4M3)
 
         x_narrow = []
         for j in range(PACK):
-            x_narrow.append(tile(f"x_narrow{j}", K, BF16, tag={0: "p_words0", 2: "lam_slots"}.get(j)))
+            x_narrow.append(tile(f"x_narrow{j}", K, BF16, tag={0: "p_table3", 1: "p_words0", 2: "lam_slots"}.get(j)))
             (nc.scalar.copy if j < 2 else nc.gpsimd.tensor_copy)(
                 x_narrow[j][:].rearrange("p (u m e) -> p u m e", u=2, e=2),
                 x_raw[:, halves(j, K)].rearrange("p (m u e) -> p u m e", u=2, e=2),
@@ -195,7 +196,7 @@ def tile_attend_gadal_kernel(tc, xT, qT, dyT, pT, lam, us, offs, out_0, out_1):
 
         v_banks = []
         for a in range(PACK):
-            if a == 2:
+            if a == 1:
                 first_words = turn_x((0,), "a0", tile_at("xr_words0", K, BF16, 4096))
             v_banks.append(bank(f"v{a}", f"v{a}"))
             for t in range(PACK):
@@ -263,6 +264,7 @@ def tile_attend_gadal_kernel(tc, xT, qT, dyT, pT, lam, us, offs, out_0, out_1):
         dq0_0 = dq_copy(tile("dq0_0", HALF, F32)[:], dq_product(0, "d0", 0)[:, halves(0)])
         last_words = turn_x((3,), "v1", tile_at("xr_words3", K, BF16, 0))
         scatter_on_scalar(0, dq0_0, 0)
+        quantize_x((3,), last_words, tile("xr_codes3", P, U32), tile("xr_scales3", P, U8))
 
         w_turned = []
 
@@ -288,11 +290,10 @@ def tile_attend_gadal_kernel(tc, xT, qT, dyT, pT, lam, us, offs, out_0, out_1):
         nc.sync.dma_start(out_rows[0], windows[0][:])
         scatter_on_scalar(2, dq2_0, 0)
 
-        quantize_x((3,), last_words, tile("xr_codes3", P, U32), tile_at("xr_scales3", P, U8, 18432))
-        nc.vector.tensor_copy(listed(windows[1]), dq1)
-        nc.sync.dma_start(out_rows[1], windows[1][:])
         acc3 = dq_product(3, "a1")
         dq3_1 = dq_copy(tile("dq3_1", HALF, F32)[:], acc3[:, halves(1)], nc.vector.tensor_copy)
+        nc.vector.tensor_copy(listed(windows[1]), dq1)
+        nc.sync.dma_start(out_rows[1], windows[1][:])
 
         xd_words = tile_at("xd_words", PACK * K, BF16, 0)
         nc.gpsimd.tensor_copy(

@@ -70,7 +70,6 @@ def tile_attend_gadal_kernel(tc, xT, qT, dyT, pT, lam, us, offs, out_0, out_1):
         x_rows = xT.rearrange("(p t) r -> p (t r)", t=PACK)
         p_tables = [tile(f"p_table{t}", PIECES, F32) for t in range(PACK)]
         q_tables = [tile(f"q_table{t}", PIECES, F32) for t in range(PACK)]
-        q_tables[0] = tile_at("q_table_first", PIECES, F32, 16384)
         q_tables[1] = tile_at("q_table_scalar", PIECES, F32, 8192)
         dy_raw = tile("dy_raw", PACK * K, F32)
         x_raw = tile("x_raw", PACK * K, F32)
@@ -280,10 +279,9 @@ def tile_attend_gadal_kernel(tc, xT, qT, dyT, pT, lam, us, offs, out_0, out_1):
         def gather_q(t):
             nc.vector.tensor_copy(q_planes[:, halves(t, SLOTS)], listed(q_tables[t]))
 
-        gather_q(0)
         make_w(0, "v3", None)
-        dq0_1 = dq_copy(tile("dq0_1", HALF, F32)[:], dq_product(0, "d1", 1)[:, halves(1)])
-        dq1 = dq_copy(tile_at("dq1", SLOTS, F32, 16384)[:], dq_product(1, "v2")[:], nc.vector.tensor_copy)
+        dq0_1 = dq_copy(tile("dq0_1", HALF, F32)[:], dq_product(0, "d1", 1)[:, halves(1)], nc.vector.tensor_copy)
+        dq1 = dq_copy(tile("dq1", SLOTS, F32)[:], dq_product(1, "v2")[:], nc.vector.tensor_copy)
         acc2 = dq_product(2, "v0")
         dq2_0 = dq_copy(tile("dq2_0", HALF, F32)[:], acc2[:, halves(0)])
         scatter_on_scalar(0, dq0_1, 1)
@@ -301,6 +299,7 @@ def tile_attend_gadal_kernel(tc, xT, qT, dyT, pT, lam, us, offs, out_0, out_1):
             x_raw[:].rearrange("p (j m t) -> p t m j", j=PACK, t=PACK),
         )
 
+        gather_q(0)
         gather_q(2)
         for half in range(2):
             nc.vector.tensor_copy(q_planes[:, halves(6 + half)], listed(q_tables[3], half))

@@ -311,7 +311,7 @@ def tile_attend_gadal_kernel(tc, xT, qT, dyT, pT, lam, us, offs, out_0, out_1):
         nc.sync.dma_start(out_rows[2], windows[2][:])
         scatter_on_scalar(3, dq3_0, 0)
         scatter_on_scalar(3, dq3_1, 1)
-        nc.sync.dma_start(out_rows[3], windows[3][:])
+        nc.scalar.dma_start(out_rows[3], windows[3][:])
 
         xd_codes = tile("xd_codes", K, U32)
         xd_scales = tile("xd_scales", K, U8, tag="q_table3")
@@ -381,7 +381,7 @@ def tile_attend_gadal_kernel(tc, xT, qT, dyT, pT, lam, us, offs, out_0, out_1):
             nc.scalar.activation(spent[:, halves(b, P)], total[:, halves(b, P)], COPY, accum_out=sums[:, col : col + 1])
         s_rows = tile("s_rows", QUAD, F32)
         nc.vector.transpose(s_rows[:], sums[:])
-        for half in range(2):
-            nc.sync.dma_start(
+        for half, queue in enumerate((nc.scalar, nc.sync)):
+            queue.dma_start(
                 out_0[:, halves(half)].rearrange("o (n k) -> (o n) k", k=QUAD), s_rows[half * step : P : 2 * step, :]
             )

@@ -215,9 +215,9 @@ def tile_attend_gadal_kernel(tc, xT, qT, dyT, pT, lam, us, offs, out_0, out_1):
 
         def form_g(a):
             nc.vector.tensor_tensor(
-                g_words[a // 2][:, halves(a % 2, K)].rearrange("p (n t) -> p n t", t=PACK),
-                v_banks[a][:].rearrange("p (t n) -> p n t", t=PACK),
-                factors[a][:].rearrange("p (n t) -> p n t", t=PACK),
+                g_words[a // 2][:, halves(a % 2, K)].rearrange("p (c i t) -> p c t i", i=2, t=PACK),
+                v_banks[a][:].rearrange("p (t c i) -> p c t i", i=2, t=PACK),
+                factors[a][:].rearrange("p (c i t) -> p c t i", i=2, t=PACK),
                 MULT,
             )
 

from contextlib import ExitStack

import concourse.mybir as mybir
from concourse.masks import make_identity

F32 = mybir.dt.float32
BF16 = mybir.dt.bfloat16
U32 = mybir.dt.uint32
I32 = mybir.dt.int32
U16 = mybir.dt.uint16
U8 = mybir.dt.uint8
E4M3 = mybir.dt.float8_e4m3fn_x4
E5M2 = mybir.dt.float8_e5m2_x4
MULT = mybir.AluOpType.mult
COPY = mybir.ActivationFunctionType.Copy

P = 128
PACK = 4
K = P * PACK
SLOTS = 512
PIECES = 2048
HALF = SLOTS // 2
RUN = 4
QUAD = 32

FLOPS = 3 * 2 * K * K * SLOTS
BYTES = 4 * (2 * K * K + 3 * K * PIECES + PIECES + K + SLOTS) + 2 * P * SLOTS // 16


def halves(half, width=HALF):
    return slice(half * width, (half + 1) * width)


def by_slot(ap, inner):
    return ap.rearrange("p (b a k t) -> p a b k t", b=2, a=PACK, t=inner)


def tile_attend_gadal_kernel(tc, xT, qT, dyT, pT, lam, us, offs, out_0, out_1):
    nc = tc.nc
    with ExitStack() as ctx:
        sb = ctx.enter_context(tc.tile_pool(name="sb", bufs=1))
        laid = ctx.enter_context(tc.tile_pool(name="laid", bufs=1))
        ps = ctx.enter_context(tc.psum_pool(name="ps", bufs=1))

        def tile(name, width, dtype, tag=None):
            return sb.tile([P, width], dtype, name=name, tag=tag or name, align_bytes=64)

        def tile_at(name, width, dtype, offset):
            return laid.tile([P, width], dtype, name=name, offset=offset, align_bytes=64)

        def bank(name, tag):
            return ps.tile([P, SLOTS], F32, name=name, tag=tag)

        def quantize(codes, scales, values, fmt):
            nc.vector.quantize_mx(out=codes.bitcast(fmt), scales=scales, in_=values)

        def matmul(out, lhs, lhs_scales, lhs_fmt, rhs, rhs_scales, rhs_fmt):
            nc.tensor.matmul_mx(
                out=out,
                lhsT=lhs.bitcast(lhs_fmt),
                lhsT_scale=lhs_scales,
                rhs=rhs.bitcast(rhs_fmt),
                rhs_scale=rhs_scales,
                start=True,
                stop=True,
            )

        p_rows = pT.rearrange("(p t) n -> t p n", t=PACK)
        q_rows = qT.rearrange("(p t) n -> t p n", t=PACK)
        x_rows = xT.rearrange("(p t) r -> p (t r)", t=PACK)
        p_tables = [tile(f"p_table{t}", PIECES, F32) for t in range(PACK)]
        q_tables = [tile(f"q_table{t}", PIECES, F32) for t in range(PACK)]
        q_tables[1] = tile_at("q_table_scalar", PIECES, F32, 8192)
        dy_raw = tile("dy_raw", PACK * K, F32)
        x_raw = tile("x_raw", PACK * K, F32)
        offsets = tile("offsets", SLOTS // 16, U16)
        lam_cols = tile("lam_cols", PIECES // P, F32)
        us_cols = tile("us_cols", PACK, F32)

        nc.sync.dma_start(lam_cols[:], lam[0:1, :].rearrange("o (p c) -> (o p) c", p=P))
        nc.sync.dma_start(dy_raw[:], dyT.rearrange("(p t) r -> p (t r)", t=PACK))
        nc.sync.dma_start(offsets[:], offs)
        nc.sync.dma_start(us_cols[:], us.rearrange("(p t) o -> p (t o)", t=PACK))
        for t in range(PACK):
            nc.sync.dma_start(p_tables[t][:], p_rows[t])
        for cols in (slice(0, K), slice(K, 2 * K), slice(2 * K, PACK * K)):
            nc.sync.dma_start(x_raw[:, cols], x_rows[:, cols])
        for t in range(PACK):
            nc.sync.dma_start(q_tables[t][:], q_rows[t])

        def listed(window, half=None):
            if half is None:
                return window[:].indirect(offsets[:])
            return window[:].indirect(offsets[:, halves(half, HALF // 16)])

        ident = tile("ident", P, F32)
        make_identity(nc, ident[:])
        sums = tile("sums", QUAD, F32)
        nc.gpsimd.memset(sums[:], 0.0)
        windows = [tile(f"window{j}", PIECES, F32) for j in range(PACK - 1)]
        for window in windows:
            nc.vector.memset(window[:], 0.0)

        lam_table = tile("lam_table", PIECES, F32)
        for group in range(PACK):
            spread = bank(f"lam_spread{group}", f"v{group}")
            for c in range(PACK):
                col = PACK * group + c
                nc.tensor.transpose(
                    spread[:, c * P : (c + 1) * P], lam_cols[:, col : col + 1].to_broadcast([P, P]), ident[:]
                )
            nc.scalar.activation(
                lam_table[:].rearrange("p (n g c) -> p g n c", g=PACK, c=PACK)[:, group],
                spread[:].rearrange("p (c n) -> p n c", c=PACK),
                COPY,
            )
        windows.append(tile("window3", PIECES, F32, tag="lam_cols"))
        nc.gpsimd.memset(windows[-1][:], 0.0)
        lam_slots = tile("lam_slots", SLOTS, F32)
        nc.scalar.activation(lam_slots[:], listed(lam_table), COPY)

        spread = bank("us_spread", "a0")
        for t in range(PACK):
            nc.tensor.transpose(spread[:, halves(t, P)], us_cols[:, t : t + 1].to_broadcast([P, P]), ident[:])
        us_rows = tile("us_rows", K, F32)
        nc.scalar.copy(us_rows[:], spread[:])

        dy_words = tile("dy_words", PACK * K, BF16)
        for pair in range(2):
            nc.vector.tensor_copy(
                dy_words[:, halves(pair, 2 * K)].rearrange("p (t m j) -> p m j t", t=2, j=PACK),
                dy_raw[:].rearrange("p (j m t) -> p m j t", j=PACK, t=PACK)[:, :, :, 2 * pair : 2 * pair + 2],
            )
        dy_codes = tile("dy_codes", K, U32)
        dy_scales = tile("dy_scales", K, U8)
        quantize(dy_codes[:], dy_scales[:], dy_words[:], E5M2)

        factors = [tile(f"factors{a}", PACK * P, F32) for a in range(PACK)]
        for a in range(PACK):
            nc.gpsimd.tensor_tensor(
                factors[a][:].rearrange("p (a k t) -> p a k t", a=PACK, t=PACK),
                lam_slots[:, halves(a // 2)]
                .rearrange("p (a b k) -> p b a k", a=PACK, b=2)[:, a % 2]
                .unsqueeze(3)
                .to_broadcast([P, PACK, QUAD, PACK]),
                us_cols[:].unsqueeze(1).unsqueeze(1).to_broadcast([P, PACK, QUAD, PACK]),
                MULT,
            )

        p_words = [tile(f"p_words{half}", PACK * HALF, BF16)[:] for half in range(2)]
        for t in range(2):
            for half in range(2):
                nc.vector.tensor_copy(by_slot(p_words[half], PACK)[:, :, :, :, t], listed(p_tables[t], half))
        p_late = tile("p_late", 2 * HALF, BF16, tag="lam_table")
        for t in (2, 3):
            nc.vector.tensor_copy(by_slot(p_words[0], PACK)[:, :, :, :, t], listed(p_tables[t], 0))
            nc.scalar.activation(p_late[:, halves(t - 2)], listed(p_tables[t], 1), COPY)
        p_codes = tile("p_codes", SLOTS, U32)
        p_scales = tile("p_scales", SLOTS, U8)
        quantize(p_codes[:, halves(0, P)], p_scales[:, halves(0, P)], p_words[0][:, halves(0, K)], E4M3)
        nc.vector.tensor_copy(
            by_slot(p_words[1], PACK)[:, :, :, :, 2:PACK],
            p_late[:].rearrange("p (t a b k) -> p a b k t", t=2, a=PACK, b=2),
        )
        quantize(p_codes[:, halves(1, P)], p_scales[:, halves(1, P)], p_words[0][:, halves(1, K)], E4M3)
        quantize(p_codes[:, halves(1)], p_scales[:, halves(1)], p_words[1], E4M3)

        x_narrow = []
        for j in range(PACK):
            x_narrow.append(tile(f"x_narrow{j}", K, BF16, tag={0: "p_table3", 1: "p_words0", 2: "lam_slots"}.get(j)))
            (nc.scalar.copy if j < 2 else nc.gpsimd.tensor_copy)(
                x_narrow[j][:].rearrange("p (u m e) -> p u m e", u=2, e=2),
                x_raw[:, halves(j, K)].rearrange("p (m u e) -> p u m e", u=2, e=2),
            )

        xr = {}

        def turn_x(planes, bank_tag, words):
            turned = bank(f"x_turned{planes[0]}", bank_tag)
            for n, j in enumerate(planes):
                for u in range(2):
                    nc.tensor.transpose(
                        turned[:, halves(2 * n + u, P)], x_narrow[j][:].bitcast(F32)[:, halves(u, P)], ident[:]
                    )
            nc.scalar.copy(
                words[:].bitcast(F32).rearrange("p (j c u) -> p j c u", c=P, u=2),
                turned[:, : len(planes) * 2 * P].rearrange("p (j u c) -> p j c u", c=P, u=2),
            )
            return words

        def quantize_x(planes, words, codes, scales):
            quantize(codes[:], scales[:], words[:], E4M3)
            for n, j in enumerate(planes):
                xr[j] = (codes[:, halves(n, P)], scales[:, halves(n, P)])

        v_banks = []
        for a in range(PACK):
            if a == 1:
                first_words = turn_x((0,), "a0", tile_at("xr_words0", K, BF16, 4096))
            v_banks.append(bank(f"v{a}", f"v{a}"))
            for t in range(PACK):
                matmul(
                    v_banks[a][:, halves(t, P)],
                    dy_codes[:, halves(t, P)],
                    dy_scales[:, halves(t, P)],
                    E5M2,
                    p_codes[:, halves(a, P)],
                    p_scales[:, halves(a, P)],
                    E4M3,
                )

        g_words = [tile("g_words0", PACK * HALF, BF16), tile_at("g_words1", PACK * HALF, BF16, 4096)]
        g_codes = tile("g_codes", SLOTS, U32)
        g_scales = tile("g_scales", SLOTS, U8)

        def form_g(a):
            nc.vector.tensor_tensor(
                g_words[a // 2][:, halves(a % 2, K)].rearrange("p (c i t) -> p c t i", i=2, t=PACK),
                v_banks[a][:].rearrange("p (t c i) -> p c t i", i=2, t=PACK),
                factors[a][:].rearrange("p (c i t) -> p c t i", i=2, t=PACK),
                MULT,
            )

        def quantize_g(half):
            quantize(g_codes[:, halves(half)], g_scales[:, halves(half)], g_words[half][:], E5M2)

        form_g(0)
        form_g(1)
        quantize_x((0,), first_words, tile("xr_codes0", P, U32), tile("xr_scales0", P, U8))
        quantize_g(0)
        form_g(2)
        form_g(3)

        v_planes = tile("v_planes", PACK * HALF, F32)
        for b in range(2):
            nc.scalar.copy(
                v_planes[:].rearrange("p (t b n) -> p b t n", t=PACK, b=2)[:, b],
                v_banks[b][:].rearrange("p (t n) -> p t n", t=PACK),
            )

        words = turn_x((1, 2), "a0", tile("xr_words12", 2 * K, BF16))
        quantize_x((1, 2), words, tile("xr_codes12", 2 * P, U32), tile("xr_scales12", 2 * P, U8))
        quantize_g(1)

        out_rows = out_1.rearrange("(p j) n -> j p n", j=PACK)

        def dq_product(j, bank_tag, half=None):
            acc = bank(f"dq_acc{j}_{half}", bank_tag)
            cols = slice(0, SLOTS) if half is None else halves(half)
            matmul(acc[:, cols], xr[j][0], xr[j][1], E4M3, g_codes[:, cols], g_scales[:, cols], E5M2)
            return acc

        def dq_copy(dq, acc, copy=nc.scalar.copy):
            copy(
                dq.rearrange("p (h a b k) -> p h a b k", a=PACK, b=2, k=QUAD),
                acc.rearrange("p (h b a k) -> p h a b k", a=PACK, b=2, k=QUAD),
            )
            return dq

        def scatter_on_scalar(j, dq, half):
            nc.scalar.activation(listed(windows[j], half), dq, COPY)

        dq0_0 = dq_copy(tile("dq0_0", HALF, F32)[:], dq_product(0, "d0", 0)[:, halves(0)])
        last_words = turn_x((3,), "v1", tile_at("xr_words3", K, BF16, 0))
        scatter_on_scalar(0, dq0_0, 0)
        quantize_x((3,), last_words, tile("xr_codes3", P, U32), tile("xr_scales3", P, U8))

        w_turned = []

        def make_w(b, bank_tag, tag):
            v_turned = bank(f"v_turned{b}", bank_tag)
            cols = halves(2 + b, P)
            matmul(v_turned[:], p_codes[:, cols], p_scales[:, cols], E4M3, dy_codes[:], dy_scales[:], E5M2)
            w_turned.append(tile(f"w_turned{b}", K, F32, tag=tag))
            nc.vector.tensor_tensor(w_turned[b][:], v_turned[:], us_rows[:], MULT)

        q_planes = tile_at("q_planes", PACK * SLOTS, BF16, 4096)

        def gather_q(t):
            nc.vector.tensor_copy(q_planes[:, halves(t, SLOTS)], listed(q_tables[t]))

        make_w(0, "v3", None)
        dq0_1 = dq_copy(tile("dq0_1", HALF, F32)[:], dq_product(0, "d1", 1)[:, halves(1)], nc.vector.tensor_copy)
        dq1 = dq_copy(tile("dq1", SLOTS, F32)[:], dq_product(1, "v2")[:], nc.vector.tensor_copy)
        acc2 = dq_product(2, "v0")
        dq2_0 = dq_copy(tile("dq2_0", HALF, F32)[:], acc2[:, halves(0)])
        scatter_on_scalar(0, dq0_1, 1)
        nc.sync.dma_start(out_rows[0], windows[0][:])
        scatter_on_scalar(2, dq2_0, 0)

        acc3 = dq_product(3, "a1")
        dq3_1 = dq_copy(tile("dq3_1", HALF, F32)[:], acc3[:, halves(1)], nc.vector.tensor_copy)
        nc.vector.tensor_copy(listed(windows[1]), dq1)
        nc.sync.dma_start(out_rows[1], windows[1][:])

        xd_words = tile_at("xd_words", PACK * K, BF16, 0)
        nc.gpsimd.tensor_copy(
            xd_words[:].rearrange("p (t m j) -> p t m j", t=PACK, j=PACK),
            x_raw[:].rearrange("p (j m t) -> p t m j", j=PACK, t=PACK),
        )

        gather_q(0)
        gather_q(2)
        for half in range(2):
            nc.vector.tensor_copy(q_planes[:, halves(6 + half)], listed(q_tables[3], half))

        nc.scalar.activation(q_planes[:, halves(1, SLOTS)], listed(q_tables[1]), COPY)
        dq2_1 = dq_copy(tile_at("dq2_1", HALF, F32, 8192)[:], acc2[:, halves(1)])
        dq3_0 = dq_copy(tile_at("dq3_0", HALF, F32, 9216)[:], acc3[:, halves(0)])
        scatter_on_scalar(2, dq2_1, 1)
        nc.sync.dma_start(out_rows[2], windows[2][:])
        scatter_on_scalar(3, dq3_0, 0)
        scatter_on_scalar(3, dq3_1, 1)
        nc.scalar.dma_start(out_rows[3], windows[3][:])

        xd_codes = tile("xd_codes", K, U32)
        xd_scales = tile("xd_scales", K, U8, tag="q_table3")
        q_words = [tile(f"q_words{half}", PACK * HALF, BF16) for half in range(2)]
        q_codes = tile("q_codes", SLOTS, U32)
        q_scales = tile("q_scales", SLOTS, U8)

        def interleave_q(half, b):
            nc.vector.tensor_copy(
                q_words[half][:, halves(b, K)].rearrange("p (a c i t) -> p a c t i", a=PACK, i=RUN, t=PACK),
                q_planes[:].rearrange("p (t h a b c i) -> p h b a c t i", t=PACK, h=2, a=PACK, b=2, i=RUN)[:, half, b],
            )

        def quantize_q(half):
            quantize(q_codes[:, halves(half)], q_scales[:, halves(half)], q_words[half][:], E4M3)

        interleave_q(0, 0)
        interleave_q(0, 1)
        quantize(xd_codes[:], xd_scales[:], xd_words[:], E4M3)
        quantize_q(0)
        interleave_q(1, 0)
        interleave_q(1, 1)
        make_w(1, "d0", "q_words0")
        quantize_q(1)

        step = QUAD // PACK
        u_banks = [bank(f"u{pair}", f"v{pair}") for pair in range(2)]
        for t in range(PACK):
            matmul(
                u_banks[t // 2][:, halves(t % 2)],
                xd_codes[:, halves(t, P)],
                xd_scales[:, halves(t, P)],
                E4M3,
                q_codes[:, halves(0)],
                q_scales[:, halves(0)],
                E4M3,
            )
        u_turned = []
        for b, tag in ((0, "v3"), (1, "v2")):
            u_turned.append(bank(f"u_turned{b}", tag))
            cols = halves(2 + b, P)
            matmul(u_turned[b][:], q_codes[:, cols], q_scales[:, cols], E4M3, xd_codes[:], xd_scales[:], E4M3)
        total = bank("total", "d1")
        for t in range(PACK):
            h = tile(f"h{t}", HALF, F32)
            nc.vector.scalar_tensor_tensor(
                h[:], u_banks[t // 2][:, halves(t % 2)], us_cols[:, t : t + 1], v_planes[:, halves(t)], MULT, MULT
            )
            for b in range(2):
                nc.tensor.matmul(
                    total[:, halves(b, P)],
                    h[:, halves(b, P)],
                    ident[:],
                    start=(t == 0 and b == 0),
                    stop=(t == PACK - 1 and b == 1),
                    is_transpose=True,
                )
        for b in range(2):
            h = tile(f"h_turned{b}", K, F32)
            col = (2 * b + 1) * step
            nc.vector.scalar_tensor_tensor(
                h[:], u_turned[b][:], 1.0, w_turned[b][:], MULT, MULT, accum_out=sums[:, col : col + 1]
            )
        spent = tile("spent", HALF, BF16)
        for b in range(2):
            col = 2 * b * step
            nc.scalar.activation(spent[:, halves(b, P)], total[:, halves(b, P)], COPY, accum_out=sums[:, col : col + 1])
        s_rows = tile("s_rows", QUAD, F32)
        nc.vector.transpose(s_rows[:], sums[:])
        for half, queue in enumerate((nc.scalar, nc.sync)):
            queue.dma_start(
                out_0[:, halves(half)].rearrange("o (n k) -> (o n) k", k=QUAD), s_rows[half * step : P : 2 * step, :]
            )
